import numpy as np, ml_dtypes
CORES = [24,25,26,27,28,29,30,31]
N = 8
BF = ml_dtypes.bfloat16
def gentries(a):
    return np.ascontiguousarray(a.reshape(8, 16, -1).transpose(0, 2, 1)).reshape(8, -1)
def gtable(e):
    e = np.asarray(e); return np.ascontiguousarray(e.reshape(8, -1, 16).transpose(0, 2, 1)).reshape(128, -1).astype(np.int32)
W, C, RO = 4096, 256, 3
LA, LB, LE, WD = 880, 1040, 960, 32
def parts(rng):
    x = rng.integers(0, 256, (N, 8, 16, W)); a = rng.integers(0, W, (N, 8, C, 16)); p = rng.integers(0, W, (N, 8, C, 16))
    pool = rng.integers(0, W, (N, 8, 32)); hot = np.take_along_axis(pool, rng.integers(0, 32, (N, 8, C * 16)), 2).reshape(N, 8, C, 16)
    return x, a, np.where(rng.random((N, 8, C, 16)) < 0.3, hot, p)
def pack(x, a, p):
    return {"x0": np.ascontiguousarray(x.reshape(N, 128, W)).astype(np.float32).astype(BF), "ka": np.stack([gtable(v.reshape(8, -1)) for v in a]), "ph": np.stack([gtable(v.reshape(8, -1)) for v in p])}
def alike(rng, a, p, share):
    m = (rng.random((N, 8, C, 1)) < share) & (np.arange(16) == rng.integers(0, 16, (N, 8, C, 1)))
    return np.where(m, a, p)
def setup_inputs(rng):
    x, a, p = parts(rng)
    return pack(x, a, alike(rng, a, p, 0.08))
def setup_inputs_spread(rng):
    x, a, p = parts(rng)
    v = np.minimum((np.exp2(8 * rng.random((N, 8, 1, W))) * rng.random(x.shape)).astype(np.int64), 255)
    x = np.where(rng.random(x.shape) < 0.5, v, 255 - v)
    a = np.minimum((W * rng.random(a.shape) ** 2).astype(np.int64), W - 1); u = np.minimum((W * rng.random(a.shape) ** 3).astype(np.int64), W - 1)
    return pack(x, a, np.where(rng.random(a.shape) < 0.5, u, p))
def setup_inputs_ends(rng):
    x, a, p = parts(rng); x = 255 * rng.integers(0, 2, x.shape)
    h = rng.choice(np.array([3, 4, 4, 5, 16]), (N, 8)); h[N - 1, 7] = 16; h[0, 7] = 4; h[0, 0] = 4; h[0, 1] = 3; h[N - 1, 6] = 4
    for r in range(N):
        for g in range(8):
            w = x[r, g]; w[:, W - 1] = w[:, 0]; o = rng.permutation(16)[:h[r, g]]
            if h[r, g] == 16: w[:, 0] = 0
            w[o, W - 1] = 255 - w[o, 0]
    kind = rng.choice(np.array([0, 1, 2]), (N, 8, C, 1), p=[0.4, 0.34, 0.26]); kind[:, :, [0, 1, 3, C - 2, C - 1]] = 0
    e = rng.integers(0, 2, (N, 8, C, 1))
    a = np.where(kind == 0, e * (W - 1), np.where(kind == 1, (W - 1) * rng.integers(0, 2, a.shape), a))
    p = np.where(kind == 0, (1 - e) * (W - 1), np.where(kind == 1, (W - 1) * rng.integers(0, 2, a.shape), p))
    return pack(x, a, p)
def setup_inputs_corners(rng):
    x = np.zeros((N, 8, 16, W), np.int64); a = np.zeros((N, 8, C, 16), np.int64); p = np.zeros((N, 8, C, 16), np.int64)
    far = np.array([LA - 1, LA, LA + 1, LB - 1, LB, LB + 3, LB + 4, LB + 59, LB + 60]); h = W // 2; M = 36; lane = np.arange(16)
    signs = np.stack([np.ones(16, np.int64), -np.ones(16, np.int64), 1 - 2 * (lane & 1)])
    for g in range(8):
        q = rng.permutation(W); low = q[1:h]; high = q[h + M:]; mids = q[h:h + M]
        m0 = rng.choice(np.array([-1, 0, 15, 15, 6]), C); o = lane[None, :] == m0[:, None]; o = o ^ (rng.random((C, 1)) < 0.5)
        k = rng.integers(0, 16, C); k = np.where(k == m0, (k + 1) & 15, k); swap = rng.random(C) < 0.5
        for r in range(N):
            w = x[r, g]; w[:, low] = rng.integers(0, 31, (16, len(low))); w[:, high] = rng.integers(215, 256, (16, len(high)))
            b = rng.integers(100, 151, 16); w[:, q[0]] = b; T = rng.permutation(np.resize(far, M))
            am = T[None, :] // 16 + (lane[:, None] < T[None, :] % 16); w[:, mids] = b[:, None] + am * signs[rng.integers(0, 3, M)].T
            lo1 = low[rng.integers(0, len(low), (C, 16))]; lo2 = low[rng.integers(0, len(low), (C, 16))]; hi1 = high[rng.integers(0, len(high), (C, 16))]; hi2 = high[rng.integers(0, len(high), (C, 16))]
            u = np.where(o, hi1, lo1); v = np.where(o, lo2, hi2)
            n = (0, 16, 15, C, 1, 17, 14, 31)[(g + 3 * r) % 8]; oc = rng.permutation(C); die = oc[:n]; rest = oc[n:]
            v[die, k[die]] = np.where(o[die, k[die]], hi2[die, k[die]], lo2[die, k[die]])
            edge = die[1::2]; under = mids[T == LA - 1]; md = under[rng.integers(0, len(under), len(edge))]
            u[edge, k[edge]] = np.where(swap[edge], md, q[0]); v[edge, k[edge]] = np.where(swap[edge], q[0], md)
            over = mids[T >= LA]; md = over[rng.integers(0, len(over), len(rest))]
            u[rest, k[rest]] = np.where(swap[rest], md, q[0]); v[rest, k[rest]] = np.where(swap[rest], q[0], md)
            assert int(np.sum(np.min(np.add.reduce(np.abs(w[:, u] - w[:, v]), axis=0), axis=1) < LA)) == n
            a[r, g] = u; p[r, g] = v
    return pack(x, a, p)
def setup_inputs_full(rng):
    x, a, p = parts(rng); lane = np.arange(16); h = W // 2; u = W // 4; z = int(rng.integers(0, N)); dead = int(rng.integers(0, 8))
    for g in range(8):
        if g == dead: continue
        for r in range(N):
            w = x[r, g]; q = rng.permutation(W); right = q[:h]; left = q[h:h + u]; out = q[h + u:]; b = rng.integers(100, 151, (16, 1))
            w[:, right] = b + rng.integers(0, 4, (16, h))
            far = np.where(rng.random((16, u)) < 0.5, 78 + rng.integers(0, 3, (16, u)), -75 - rng.integers(0, 3, (16, u)))
            near = np.argsort(rng.random((16, u)), axis=0) < 4
            w[:, left] = b + np.where(near, rng.integers(-8, 12, (16, u)), far)
            w[:, out] = b + rng.integers(90, 100, (16, len(out))) * (1 - 2 * rng.integers(0, 2, (16, len(out))))
            i = (rng.permutation(h)[:C], np.full(C, int(rng.integers(0, h))), rng.integers(0, 6, C))[(g + r) % 3]
            here = lane[None, :] == rng.integers(0, 16, (C, 1))
            a[r, g] = np.where(here, left[rng.integers(0, u, (C, 16))], right[rng.integers(0, h, (C, 16))])
            p[r, g] = np.where(here, right[i][:, None], out[rng.integers(0, len(out), (C, 16))])
    q = rng.permutation(np.arange(1, W)); s1 = q[:h]; s2 = q[h:h + u]; s0 = np.append(q[h + u:], 0)
    a[:, dead] = 0; p[:, dead] = s0[rng.integers(0, len(s0), (N, C, 16))]
    far = np.array([LB - 1, LB, LB + 1, LB + 3, LB + 4, LB + 31, LB + 59, LB + 60]); T = far[np.arange(h) % 8]
    cl = np.minimum(rng.integers(0, 8, (C, 1)) + rng.integers(0, 3, (C, 16)), 7)
    a[(z - 2) % N, dead] = s1[cl + 8 * rng.integers(0, h // 8, (C, 16))]; p[(z + 2) % N, dead] = s2[rng.integers(0, u, (C, 16))]
    x[:, dead] = rng.integers(215, 256, (N, 16, W))
    for r in range(N):
        w = x[r, dead]; w[:, s1] = rng.integers(0, 31, (16, h))
        if r == z:
            b = rng.integers(100, 151, (16, 1)); w[:] = b + rng.integers(0, 4, (16, W)); w[:, s2] = b
            w[:, s1] = b + (T[None, :] // 16 + (lane[:, None] < T[None, :] % 16)) * (1 - 2 * rng.integers(0, 2, (16, h)))
    return pack(x, a, p)
def setup_inputs_ties(rng):
    x, a, p = parts(rng); x = rng.integers(0, 176, x.shape)
    pool = rng.integers(0, W, (N, 8, 8)); pool[..., 0] = 0; pool[..., 7] = W - 1
    hot = np.take_along_axis(pool, rng.integers(0, 8, (N, 8, C * 16)), 2).reshape(N, 8, C, 16); p[:, 1::2] = hot[:, 1::2]
    src = np.arange(16) % rng.choice(np.array([1, 1, 1, 2, 4, 16]), (N, 8, C, 1))
    return pack(x, np.take_along_axis(a, src, 3), np.take_along_axis(p, src, 3))
def check_inputs(d):
    bad = []
    for k, lo, hi in (("x0", 0, 255), ("ka", 0, W - 1), ("ph", 0, W - 1)):
        v = np.asarray(d[k]).astype(np.float64)
        if not (np.min(v) >= lo and np.max(v) <= hi): bad.append("range of " + k)
    v = np.asarray(d["x0"]).astype(np.float64)
    if np.any(v != np.floor(v)): bad.append("whole numbers of x0")
    return bad
def reference(x0, ka, ph):
    X = x0.astype(np.float32).astype(np.int32).reshape(N, 8, 16, W)
    K = np.stack([gentries(v) for v in ka]).astype(np.int64).reshape(N, 8, C, 16)
    P = np.stack([gentries(v) for v in ph]).astype(np.int64).reshape(N, 8, C, 16)
    A = np.zeros((N, 8, 1), np.int64); place = np.arange(16)
    for t in range(RO):
        if t > 0: K = np.roll(K, 1, axis=0); P = np.roll(P, -1, axis=0)
        for r in range(N):
            x, a, p = X[r], K[r].copy(), P[r].copy()
            s = np.take_along_axis(x, a.reshape(8, 1, C * 16), 2).reshape(8, 16, C, 16); y = np.take_along_axis(x, p.reshape(8, 1, C * 16), 2).reshape(8, 16, C, 16)
            D = np.add.reduce(np.abs(s - y), axis=1)
            k = np.argmin(D, axis=2)
            d = np.take_along_axis(D, k[:, :, None], 2)[:, :, 0]
            sk = np.take_along_axis(s, k[:, None, :, None], 3)[..., 0]; yk = np.take_along_axis(y, k[:, None, :, None], 3)[..., 0]
            kill = d < LA; prime = ~kill & (d < LB + 4 * (A[r] & 15))
            step = np.where(np.add.reduce(sk, axis=1) > np.add.reduce(yk, axis=1), 1, -1) * (1 + (d & 3))
            n = np.take_along_axis(p, ((k + step) & 15)[:, :, None], 2)[:, :, 0]
            xn = np.take_along_axis(x, n[:, None, :], 2)
            near = np.add.reduce(np.abs(s - xn[..., None]), axis=1) < LE
            m = np.where(np.any(near, axis=2), np.argmax(near, axis=2), -1)
            fresh = np.take_along_axis(a, np.clip(m[:, :, None] + place, 0, 15), 2); fresh[:, :, 0] = n
            v = np.take_along_axis(p, k[:, :, None], 2)[:, :, 0]; new = np.where(np.abs(sk - yk) <= WD, (yk + 128) & 255, yk)
            for g in range(8):
                c = np.nonzero(prime[g])[0]; w = c[np.unique(v[g, c], return_index=True)[1]]
                x[g][:, v[g, w]] = new[g][:, w]
            P[r] = np.where(kill[:, :, None], (((a * p) >> 5) + p) & (W - 1), p)
            K[r] = np.where(prime[:, :, None], fresh, a)
            A[r] = A[r] + np.add.reduce(kill.astype(np.int64), axis=1)[:, None]
    return {"yk": np.stack([gtable(v.reshape(8, -1)) for v in K]).astype(np.float32), "yp": np.stack([gtable(v.reshape(8, -1)) for v in P]).astype(np.float32), "yx": X.reshape(N, 128, W).astype(np.float32).astype(BF)}

@@ -1,0 +1,498 @@
+from concourse.mybir import AluOpType as ALU, AxisListType, ActivationFunctionType as AF
+
+BIG = 1.0e6
+_B = "bfloat16"
+_F = "float32"
+_I = "int32"
+_U = "uint16"
+SCRATCH = {
+    "X": ("sbuf", [128, 4352], _B),
+    "KS": ("sbuf", [128, 4608], _F),
+    "kd": ("dram", [8, 33, 256], _F),
+    "kz": ("dram", [8, 4096], _F),
+    "cm": ("sbuf", [128, 256], _F),
+    "k15": ("sbuf", [128, 256], _F),
+    "kin": ("sbuf", [128, 256], _I), "pin": ("sbuf", [128, 256], _I),
+    "kl0": ("sbuf", [128, 256], _U), "kl1": ("sbuf", [128, 256], _U), "kl2": ("sbuf", [128, 256], _U),
+    "pl0": ("sbuf", [128, 256], _U), "pl1": ("sbuf", [128, 256], _U), "pl2": ("sbuf", [128, 256], _U),
+    "ku": ("sbuf", [128, 4, 16, 4], _U), "pu": ("sbuf", [128, 256], _U),
+    "kout": ("sbuf", [128, 4, 16, 4], _F), "pout": ("sbuf", [128, 256], _F),
+    "Pf": ("sbuf", [128, 256], _F), "P4": ("sbuf", [128, 256], _F),
+    "t1": ("sbuf", [128, 256], _I), "t2": ("sbuf", [128, 256], _I),
+    "pw": ("sbuf", [128, 256], _I), "px_": ("sbuf", [128, 256], _I),
+    "pid": ("sbuf", [128, 4], _I), "row": ("sbuf", [128, 128], _I), "row2": ("sbuf", [128, 128], _I),
+    "rowm": ("sbuf", [128, 128], _F), "rowi": ("sbuf", [128, 128], _F),
+    "col": ("sbuf", [128, 16], _F), "r16": ("sbuf", [128, 16], _F), "OH": ("sbuf", [128, 16], _F),
+    "GM": ("sbuf", [128, 8], _F), "pw2": ("sbuf", [128, 64], _F),
+    "SEL": ("sbuf", [128, 16, 128], _B), "SELN": ("sbuf", [128, 16, 128], _B),
+    "SELP": ("sbuf", [128, 16, 128], _B), "IDN": ("sbuf", [128, 128], _B),
+    "SELW": ("sbuf", [128, 16, 128], _B), "SELT": ("sbuf", [128, 16, 128], _B),
+    "BLK": ("sbuf", [128, 128], _B), "BLKF": ("sbuf", [128, 128], _F), "BLK0": ("sbuf", [128, 128], _F),
+    "S15": ("sbuf", [128, 128], _F), "ID": ("sbuf", [128, 128], _B), "IDW": ("sbuf", [128, 128], _B),
+    "JR": ("sbuf", [128, 256], _B), "JRF": ("sbuf", [128, 256], _F), "Z0": ("sbuf", [128, 256], _B),
+    "RST": ("sbuf", [128, 256], _F), "RSE": ("sbuf", [128, 256], _F), "BC0": ("sbuf", [128, 256], _F),
+    "C16": ("sbuf", [128, 16], _F), "CB": ("sbuf", [128, 16], _F), "DM": ("sbuf", [128, 16], _F),
+    "DMH": ("sbuf", [128, 16], _F), "TRB": ("sbuf", [128, 4, 64], _B), "tri": ("sbuf", [128, 64], _F),
+    "us": ("sbuf", [128, 256], _F), "key": ("sbuf", [128, 256], _F), "R": ("sbuf", [128, 256], _F), "sg": ("sbuf", [128, 256], _B),
+    "sf": ("sbuf", [128, 384], _F), "si": ("sbuf", [128, 128], _I),
+    "offF": ("sbuf", [128, 16], _U), "offK": ("sbuf", [128, 16], _U), "offV": ("sbuf", [128, 16], _U),
+    "offX": ("sbuf", [128, 16], _U),
+    "kill": ("sbuf", [128, 16], _B), "k1b": ("sbuf", [128, 16], _B), "f1b": ("sbuf", [128, 16], _B),
+    "A": ("sbuf", [128, 4], _F), "A1": ("sbuf", [128, 4], _F), "Ai": ("sbuf", [128, 4], _I), "thr": ("sbuf", [128, 4], _F),
+    "xn": ("sbuf", [128, 4, 64], _B), "xz": ("sbuf", [128, 256], _F), "xb": ("sbuf", [128, 256], _F),
+    "nn": ("sbuf", [128, 256], _F), "fs": ("sbuf", [128, 256], _F), "a1": ("sbuf", [128, 256], _F),
+    "kp": ("sbuf", [128, 4, 64], _F),
+    "HPk": ("sbuf", [128, 4, 16, 4], _F), "HPf": ("sbuf", [128, 4, 16, 4], _F),
+    "b1": ("sbuf", [128, 256], _I), "b2": ("sbuf", [128, 256], _I), "FB": ("sbuf", [128, 256], _B),
+    "BD": ("sbuf", [128, 16, 8, 16], _B), "junk": ("sbuf", [128, 4096], _B),
+    "ak": ("sbuf", [128, 256], _B), "yk_": ("sbuf", [128, 256], _B), "sw": ("sbuf", [128, 256], _B),
+    "sy": ("sbuf", [128, 256], _B), "e2": ("sbuf", [128, 256], _B),
+    "pk": ("psum", [128, 512], _F), "ps": ("psum", [128, 512], _F), "px": ("psum", [128, 4, 16, 4], _F),
+    "pe": ("psum", [128, 256], _F), "pb": ("psum", [128, 8, 16, 4], _F), "pone": ("psum", [128, 512], _F),
+    "pn": ("psum", [128, 8, 4, 16], _F), "pg": ("psum", [128, 512], _F),
+}
+for _c in range(4):
+    for _n in ("y", "s", "d", "rl", "mx"):
+        SCRATCH["%s%d" % (_n, _c)] = ("sbuf", [128, 1024], _B)
+PSUM = ("pk", "ps", "px", "pe", "pb", "pone", "pn", "pg")
+SEMAPHORES = ["qv", "qs", "qt", "qg"] + ["dm%d" % i for i in range(24)] + ["rk1", "rk2", "rp1", "rp2", "lk1", "lk2", "lp1", "lp2"]
+ROUNDS = 3
+SMF = ("w", "h1", "h2", "fo", "ko", "plt", "nk", "pr", "k1", "f1", "pr4", "bs", "bs2", "o1", "o2", "cnt", "nd", "win", "w1", "w2", "w3")
+SMI = ("ki", "zm", "ub", "kk", "h3", "fi")
+
+
+def rank_program(g, core, T, topo):
+    rank = T.rank_of(core)
+    if rank is None:
+        return
+    n_ranks = len(T.cores)
+    eng = {"v": g.vector, "s": g.scalar, "t": g.tensor, "g": g, "y": g.sync}
+    count = {"v": 0, "s": 0, "t": 0, "g": 0}
+    total = {}
+    waited = {}
+    log = {}
+    dmas = [0]
+
+    def deps(q, reads, writes):
+        need = {}
+        for is_w, regs in ((False, reads), (True, writes)):
+            for name, lo, hi in regs:
+                bank = name in PSUM
+                for (l, h, oq, sem, val, ow) in log.get(name, []):
+                    if not bank and (h <= lo or hi <= l):
+                        continue
+                    if oq == q:
+                        if q == "t" or (not ow):
+                            continue
+                        if is_w and bank and (h <= lo or hi <= l):
+                            continue
+                        if not is_w and (h <= lo or hi <= l):
+                            continue
+                    elif not bank and not ow and not is_w:
+                        continue
+                    if val > need.get(sem, 0):
+                        need[sem] = val
+        for sem in sorted(need):
+            if waited.get((q, sem), 0) < need[sem]:
+                waited[(q, sem)] = need[sem]
+                eng[q].wait_ge(T.sem[sem], need[sem])
+
+    def note(q, sem, val, reads, writes):
+        for is_w, regs in ((False, reads), (True, writes)):
+            for name, lo, hi in regs:
+                old = log.get(name, [])
+                if is_w:
+                    old = [e for e in old if not (lo <= e[0] and e[1] <= hi)]
+                else:
+                    old = [e for e in old if not (e[2] == q and not e[5] and e[3] == sem and lo <= e[0] and e[1] <= hi)]
+                old.append((lo, hi, q, sem, val, is_w))
+                log[name] = old
+
+    def m(name):
+        if name in SMF:
+            i = 16 * SMF.index(name)
+            return T.sf[:, i:i + 16]
+        if name in SMI:
+            i = 16 * SMI.index(name)
+            return T.si[:, i:i + 16]
+        return T[name][:]
+
+    def flat(name, lo=None, hi=None):
+        if lo is None and (name in SMF or name in SMI):
+            return (name, 0, 16)
+        if lo is None:
+            n = 1
+            for x in SCRATCH[name][1][1:]:
+                n *= x
+            return (name, 0, n)
+        return (name, lo, hi)
+
+    def op(q, fn, reads, writes):
+        reads = [flat(*r) if isinstance(r, tuple) else flat(r) for r in reads]
+        writes = [flat(*r) if isinstance(r, tuple) else flat(r) for r in writes]
+        deps(q, reads, writes)
+        count[q] += 1
+        sem = "q" + q
+        total[sem] = count[q]
+        fn().then_inc(T.sem[sem], 1)
+        note(q, sem, count[q], reads, writes)
+
+    def dma(q, pairs):
+        sem = "dm%d" % dmas[0]
+        dmas[0] += 1
+        val = 16 * len(pairs)
+        total[sem] = val
+        done = []
+        for out, in_, w, r in pairs:
+            r = [flat(*x) if isinstance(x, tuple) else flat(x) for x in r]
+            w = [flat(*x) if isinstance(x, tuple) else flat(x) for x in w]
+            deps(q, r, w)
+            eng[q].dma_start(out, in_).then_inc(T.sem[sem], 16)
+            done.append((r, w))
+        for r, w in done:
+            note("dma", sem, val, r, [])
+        for r, w in done:
+            for x in w:
+                log.setdefault(x[0], []).append((x[1], x[2], "dma", sem, val, True))
+
+    def tt(out, a, b, o, reads, writes):
+        op("v", lambda: g.vector.tensor_tensor(out, a, b, o), reads, writes)
+
+    def ts(out, a, s1, o1, reads, writes, s2=None, o2=None):
+        if o2 is None:
+            op("v", lambda: g.vector.tensor_scalar(out, a, s1, None, o1), reads, writes)
+        else:
+            op("v", lambda: g.vector.tensor_scalar(out, a, s1, s2, o1, o2), reads, writes)
+
+    def q1(out, a, s1, o1, s2=None, o2=None):
+        ts(m(out), m(a), s1, o1, [a], [out], s2, o2)
+
+    def q2(out, a, b, o):
+        tt(m(out), m(a), m(b), o, [a, b], [out])
+
+    def cp(out, a, reads, writes):
+        op("v", lambda: g.vector.tensor_copy(out, a), reads, writes)
+
+    def fill(name, c, ap=None):
+        op("v", lambda: g.vector.memset(T[name][:] if ap is None else ap, c), [], [name])
+
+    def act(out, a, f, reads, writes, **kw):
+        op("s", lambda: g.scalar.activation(out, a, f, **kw), reads, writes)
+
+    def mm(out, l, r, st, sp, reads, writes):
+        op("t", lambda: g.tensor.matmul(out, l, r, st, sp), reads, writes)
+
+    def scan(out, a, b, o1, o2, reads, writes):
+        op("v", lambda: g.vector.tensor_tensor_scan(out, a, b, 0.0, o1, o2), reads, writes)
+
+    def iota(name, ap, pat, base, mult):
+        op("g", lambda: g.iota(ap, pat, base, mult, allow_small_or_imprecise_dtypes=True), [], [name])
+
+    dma("y", [(T.pin[:], T.ph[:], ["pin"], [])])
+    dma("y", [(T.kin[:], T.ka[:], ["kin"], [])])
+    dma("y", [(T.X[:, 0:4096], T.x0[:], [("X", 0, 4096)], [])])
+    iota("pid", T.pid[:, 0:1], [[0, 1]], 0, 1)
+    iota("row", T.row[:], [[1, 128]], 0, 0)
+    iota("r16", T.r16[:], [[1, 16]], 0, 0)
+    iota("JRF", T.JRF[:], [[0, 16], [4, 16]], 1, 0)
+    iota("C16", T.C16[:], [[0, 4], [16, 4]], 0, 0)
+    iota("CB", T.CB[:], [[64, 4], [1, 4]], 0, 0)
+    iota("DM", T.DM[:], [[16, 16]], 4096, 0)
+    iota("tri", T.tri[:], [[1, 4], [4, 16]], 0, 0)
+    fill("cm", -4096.0)
+    dma("y", [(T.kz[:], T.cm[:], ["kz"], ["cm"]), (T.kd[:, 0, :], T.cm[0:8, :], [("kd", 0, 1)], ["cm"])])
+    dma("y", [(T.KS[0::16, 0:4096], T.kz[:], [("KS", 0, 4096)], ["kz"])])
+    fill("SEL", 0.0)
+    ts(T.pid[:, 1:2], T.pid[:, 0:1], 15, ALU.bitwise_and, [("pid", 0, 1)], [("pid", 1, 2)])
+    ts(T.pid[:, 2:3], T.pid[:, 0:1], 4, ALU.arith_shift_right, [("pid", 0, 1)], [("pid", 2, 3)])
+    ts(T.row2[:], T.row[:], 4, ALU.arith_shift_right, ["row"], ["row2"])
+    cp(T.rowi[:], T.row[:], ["row"], ["rowi"])
+    cp(T.col[:, 0:3], T.pid[:, 0:3], [("pid", 0, 3)], [("col", 0, 3)])
+    cp(T.rowm[:], T.row2[:], ["row2"], ["rowm"])
+    ts(T.col[:, 3:4], T.col[:, 1:2], 1.0, ALU.add, [("col", 1, 2)], [("col", 3, 4)])
+    ts(T.col[:, 4:5], T.col[:, 1:2], 64.0, ALU.mult, [("col", 1, 2)], [("col", 4, 5)])
+    ts(T.col[:, 7:8], T.col[:, 1:2], 4.0, ALU.mult, [("col", 1, 2)], [("col", 7, 8)])
+    ts(T.BLK[:], T.rowm[:], T.col[:, 2:3], ALU.is_equal, ["rowm", ("col", 2, 3)], ["BLK"])
+    ts(T.OH[:], T.r16[:], T.col[:, 1:2], ALU.is_equal, ["r16", ("col", 1, 2)], ["OH"])
+    for q in range(16):
+        cp(T.SEL[:, q, q::16], T.BLK[:, q::16], ["BLK"], [("SEL", 128 * q, 128 * q + 128)])
+    act(T.SELN[:], T.SEL[:], AF.Copy, ["SEL"], ["SELN"], scale=-0.5)
+    act(T.SELP[:], T.SEL[:], AF.Copy, ["SEL"], ["SELP"], scale=0.5)
+    ts(T.ID[:], T.rowi[:], T.col[:, 0:1], ALU.is_equal, ["rowi", ("col", 0, 1)], ["ID"])
+    ts(T.IDW[:], T.ID[:], 1.0 / 128, ALU.mult, ["ID"], ["IDW"])
+    ts(T.IDN[:], T.ID[:], -1.0, ALU.mult, ["ID"], ["IDN"])
+    ts(T.JR[:], T.JRF[:], 1.0 / 128, ALU.mult, ["JRF"], ["JR"])
+    cp(T.kl0[:], T.kin[:], ["kin"], ["kl0"])
+    cp(T.pl0[:], T.pin[:], ["pin"], ["pl0"])
+    fill("RST", -BIG)
+    op("v", lambda: g.vector.memset(T.RST[:, 0::16], BIG), ["RST"], ["RST"])
+    fill("thr", 520.0)
+    fill("A", 0.0)
+    ts(T.C16[:], T.C16[:], T.col[:, 4:5], ALU.add, ["C16", ("col", 4, 5)], ["C16"])
+    ts(T.CB[:], T.CB[:], T.col[:, 7:8], ALU.add, ["CB", ("col", 7, 8)], ["CB"])
+    ts(T.DM[:], T.DM[:], T.col[:, 1:2], ALU.add, ["DM", ("col", 1, 2)], ["DM"])
+    ts(T.DMH[:], T.DM[:], -2047.5, ALU.add, ["DM"], ["DMH"])
+
+    def constants2():
+        for q in range(16):
+            ts(T.SELT[:, q, :], T.BLK[:], T.OH[:, q:q + 1], ALU.mult, ["BLK", "OH"], [("SELT", 128 * q, 128 * q + 128)])
+        cp(T.BLKF[:], T.BLK[:], ["BLK"], ["BLKF"])
+        fill("BLK0", 0.0)
+        op("v", lambda: g.vector.tensor_copy(T.BLK0[:, 0::16], T.BLK[:, 0::16]), ["BLK", "BLK0"], ["BLK0"])
+        ts(T.S15[:], T.BLK[:], T.OH[:, 15:16], ALU.mult, ["BLK", "OH"], ["S15"])
+        fill("Z0", 0.0)
+        fill("RSE", -1.0 / 16)
+        op("v", lambda: g.vector.memset(T.RSE[:, 0::16], BIG), ["RSE"], ["RSE"])
+        fill("BC0", 1.0)
+        op("v", lambda: g.vector.memset(T.BC0[:, 0::16], 0.0), ["BC0"], ["BC0"])
+        fill("xz", 0.0)
+        ts(T.GM[:], T.r16[:, 0:8], T.col[:, 2:3], ALU.is_equal, ["r16", ("col", 2, 3)], ["GM"])
+        fill("pw2", 0.5, T.pw2[:, 0:16])
+        fill("pw2", 2.0, T.pw2[:, 16:32])
+        op("v", lambda: g.vector.tensor_tensor_scan(T.pw2[:, 32:48], T.pw2[:, 0:16], T.Z0[:, 0:16], 8192.0, ALU.mult, ALU.add), ["pw2", "Z0"], ["pw2"])
+        op("v", lambda: g.vector.tensor_tensor_scan(T.pw2[:, 48:64], T.pw2[:, 16:32], T.Z0[:, 0:16], 0.25, ALU.mult, ALU.add), ["pw2", "Z0"], ["pw2"])
+        op("v", lambda: g.vector.memset(T.pw2[:, 45:48], 0.0), ["pw2"], ["pw2"])
+        op("v", lambda: g.vector.memset(T.pw2[:, 60:64], 0.0), ["pw2"], ["pw2"])
+        for i in (0, 1):
+            a = 32 + 16 * i
+            tt(T.pw2[:, 16 * i:16 * i + 16], T.pw2[:, a:a + 16], T.OH[:], ALU.mult, ["pw2", "OH"], ["pw2"])
+            op("v", lambda i=i: g.vector.tensor_reduce(T.col[:, 5 + i:6 + i], T.pw2[:, 16 * i:16 * i + 16], AxisListType.X, ALU.add), ["pw2"], [("col", 5 + i, 6 + i)])
+        for rl in range(4):
+            ts(T.col[:, 8 + rl:9 + rl], T.col[:, 7:8], float(rl), ALU.add, [("col", 7, 8)], [("col", 8 + rl, 9 + rl)])
+        for rl in range(4):
+            ts(T.TRB[:, rl, :], T.tri[:], T.col[:, 8 + rl:9 + rl], ALU.is_ge, ["tri", ("col", 8 + rl, 9 + rl)], [("TRB", 64 * rl, 64 * rl + 64)], -64.0, ALU.mult)
+
+    def landed(name, sem, val):
+        total[sem] = val
+        log.setdefault(name, []).append((0, 256, "rem", sem, val, True))
+
+    def send(name, land, dst, rs, ls):
+        rid, pid, _ = topo.addr(dst)
+        es = topo.engines(core, dst)[:8]
+        mask = sum(1 << e for e in es)
+        regs = [flat(name)]
+        deps("g", regs, [])
+        g.remote_dma(T[land][:], T[name][:], T.sem[rs], T.sem[ls], pid, rid, mask)
+        total[ls] = len(es)
+        note("rem", ls, len(es), regs, [])
+
+    nxt = T.cores[(rank + 1) % n_ranks]
+    prv = T.cores[(rank - 1) % n_ranks]
+    KB = 17 * 256
+    CN = 16 * SMF.index("cnt")
+
+    for t in range(ROUNDS):
+        last = t == ROUNDS - 1
+        kl, pl = "kl%d" % t, "pl%d" % t
+        KL, PL = T[kl], T[pl]
+        if t:
+            ne = len(topo.engines(core, nxt)[:8])
+            landed(kl, "rk%d" % t, ne)
+            landed(pl, "rp%d" % t, ne)
+        if t == 0:
+            fill("us", 0.0)
+            constants2()
+        cp(T.y0[:], T.X[:, 0:4096].indirect(PL[:, 0:64]), [("X", 0, 4096), pl], ["y0"])
+        for c in (1, 2, 3):
+            act(T["y%d" % c][:], T.X[:, 0:4096].indirect(PL[:, 64 * c:64 * c + 64]), AF.Copy, [("X", 0, 4096), pl], ["y%d" % c])
+        cp(T.Pf[:], PL[:], [pl], ["Pf"])
+        ts(T.P4[:], PL[:], 4096.0, ALU.add, [pl], ["P4"])
+        cp(T.KS[:, KB:KB + 256], KL[:], [kl], [("KS", KB, KB + 256)])
+        mm(T.pn[:, 0:4], T.S15[:], T.KS[:, KB:KB + 256], True, True, ["S15", ("KS", KB, KB + 256)], [("pn", 0, 256)])
+        act(T["s3"][:], T.X[:, 0:4096].indirect(KL[:, 192:256]), AF.Copy, [("X", 0, 4096), kl], ["s3"])
+        act(T.k15[:], T.pn[:, 0:4], AF.Copy, [("pn", 0, 256)], ["k15"])
+        dma("y", [(T.kd[:, 1:17, :], T.KS[:, KB:KB + 256], [("kd", 1, 17)], [("KS", KB, KB + 256)]),
+                  (T.kd[:, 17:33, :], T.k15[:], [("kd", 17, 33)], ["k15"])])
+        dma("y", [(T.KS[j::16, 0:4096], T.kd[:, j + 1:j + 17, :], [("KS", 0, 4096)], [("kd", j + 1, j + 17)]) for j in range(1, 16)]
+            + [(T.KS[:, 4096:KB], T.kd[:, 0:16, :], [("KS", 4096, KB)], [("kd", 0, 16)])])
+        mm(T.pk[:, 0:256], T.ID[:], T.JR[:], True, False, ["ID", "JR"], [("pk", 0, 256)])
+
+        def fused(c):
+            tt(T["d%d" % c][:], T.X[:, 0:4096].indirect(KL[:, 64 * c:64 * c + 64]), T["y%d" % c][:], ALU.subtract, [("X", 0, 4096), kl, "y%d" % c], ["d%d" % c])
+
+        def relu(c):
+            ts(T["rl%d" % c][:], T["d%d" % c][:], 0.0, ALU.max, ["d%d" % c], ["rl%d" % c])
+
+        def pass_(bank, lo, sel, src, first, final, rev=False):
+            for q in range(16):
+                mm(T[bank][:, lo:lo + 64], T[sel][:, q, :], T[src][:, 64 * q:64 * q + 64], first and q == 0, final and q == 15,
+                   [sel, src], [(bank, lo, lo + 64)])
+
+        def dpass(c):
+            pass_("ps", 64 * c, "SELN", "d%d" % c, True, True)
+
+        def rpass(c):
+            pass_("pk", 64 * c, "SEL", "rl%d" % c, False, False)
+
+        def sgather(c):
+            act(T["s%d" % c][:], T.X[:, 0:4096].indirect(KL[:, 64 * c:64 * c + 64]), AF.Copy, [("X", 0, 4096), kl], ["s%d" % c])
+
+        for h, bank in ((0, "pone"), (1, "pg")):
+            mm(T[bank][:], T.ID[:], T.s3[:, 512 * h:512 * h + 512], True, False, ["ID", "s3"], [bank])
+            mm(T[bank][:], T.IDN[:], T.y3[:, 512 * h:512 * h + 512], False, True, ["IDN", "y3"], [bank])
+            act(T.rl3[:, 512 * h:512 * h + 512], T[bank][:], AF.Abs, [bank], [("rl3", 512 * h, 512 * h + 512)], scale=0.5)
+        sgather(0)
+        fused(0)
+        relu(0)
+        fused(1)
+        dpass(0)
+        rpass(0)
+        pass_("ps", 192, "SELN", "s3", True, False)
+        pass_("ps", 192, "SELP", "y3", False, True)
+        rpass(3)
+        relu(1)
+        fused(2)
+        dpass(1)
+        rpass(1)
+        relu(2)
+        dpass(2)
+        rpass(2)
+        tt(T.t1[:], T.KS[:, KB:KB + 256], T.Pf[:], ALU.mult, [("KS", KB, KB + 256), "Pf"], ["t1"])
+        ts(T.t2[:], T.t1[:], 5, ALU.arith_shift_right, ["t1"], ["t2"])
+        sgather(1)
+        act(T.sg[:], T.ps[:, 0:256], AF.Sign, [("ps", 0, 256)], ["sg"], scale=-1.0, bias=-0.25)
+        act(T.us[:, 0:192], T.ps[:, 0:192], AF.Copy, [("ps", 0, 192)], [("us", 0, 192)])
+        mm(T.pk[:, 0:256], T.IDW[:], T.sg[:], False, True, ["IDW", "sg"], [("pk", 0, 256)])
+        sgather(2)
+        if t == 0:
+            act(T.SELW[:], T.SEL[:], AF.Copy, ["SEL", ("col", 6, 7)], ["SELW"], scale=T.col[:, 6:7])
+        mm(T.pe[:], T.ID[:], T.Z0[:], True, False, ["ID", "Z0"], ["pe"])
+        for c in (3, 0, 1, 2):
+            pass_("pe", 64 * c, "SELN", "s%d" % c, False, False)
+        tt(T.key[:], T.pk[:, 0:256], T.us[:], ALU.add, [("pk", 0, 256), "us"], ["key"])
+        scan(T.R[:], T.RST[:], T.key[:], ALU.max, ALU.min, ["RST", "key"], ["R"])
+        r = T.R[:, 15::16]
+        ts(m("ki"), r, 64.0, ALU.mult, ["R"], ["ki"])
+        ts(m("nk"), r, 440.0, ALU.is_ge, ["R"], ["nk"])
+        ts(m("plt"), r, T.thr[:, 0:1], ALU.is_lt, ["R", "thr"], ["plt"])
+        q1("ub", "ki", 1, ALU.bitwise_and)
+        q1("zm", "ki", 5, ALU.arith_shift_right, 3, ALU.bitwise_and)
+        q1("kk", "ki", 1, ALU.arith_shift_right, 15, ALU.bitwise_and)
+        q1("w", "ub", 2.0, ALU.mult, -1.0, ALU.add)
+        q2("pr", "plt", "nk", ALU.mult)
+        q2("h2", "zm", "w", ALU.mult)
+        q2("h1", "kk", "w", ALU.add)
+        q2("h3", "h1", "h2", ALU.add)
+        q1("fi", "h3", 15, ALU.bitwise_and)
+        q2("fo", "fi", "C16", ALU.add)
+        cp(T.offF[:], m("fo"), ["fo"], ["offF"])
+        for c in range(4):
+            cp(T.xn[:, c, :], T["y%d" % c][:].indirect(T.offF[:, 4 * c:4 * c + 4]), ["y%d" % c, "offF"], [("xn", 64 * c, 64 * c + 64)])
+        for rl in range(4):
+            mm(T.px[:, :, :, rl], T.ID[:], T.xn[:, :, 16 * rl:16 * rl + 16], True, True, ["ID", "xn"], ["px"])
+        q1("k1", "kk", 1.0, ALU.add)
+        q1("f1", "fi", 1.0, ALU.add)
+        q2("ko", "kk", "C16", ALU.add)
+        q2("k1b", "k1", "pr", ALU.mult)
+        q2("f1b", "f1", "pr", ALU.mult)
+        cp(T.offK[:], m("ko"), ["ko"], ["offK"])
+        ts(T.kill[:], r, 440.0, ALU.is_lt, ["R"], ["kill"])
+
+        def spread(b, src):
+            for q in range(16):
+                mm(T.pb[:, b:b + 4, q, :], T.SELT[:, q, :], T[src][:], True, True, ["SELT", src], [("pb", 64 * b, 64 * b + 256)])
+
+        spread(0, "k1b")
+        spread(4, "f1b")
+
+        def second(c):
+            for j in range(16):
+                tt(T["mx%d" % c][:, j::16], T["s%d" % c][:, j::16], T.px[:, c], ALU.max, ["s%d" % c, "px"], [("mx%d" % c, 64 * j, 64 * j + 64)])
+            pass_("pe", 64 * c, "SEL", "mx%d" % c, False, c == 3)
+
+        second(0)
+        ts(T.pone[:], T.pb[:], T.col[:, 3:4], ALU.is_equal, ["pb", ("col", 3, 4)], ["pone"])
+        tt(T.HPk[:], T.pone[:, 0:256], T.P4[:], ALU.mult, [("pone", 0, 256), "P4"], ["HPk"])
+        tt(T.HPf[:], T.pone[:, 256:512], T.P4[:], ALU.mult, [("pone", 256, 512), "P4"], ["HPf"])
+        for rl in range(4):
+            mm(T.pn[:, 0:4, rl, :], T.BLKF[:], T.HPk[:, :, :, rl], True, True, ["BLKF", "HPk"], [("pn", 0, 256)])
+        for q in range(16):
+            mm(T.ps[:, 256:272], T.SELN[:, q, :], T.xn[:, :, q::16], q == 0, q == 15, ["SELN", "xn"], [("ps", 256, 272)])
+        spread(0, "kill")
+        for c in range(4):
+            src = "d%d" % c if c < 3 else "rl3"
+            act(T.ak[:, 64 * c:64 * c + 64], T[src][:].indirect(T.offK[:, 4 * c:4 * c + 4]), AF.Abs, [src, "offK"], [("ak", 64 * c, 64 * c + 64)],
+                scale=1.0 if c < 3 else 2.0)
+        for c in range(4):
+            act(T.yk_[:, 64 * c:64 * c + 64], T["y%d" % c][:].indirect(T.offK[:, 4 * c:4 * c + 4]), AF.Copy, ["y%d" % c, "offK"], [("yk_", 64 * c, 64 * c + 64)])
+        act(T.sw[:], T.ak[:], AF.Sign, ["ak"], ["sw"], scale=-1.0, bias=32.5)
+        act(T.sy[:], T.yk_[:], AF.Sign, ["yk_"], ["sy"], scale=-1.0, bias=127.5)
+        second(1)
+        ts(T.b1[:], T.pn[:, 0:4], T.col[:, 5:6], ALU.mult, [("pn", 0, 256), ("col", 5, 6)], ["b1"])
+        ts(T.b2[:], T.b1[:], 4096, ALU.bitwise_and, ["b1"], ["b2"])
+        ts(T.FB[:], T.b2[:], 1.0 / 2048, ALU.mult, ["b2"], ["FB"], -1.0, ALU.add)
+        for i in range(8):
+            ts(T.BD[:, :, i, :], T.FB[:], T.GM[:, i:i + 1], ALU.mult, ["FB", "GM"], [("BD", 256 * i, 256 * i + 256)])
+        for rl in range(4):
+            mm(T.pn[:, 4:8, rl, :], T.BLK0[:], T.HPf[:, :, :, rl], True, True, ["BLK0", "HPf"], [("pn", 256, 512)])
+        act(T.a1[:], T.pn[:, 4:8], AF.Copy, [("pn", 256, 512)], ["a1"])
+        for q in range(16):
+            mm(T.ps[:, 272:288], T.SELW[:, q, :], T.FB[:, q::16], q == 0, q == 15, ["SELW", "FB"], [("ps", 272, 288)])
+        mm(T.ps[:, 288:304], T.BLK[:], T.kill[:], True, True, ["BLK", "kill"], [("ps", 288, 304)])
+        tt(T.pb[:, 4:8], T.t2[:], T.pb[:, 0:4], ALU.mult, ["t2", ("pb", 0, 256)], [("pb", 256, 512)])
+        tt(T.pw[:], T.pb[:, 4:8], T.Pf[:], ALU.add, [("pb", 256, 512), "Pf"], ["pw"])
+        ts(T.px_[:], T.pw[:], 4095, ALU.bitwise_and, ["pw"], ["px_"])
+        if last:
+            cp(T.pout[:], T.px_[:], ["px_"], ["pout"])
+            dma("y", [(T.yp[:], T.pout[:], [], ["pout"])])
+        else:
+            cp(T.pu[:], T.px_[:], ["px_"], ["pu"])
+            send("pu", "pl%d" % (t + 1), prv, "rp%d" % (t + 1), "lp%d" % (t + 1))
+        for bank, rrs in (("pg", (12, 13)), ("pk", (14, 15)), ("pone", (8, 9)), ("pb", (10, 11)), ("pg", (4, 5, 6, 7)), ("pk", (0, 1, 2, 3))):
+            lo = 0
+            todo = []
+            for rr in rrs:
+                rh, rl = rr // 4, rr % 4
+                n = 64 * (rh + 1)
+                G = T[bank][:, lo // 64:(lo + n) // 64] if bank == "pb" else T[bank][:, lo:lo + n]
+                mm(G, T.BD[:, rr, :, :], T.FB[:, 0:n], True, False, ["BD", "FB"], [(bank, lo, lo + n)])
+                G2 = T[bank][:, (lo + n) // 64 - 1:(lo + n) // 64] if bank == "pb" else T[bank][:, lo + n - 64:lo + n]
+                mm(G2, T.ID[:], T.TRB[:, rl, :], False, True, ["ID", "TRB"], [(bank, lo, lo + n)])
+                todo.append((rr, n, lo, G))
+                lo += n
+            for rr, n, lo, G in todo:
+                act(T.junk[:, 256 * rr:256 * rr + n], G, AF.Relu, [(bank, lo, lo + n)], [("cnt", rr, rr + 1), ("junk", 256 * rr, 256 * rr + n)], bias=-15.0,
+                    accum_out=T.sf[:, CN + rr:CN + rr + 1])
+        ts(T.xz[:, 0::16], T.ps[:, 256:272], -1.0, ALU.mult, [("ps", 256, 272)], ["xz"], 480.0, ALU.add)
+        q1("pr4", "pr", 4096.0, ALU.mult)
+        q1("bs", "pr", -512.0, ALU.mult, 4352.0, ALU.add)
+        scan(T.xb[:], T.BC0[:], T.xz[:], ALU.mult, ALU.add, ["BC0", "xz"], ["xb"])
+        q2("bs2", "bs", "CB", ALU.add)
+        second(2)
+        if not last:
+            second(3)
+        ts(T.pn[:, 0:4], T.sw[:], 1.0, ALU.add, ["sw"], [("pn", 0, 256)], 64.0, ALU.mult)
+        tt(m("w1"), T.ps[:, 272:288], T.DMH[:], ALU.subtract, [("ps", 272, 288), "DMH"], ["w1"])
+        tt(T.e2[:], T.pn[:, 0:4], T.sy[:], ALU.mult, [("pn", 0, 256), "sy"], ["e2"])
+        q1("nd", "cnt", 0.5, ALU.is_lt)
+        q2("win", "nd", "pr", ALU.mult)
+        q2("w2", "w1", "win", ALU.mult)
+        q2("w3", "w2", "DM", ALU.add)
+        cp(T.offX[:], m("w3"), ["w3"], ["offX"])
+        tt(T.X[:].indirect(T.offX[:]), T.yk_[:], T.e2[:], ALU.add, ["yk_", "e2", "offX"], ["X"])
+        if last:
+            dma("y", [(T.yx[:], T.X[:, 0:4096], [], [("X", 0, 4096)])])
+            second(3)
+        tt(T.nn[:], T.pe[:], T.xb[:], ALU.is_ge, ["pe", "xb"], ["nn"])
+        scan(T.fs[:], T.RSE[:], T.nn[:], ALU.add, ALU.min, ["RSE", "nn"], ["fs"])
+        tt(m("o1"), T.fs[:, 15::16], m("pr4"), ALU.mult, ["fs", "pr4"], ["o1"])
+        q2("o2", "o1", "bs2", ALU.add)
+        cp(T.offV[:], m("o2"), ["o2"], ["offV"])
+        for c in range(4):
+            tt(T.kp[:, c, :], T.KS[:].indirect(T.offV[:, 4 * c:4 * c + 4]), T.a1[:, 64 * c:64 * c + 64], ALU.add, ["KS", "offV", "a1"], [("kp", 64 * c, 64 * c + 64)])
+        dst = "kout" if last else "ku"
+        for rl in range(4):
+            cp(T[dst][:, :, :, rl], T.kp[:, :, 16 * rl:16 * rl + 16], ["kp"], [(dst, 64 * rl, 64 * rl + 64)])
+        if last:
+            dma("y", [(T.yk[:], T.kout[:], [], ["kout"])])
+        else:
+            send("ku", "kl%d" % (t + 1), nxt, "rk%d" % (t + 1), "lk%d" % (t + 1))
+        if not last:
+            op("v", lambda: g.vector.tensor_reduce(T.A1[:, 0:1], T.ps[:, 288:304], AxisListType.X, ALU.add), [("ps", 288, 304)], ["A1"])
+            tt(T.A[:, 0:1], T.A[:, 0:1], T.A1[:, 0:1], ALU.add, ["A", "A1"], ["A"])
+            cp(T.Ai[:, 0:1], T.A[:, 0:1], ["A"], [("Ai", 0, 1)])
+            ts(T.Ai[:, 1:2], T.Ai[:, 0:1], 15, ALU.bitwise_and, [("Ai", 0, 1)], [("Ai", 1, 2)])
+            ts(T.thr[:, 0:1], T.Ai[:, 1:2], 2.0, ALU.mult, [("Ai", 1, 2)], ["thr"], 520.0, ALU.add)
+    for sem in sorted(total):
+        if waited.get(("g", sem), 0) < total[sem]:
+            g.wait_ge(T.sem[sem], total[sem])

@@ -1,64 +1,57 @@
-from concourse.mybir import AluOpType as ALU, AxisListType, ActivationFunctionType as AF
+from concourse.mybir import AluOpType as ALU, ActivationFunctionType as AF
 
 BIG = 1.0e6
 _B = "bfloat16"
 _F = "float32"
+_H = "float16"
 _I = "int32"
 _U = "uint16"
+KW = 24 * 128
 SCRATCH = {
     "X": ("sbuf", [128, 4352], _B),
-    "KS": ("sbuf", [128, 4608], _F),
-    "kd": ("dram", [8, 33, 256], _F),
-    "kz": ("dram", [8, 4096], _F),
-    "cm": ("sbuf", [128, 256], _F),
-    "k15": ("sbuf", [128, 256], _F),
-    "kin": ("sbuf", [128, 256], _I), "pin": ("sbuf", [128, 256], _I),
-    "kl0": ("sbuf", [128, 256], _U), "kl1": ("sbuf", [128, 256], _U), "kl2": ("sbuf", [128, 256], _U),
-    "pl0": ("sbuf", [128, 256], _U), "pl1": ("sbuf", [128, 256], _U), "pl2": ("sbuf", [128, 256], _U),
-    "ku": ("sbuf", [128, 4, 16, 4], _U), "pu": ("sbuf", [128, 256], _U),
-    "kout": ("sbuf", [128, 4, 16, 4], _F), "pout": ("sbuf", [128, 256], _F),
-    "Pf": ("sbuf", [128, 256], _F), "P4": ("sbuf", [128, 256], _F),
+    "s": ("sbuf", [128, 4096], _B), "d": ("sbuf", [128, 4096], _B), "rl": ("sbuf", [128, 4096], _B),
+    "ab": ("sbuf", [128, 256, 16], _B),
+    "KS": ("sbuf", [128, 2 * KW], _F), "PS": ("sbuf", [128, 4352], _F),
+    "kd": ("dram", [2, 8, 33, 128], _F),
+    "k15": ("sbuf", [128, 256], _F), "kin": ("sbuf", [128, 256], _I),
+    "ku": ("sbuf", [128, 256], _U), "kp": ("sbuf", [128, 256], _F), "a1": ("sbuf", [128, 256], _F),
+    "pu": ("sbuf", [128, 256], _U), "Pf": ("sbuf", [128, 256], _F), "po": ("sbuf", [128, 256], _I), "pout": ("sbuf", [128, 256], _F),
+    "Pm": ("sbuf", [128, 2, 4, 2, 16], _H), "PT": ("sbuf", [128, 2, 4, 2, 16], _H),
     "t1": ("sbuf", [128, 256], _I), "t2": ("sbuf", [128, 256], _I),
-    "pw": ("sbuf", [128, 256], _I), "px_": ("sbuf", [128, 256], _I),
-    "pid": ("sbuf", [128, 4], _I), "row": ("sbuf", [128, 128], _I), "row2": ("sbuf", [128, 128], _I),
-    "rowm": ("sbuf", [128, 128], _F), "rowi": ("sbuf", [128, 128], _F),
-    "col": ("sbuf", [128, 16], _F), "r16": ("sbuf", [128, 16], _F), "OH": ("sbuf", [128, 16], _F),
-    "GM": ("sbuf", [128, 8], _F), "pw2": ("sbuf", [128, 64], _F),
-    "SEL": ("sbuf", [128, 16, 128], _B), "SELN": ("sbuf", [128, 16, 128], _B),
-    "SELP": ("sbuf", [128, 16, 128], _B), "IDN": ("sbuf", [128, 128], _B),
-    "SELW": ("sbuf", [128, 16, 128], _B), "SELT": ("sbuf", [128, 16, 128], _B),
-    "BLK": ("sbuf", [128, 128], _B), "BLKF": ("sbuf", [128, 128], _F), "BLK0": ("sbuf", [128, 128], _F),
-    "S15": ("sbuf", [128, 128], _F), "ID": ("sbuf", [128, 128], _B), "IDW": ("sbuf", [128, 128], _B),
-    "JR": ("sbuf", [128, 256], _B), "JRF": ("sbuf", [128, 256], _F), "Z0": ("sbuf", [128, 256], _B),
-    "RST": ("sbuf", [128, 256], _F), "RSE": ("sbuf", [128, 256], _F), "BC0": ("sbuf", [128, 256], _F),
-    "C16": ("sbuf", [128, 16], _F), "CB": ("sbuf", [128, 16], _F), "DM": ("sbuf", [128, 16], _F),
-    "DMH": ("sbuf", [128, 16], _F), "TRB": ("sbuf", [128, 4, 64], _B), "tri": ("sbuf", [128, 64], _F),
-    "us": ("sbuf", [128, 256], _F), "key": ("sbuf", [128, 256], _F), "R": ("sbuf", [128, 256], _F), "sg": ("sbuf", [128, 256], _B),
-    "sf": ("sbuf", [128, 384], _F), "si": ("sbuf", [128, 128], _I),
-    "offF": ("sbuf", [128, 16], _U), "offK": ("sbuf", [128, 16], _U), "offV": ("sbuf", [128, 16], _U),
-    "offX": ("sbuf", [128, 16], _U),
-    "kill": ("sbuf", [128, 16], _B), "k1b": ("sbuf", [128, 16], _B), "f1b": ("sbuf", [128, 16], _B),
-    "A": ("sbuf", [128, 4], _F), "A1": ("sbuf", [128, 4], _F), "Ai": ("sbuf", [128, 4], _I), "thr": ("sbuf", [128, 4], _F),
-    "xn": ("sbuf", [128, 4, 64], _B), "xz": ("sbuf", [128, 256], _F), "xb": ("sbuf", [128, 256], _F),
-    "nn": ("sbuf", [128, 256], _F), "fs": ("sbuf", [128, 256], _F), "a1": ("sbuf", [128, 256], _F),
-    "kp": ("sbuf", [128, 4, 64], _F),
-    "HPk": ("sbuf", [128, 4, 16, 4], _F), "HPf": ("sbuf", [128, 4, 16, 4], _F),
-    "b1": ("sbuf", [128, 256], _I), "b2": ("sbuf", [128, 256], _I), "FB": ("sbuf", [128, 256], _B),
-    "BD": ("sbuf", [128, 16, 8, 16], _B), "junk": ("sbuf", [128, 4096], _B),
-    "ak": ("sbuf", [128, 256], _B), "yk_": ("sbuf", [128, 256], _B), "sw": ("sbuf", [128, 256], _B),
-    "sy": ("sbuf", [128, 256], _B), "e2": ("sbuf", [128, 256], _B),
-    "pk": ("psum", [128, 512], _F), "ps": ("psum", [128, 512], _F), "px": ("psum", [128, 4, 16, 4], _F),
-    "pe": ("psum", [128, 256], _F), "pb": ("psum", [128, 8, 16, 4], _F), "pone": ("psum", [128, 512], _F),
-    "pn": ("psum", [128, 8, 4, 16], _F), "pg": ("psum", [128, 512], _F),
+    "pid": ("sbuf", [128, 8], _I), "col": ("sbuf", [128, 24], _F), "rowi": ("sbuf", [128, 128], _F), "rowg": ("sbuf", [128, 128], _F),
+    "isel": ("sbuf", [128, 2048], _B), "iselt": ("sbuf", [128, 2048], _B),
+    "SEL": ("sbuf", [128, 16, 128], _B), "SEL2": ("sbuf", [128, 16, 128], _B), "SELN": ("sbuf", [128, 16, 128], _B),
+    "SELT": ("sbuf", [128, 16, 128], _H), "PERM": ("sbuf", [128, 4, 128], _H), "BLK": ("sbuf", [128, 128], _H),
+    "ID": ("sbuf", [128, 128], _B), "IDN": ("sbuf", [128, 128], _B), "ID64": ("sbuf", [128, 128], _B),
+    "IDF": ("sbuf", [128, 128], _F), "S15": ("sbuf", [128, 128], _F),
+    "JR": ("sbuf", [128, 256], _B), "CD": ("sbuf", [128, 256], _B),
+    "RST": ("sbuf", [128, 256], _F), "RSE": ("sbuf", [128, 256], _B), "RSD": ("sbuf", [128, 1024], _B),
+    "C16": ("sbuf", [128, 32], _F), "CB": ("sbuf", [128, 32], _F), "CV": ("sbuf", [128, 16], _F), "DM": ("sbuf", [128, 16], _F),
+    "DM8": ("sbuf", [128, 16], _F), "CW": ("sbuf", [128, 32], _F), "CP": ("sbuf", [128, 48], _F),
+    "R": ("sbuf", [128, 256], _F), "sg": ("sbuf", [128, 256], _B),
+    "sf": ("sbuf", [128, 320], _F), "si": ("sbuf", [128, 128], _I), "sh": ("sbuf", [128, 48], _H), "su": ("sbuf", [128, 128], _U),
+    "kc": ("sbuf", [128, 4], _F), "kj": ("sbuf", [128, 16], _F), "Ai": ("sbuf", [128, 4], _I), "thr": ("sbuf", [128, 4], _F),
+    "df": ("sbuf", [128, 256], _B), "sn": ("sbuf", [128, 256], _B), "xs": ("sbuf", [128, 256], _B),
+    "ns": ("sbuf", [128, 256], _B), "fs": ("sbuf", [128, 256], _B),
+    "NE": ("sbuf", [128, 1024], _B), "FE": ("sbuf", [128, 1024], _B),
+    "ak": ("sbuf", [128, 256], _B), "yv": ("sbuf", [128, 256], _B), "nr": ("sbuf", [128, 256], _B), "e2": ("sbuf", [128, 256], _B),
+    "pk": ("psum", [128, 512], _F), "ps": ("psum", [128, 512], _F), "pa": ("psum", [128, 2, 4, 4, 16], _F), "pb": ("psum", [128, 8, 64], _F),
 }
-for _c in range(4):
-    for _n in ("y", "s", "d", "rl", "mx"):
-        SCRATCH["%s%d" % (_n, _c)] = ("sbuf", [128, 1024], _B)
-PSUM = ("pk", "ps", "px", "pe", "pb", "pone", "pn", "pg")
-SEMAPHORES = ["qv", "qs", "qt", "qg"] + ["dm%d" % i for i in range(24)] + ["rk1", "rk2", "rp1", "rp2", "lk1", "lk2", "lp1", "lp2"]
 ROUNDS = 3
-SMF = ("w", "h1", "h2", "fo", "ko", "plt", "nk", "pr", "k1", "f1", "pr4", "bs", "bs2", "o1", "o2", "cnt", "nd", "win", "w1", "w2", "w3")
-SMI = ("ki", "zm", "ub", "kk", "h3", "fi")
+for _c in range(4):
+    SCRATCH["db%d" % _c] = ("psum", [128, 64, 8], _F)
+for _t in range(ROUNDS):
+    SCRATCH["PW%d" % _t] = ("sbuf", [128, 512], _I)
+    SCRATCH["kl%d" % _t] = ("sbuf", [128, 256], _U)
+    SCRATCH["kf%d" % _t] = ("sbuf", [128, 256], _F)
+PSUM = ("pk", "ps", "pa", "pb", "db0", "db1", "db2", "db3")
+SEMAPHORES = (["qv", "qs", "qt", "qg"] + ["dm%d" % i for i in range(40)]
+              + [a + b + str(t) for a in "rl" for b in ("p", "u0", "u1", "f0", "f1") for t in (1, 2)])
+SMALL = {"sf": ("w", "z1", "ko", "fo", "oP", "oN", "h2", "plt", "fa", "t32", "w1", "w1p", "eq", "w2", "w3", "o1", "o2"),
+         "si": ("ki", "nm", "kk", "fi", "u2", "zm", "h3"),
+         "sh": ("kl", "pr", "t16"),
+         "su": ("offK", "offF", "offP", "offN", "offY", "offX", "offV")}
+WHERE = {n: (b, 16 * i) for b in SMALL for i, n in enumerate(SMALL[b])}
 
 
 def rank_program(g, core, T, topo):
@@ -79,14 +72,11 @@ def rank_program(g, core, T, topo):
             for name, lo, hi in regs:
                 bank = name in PSUM
                 for (l, h, oq, sem, val, ow) in log.get(name, []):
-                    if not bank and (h <= lo or hi <= l):
+                    apart = h <= lo or hi <= l
+                    if not bank and apart:
                         continue
                     if oq == q:
-                        if q == "t" or (not ow):
-                            continue
-                        if is_w and bank and (h <= lo or hi <= l):
-                            continue
-                        if not is_w and (h <= lo or hi <= l):
+                        if q == "t" or (not ow) or apart:
                             continue
                     elif not bank and not ow and not is_w:
                         continue
@@ -108,28 +98,24 @@ def rank_program(g, core, T, topo):
                 old.append((lo, hi, q, sem, val, is_w))
                 log[name] = old
 
-    def m(name):
-        if name in SMF:
-            i = 16 * SMF.index(name)
-            return T.sf[:, i:i + 16]
-        if name in SMI:
-            i = 16 * SMI.index(name)
-            return T.si[:, i:i + 16]
-        return T[name][:]
+    def m(name, n=16, at=0):
+        b, i = WHERE[name]
+        return T[b][:, i + at:i + at + n]
 
-    def flat(name, lo=None, hi=None):
-        if lo is None and (name in SMF or name in SMI):
-            return (name, 0, 16)
-        if lo is None:
-            n = 1
-            for x in SCRATCH[name][1][1:]:
-                n *= x
-            return (name, 0, n)
-        return (name, lo, hi)
+    def reg(r):
+        if isinstance(r, tuple):
+            if r[0] in WHERE:
+                b, i = WHERE[r[0]]
+                return (b, i + r[1], i + r[2])
+            return r
+        if r in WHERE:
+            b, i = WHERE[r]
+            return (b, i, i + 16)
+        return (r, 0, 1 << 20)
 
     def op(q, fn, reads, writes):
-        reads = [flat(*r) if isinstance(r, tuple) else flat(r) for r in reads]
-        writes = [flat(*r) if isinstance(r, tuple) else flat(r) for r in writes]
+        reads = [reg(r) for r in reads]
+        writes = [reg(r) for r in writes]
         deps(q, reads, writes)
         count[q] += 1
         sem = "q" + q
@@ -144,8 +130,8 @@ def rank_program(g, core, T, topo):
         total[sem] = val
         done = []
         for out, in_, w, r in pairs:
-            r = [flat(*x) if isinstance(x, tuple) else flat(x) for x in r]
-            w = [flat(*x) if isinstance(x, tuple) else flat(x) for x in w]
+            r = [reg(x) for x in r]
+            w = [reg(x) for x in w]
             deps(q, r, w)
             eng[q].dma_start(out, in_).then_inc(T.sem[sem], 16)
             done.append((r, w))
@@ -153,7 +139,8 @@ def rank_program(g, core, T, topo):
             note("dma", sem, val, r, [])
         for r, w in done:
             for x in w:
-                log.setdefault(x[0], []).append((x[1], x[2], "dma", sem, val, True))
+                log[x[0]] = [e for e in log.get(x[0], []) if e[3] == sem or not (x[1] <= e[0] and e[1] <= x[2])]
+                log[x[0]].append((x[1], x[2], "dma", sem, val, True))
 
     def tt(out, a, b, o, reads, writes):
         op("v", lambda: g.vector.tensor_tensor(out, a, b, o), reads, writes)
@@ -164,17 +151,21 @@ def rank_program(g, core, T, topo):
         else:
             op("v", lambda: g.vector.tensor_scalar(out, a, s1, s2, o1, o2), reads, writes)
 
-    def q1(out, a, s1, o1, s2=None, o2=None):
-        ts(m(out), m(a), s1, o1, [a], [out], s2, o2)
+    def q1(out, a, s1, o1, s2=None, o2=None, n=16, at=0):
+        ts(m(out, n, at), m(a, n, at), s1, o1, [(a, at, at + n)], [(out, at, at + n)], s2, o2)
 
-    def q2(out, a, b, o):
-        tt(m(out), m(a), m(b), o, [a, b], [out])
+    def q2(out, a, b, o, n=16, at=0):
+        bb = m(b, n, at) if b in WHERE else T[b][:, at:at + n]
+        tt(m(out, n, at), m(a, n, at), bb, o, [(a, at, at + n), (b, at, at + n)], [(out, at, at + n)])
 
     def cp(out, a, reads, writes):
         op("v", lambda: g.vector.tensor_copy(out, a), reads, writes)
 
+    def qc(out, a, n=16):
+        cp(m(out, n), m(a, n), [(a, 0, n)], [(out, 0, n)])
+
     def fill(name, c, ap=None):
-        op("v", lambda: g.vector.memset(T[name][:] if ap is None else ap, c), [], [name])
+        op("v", lambda: g.vector.memset(T[name][:] if ap is None else ap, c), [] if ap is None else [name], [name])
 
     def act(out, a, f, reads, writes, **kw):
         op("s", lambda: g.scalar.activation(out, a, f, **kw), reads, writes)
@@ -185,314 +176,371 @@ def rank_program(g, core, T, topo):
     def scan(out, a, b, o1, o2, reads, writes):
         op("v", lambda: g.vector.tensor_tensor_scan(out, a, b, 0.0, o1, o2), reads, writes)
 
-    def iota(name, ap, pat, base, mult):
-        op("g", lambda: g.iota(ap, pat, base, mult, allow_small_or_imprecise_dtypes=True), [], [name])
+    def iota(name, pat, base, mult=0, ap=None, w=None):
+        op("g", lambda: g.iota(T[name][:] if ap is None else ap, pat, base, mult, allow_small_or_imprecise_dtypes=True), [], [w or name])
 
-    dma("y", [(T.pin[:], T.ph[:], ["pin"], [])])
+    def col(i):
+        return T.col[:, i:i + 1]
+
+    XT = ("X", 0, 4096)
     dma("y", [(T.kin[:], T.ka[:], ["kin"], [])])
-    dma("y", [(T.X[:, 0:4096], T.x0[:], [("X", 0, 4096)], [])])
-    iota("pid", T.pid[:, 0:1], [[0, 1]], 0, 1)
-    iota("row", T.row[:], [[1, 128]], 0, 0)
-    iota("r16", T.r16[:], [[1, 16]], 0, 0)
-    iota("JRF", T.JRF[:], [[0, 16], [4, 16]], 1, 0)
-    iota("C16", T.C16[:], [[0, 4], [16, 4]], 0, 0)
-    iota("CB", T.CB[:], [[64, 4], [1, 4]], 0, 0)
-    iota("DM", T.DM[:], [[16, 16]], 4096, 0)
-    iota("tri", T.tri[:], [[1, 4], [4, 16]], 0, 0)
-    fill("cm", -4096.0)
-    dma("y", [(T.kz[:], T.cm[:], ["kz"], ["cm"]), (T.kd[:, 0, :], T.cm[0:8, :], [("kd", 0, 1)], ["cm"])])
-    dma("y", [(T.KS[0::16, 0:4096], T.kz[:], [("KS", 0, 4096)], ["kz"])])
-    fill("SEL", 0.0)
-    ts(T.pid[:, 1:2], T.pid[:, 0:1], 15, ALU.bitwise_and, [("pid", 0, 1)], [("pid", 1, 2)])
-    ts(T.pid[:, 2:3], T.pid[:, 0:1], 4, ALU.arith_shift_right, [("pid", 0, 1)], [("pid", 2, 3)])
-    ts(T.row2[:], T.row[:], 4, ALU.arith_shift_right, ["row"], ["row2"])
-    cp(T.rowi[:], T.row[:], ["row"], ["rowi"])
-    cp(T.col[:, 0:3], T.pid[:, 0:3], [("pid", 0, 3)], [("col", 0, 3)])
-    cp(T.rowm[:], T.row2[:], ["row2"], ["rowm"])
-    ts(T.col[:, 3:4], T.col[:, 1:2], 1.0, ALU.add, [("col", 1, 2)], [("col", 3, 4)])
-    ts(T.col[:, 4:5], T.col[:, 1:2], 64.0, ALU.mult, [("col", 1, 2)], [("col", 4, 5)])
-    ts(T.col[:, 7:8], T.col[:, 1:2], 4.0, ALU.mult, [("col", 1, 2)], [("col", 7, 8)])
-    ts(T.BLK[:], T.rowm[:], T.col[:, 2:3], ALU.is_equal, ["rowm", ("col", 2, 3)], ["BLK"])
-    ts(T.OH[:], T.r16[:], T.col[:, 1:2], ALU.is_equal, ["r16", ("col", 1, 2)], ["OH"])
-    for q in range(16):
-        cp(T.SEL[:, q, q::16], T.BLK[:, q::16], ["BLK"], [("SEL", 128 * q, 128 * q + 128)])
-    act(T.SELN[:], T.SEL[:], AF.Copy, ["SEL"], ["SELN"], scale=-0.5)
-    act(T.SELP[:], T.SEL[:], AF.Copy, ["SEL"], ["SELP"], scale=0.5)
-    ts(T.ID[:], T.rowi[:], T.col[:, 0:1], ALU.is_equal, ["rowi", ("col", 0, 1)], ["ID"])
-    ts(T.IDW[:], T.ID[:], 1.0 / 128, ALU.mult, ["ID"], ["IDW"])
-    ts(T.IDN[:], T.ID[:], -1.0, ALU.mult, ["ID"], ["IDN"])
-    ts(T.JR[:], T.JRF[:], 1.0 / 128, ALU.mult, ["JRF"], ["JR"])
+    dma("y", [(T.PW0[:, 0:256], T.ph[:], [("PW0", 0, 256)], [])])
+    dma("y", [(T.X[:, 0:4096], T.x0[:], [XT], [])])
+    iota("pid", [[0, 1]], 0, 1, T.pid[:, 0:1])
+    iota("rowi", [[1, 128]], 0)
+    iota("rowg", [[1, 8], [0, 16]], 0)
+    iota("isel", [[-1, 16], [32, 8], [1, 16]], 0)
+    iota("JR", [[0, 16], [4, 16]], 2)
+    iota("C16", [[0, 2], [1024, 4], [16, 4]], 0)
+    iota("CB", [[0, 2], [64, 4], [1, 4]], 0)
+    iota("CV", [[0, 2], [64, 2], [1, 4]], 23 * 128)
+    iota("DM", [[16, 16]], 4096)
+    iota("CW", [[2, 2], [0, 16]], -1)
+    for i in range(3):
+        iota("CP", [[0, 4], [4 ** i, 4]], -63, 0, T.CP[:, 16 * i:16 * i + 16], ("CP", 16 * i, 16 * i + 16))
+    iota("iselt", [[1, 16], [32, 8], [0, 16]], 0)
+    for h in range(2):
+        iota("KS", [[0, 768]], 0, 0, T.KS[:, KW * h + 2176:KW * h + 2944], ("KS", 4 * h + 1, 4 * h + 2))
+    fill("RSD", -1.0 / 128)
+    fill("RSD", BIG, T.RSD[:, 0::64])
+    for a in range(0, 4352, 1024):
+        n = min(1024, 4352 - a)
+        act(T.PS[:, a:a + n], T.RSD[:, 0:n], AF.Copy, ["RSD"], [("PS", a, a + n)], scale=0.0)
+    dma("y", [(T.KS[0::16, KW * h:KW * h + 2048], T.PS[1::16, 0:2048], [("KS", 4 * h, 4 * h + 1)], [("PS", 0, 2048)]) for h in range(2)]
+        + [(T.kd[h, :, 0, :], T.PS[1::16, 0:128], [("kd", 40 * h, 40 * h + 1)], [("PS", 0, 128)]) for h in range(2)])
+    pid = lambda i: T.pid[:, i:i + 1]
+    for i, sh, mk in ((1, 0, 15), (2, 4, 7), (3, 0, 3), (4, 2, 3), (5, 4, 1)):
+        ts(pid(i), pid(0), sh, ALU.arith_shift_right, [("pid", 0, 1)], [("pid", i, i + 1)], mk, ALU.bitwise_and)
+    cp(T.col[:, 0:6], T.pid[:, 0:6], [("pid", 0, 6)], [("col", 0, 6)])
+    for i, a, s1, s2 in ((6, 2, 32.0, 0.0), (7, 2, 32.0, col(1)), (8, 1, 64.0, 0.0), (9, 1, 4.0, 0.0), (10, 0, 1.0, -16.0), (11, 0, 1.0, 16.0),
+                         (12, 5, -2.0 ** -14, 2.0 ** -14), (13, 5, 2.0 ** -14, 0.0), (14, 3, 16.0, col(4))):
+        ts(col(i), col(a), s1, ALU.mult, [("col", 0, 6)], [("col", i, i + 1)], s2, ALU.add)
+    ts(col(15), col(1), 15.0, ALU.is_equal, [("col", 0, 6)], [("col", 15, 16)])
+    ts(T.ID[:], T.rowi[:], col(0), ALU.is_equal, ["rowi", "col"], ["ID"])
+    ts(T.IDF[:], T.rowi[:], col(0), ALU.is_equal, ["rowi", "col"], ["IDF"])
+    ts(T.S15[:], T.rowg[:], col(2), ALU.is_equal, ["rowg", "col"], ["S15"], col(15), ALU.mult)
+    fill("CD", -992.0)
+    fill("thr", 48.0)
     cp(T.kl0[:], T.kin[:], ["kin"], ["kl0"])
-    cp(T.pl0[:], T.pin[:], ["pin"], ["pl0"])
-    fill("RST", -BIG)
-    op("v", lambda: g.vector.memset(T.RST[:, 0::16], BIG), ["RST"], ["RST"])
-    fill("thr", 520.0)
-    fill("A", 0.0)
-    ts(T.C16[:], T.C16[:], T.col[:, 4:5], ALU.add, ["C16", ("col", 4, 5)], ["C16"])
-    ts(T.CB[:], T.CB[:], T.col[:, 7:8], ALU.add, ["CB", ("col", 7, 8)], ["CB"])
-    ts(T.DM[:], T.DM[:], T.col[:, 1:2], ALU.add, ["DM", ("col", 1, 2)], ["DM"])
-    ts(T.DMH[:], T.DM[:], -2047.5, ALU.add, ["DM"], ["DMH"])
+    cp(T.kf0[:], T.kin[:], ["kin"], ["kf0"])
+
+    def constants1():
+        ts(T.ID64[:], T.ID[:], 1.0 / 64, ALU.mult, ["ID"], ["ID64"])
+        ts(T.IDN[:], T.ID[:], -1.0, ALU.mult, ["ID"], ["IDN"])
+        for name, w in (("SELN", -1.0), ("SEL2", 2.0), ("SEL", 1.0)):
+            ts(T[name][:], T.isel[:], col(6), ALU.is_equal, ["isel", "col"], [name], w, ALU.mult)
+        ts(T.JR[:], T.JR[:], 1.0 / 64, ALU.mult, ["JR"], ["JR"])
 
     def constants2():
-        for q in range(16):
-            ts(T.SELT[:, q, :], T.BLK[:], T.OH[:, q:q + 1], ALU.mult, ["BLK", "OH"], [("SELT", 128 * q, 128 * q + 128)])
-        cp(T.BLKF[:], T.BLK[:], ["BLK"], ["BLKF"])
-        fill("BLK0", 0.0)
-        op("v", lambda: g.vector.tensor_copy(T.BLK0[:, 0::16], T.BLK[:, 0::16]), ["BLK", "BLK0"], ["BLK0"])
-        ts(T.S15[:], T.BLK[:], T.OH[:, 15:16], ALU.mult, ["BLK", "OH"], ["S15"])
-        fill("Z0", 0.0)
-        fill("RSE", -1.0 / 16)
-        op("v", lambda: g.vector.memset(T.RSE[:, 0::16], BIG), ["RSE"], ["RSE"])
-        fill("BC0", 1.0)
-        op("v", lambda: g.vector.memset(T.BC0[:, 0::16], 0.0), ["BC0"], ["BC0"])
-        fill("xz", 0.0)
-        ts(T.GM[:], T.r16[:, 0:8], T.col[:, 2:3], ALU.is_equal, ["r16", ("col", 2, 3)], ["GM"])
-        fill("pw2", 0.5, T.pw2[:, 0:16])
-        fill("pw2", 2.0, T.pw2[:, 16:32])
-        op("v", lambda: g.vector.tensor_tensor_scan(T.pw2[:, 32:48], T.pw2[:, 0:16], T.Z0[:, 0:16], 8192.0, ALU.mult, ALU.add), ["pw2", "Z0"], ["pw2"])
-        op("v", lambda: g.vector.tensor_tensor_scan(T.pw2[:, 48:64], T.pw2[:, 16:32], T.Z0[:, 0:16], 0.25, ALU.mult, ALU.add), ["pw2", "Z0"], ["pw2"])
-        op("v", lambda: g.vector.memset(T.pw2[:, 45:48], 0.0), ["pw2"], ["pw2"])
-        op("v", lambda: g.vector.memset(T.pw2[:, 60:64], 0.0), ["pw2"], ["pw2"])
-        for i in (0, 1):
-            a = 32 + 16 * i
-            tt(T.pw2[:, 16 * i:16 * i + 16], T.pw2[:, a:a + 16], T.OH[:], ALU.mult, ["pw2", "OH"], ["pw2"])
-            op("v", lambda i=i: g.vector.tensor_reduce(T.col[:, 5 + i:6 + i], T.pw2[:, 16 * i:16 * i + 16], AxisListType.X, ALU.add), ["pw2"], [("col", 5 + i, 6 + i)])
-        for rl in range(4):
-            ts(T.col[:, 8 + rl:9 + rl], T.col[:, 7:8], float(rl), ALU.add, [("col", 7, 8)], [("col", 8 + rl, 9 + rl)])
-        for rl in range(4):
-            ts(T.TRB[:, rl, :], T.tri[:], T.col[:, 8 + rl:9 + rl], ALU.is_ge, ["tri", ("col", 8 + rl, 9 + rl)], [("TRB", 64 * rl, 64 * rl + 64)], -64.0, ALU.mult)
+        for h in range(2):
+            for g2 in range(2):
+                ts(T.PERM[:, 2 * h + g2, :], T.rowi[:], col((10, 0, 11)[g2 - h + 1]), ALU.is_equal, ["rowi", "col"], [("PERM", 2 * h + g2, 2 * h + g2 + 1)],
+                   col(12 + h), ALU.mult)
+        fill("RST", -BIG)
+        fill("RST", BIG, T.RST[:, 0::16])
 
-    def landed(name, sem, val):
-        total[sem] = val
-        log.setdefault(name, []).append((0, 256, "rem", sem, val, True))
+    def constants3():
+        for name, c in (("C16", 8), ("CB", 9), ("DM", 1)):
+            ts(T[name][:], T[name][:], col(c), ALU.add, [name, "col"], [name])
+        ts(T.SELT[:], T.iselt[:], col(7), ALU.is_equal, ["iselt", "col"], ["SELT"])
 
-    def send(name, land, dst, rs, ls):
-        rid, pid, _ = topo.addr(dst)
-        es = topo.engines(core, dst)[:8]
-        mask = sum(1 << e for e in es)
-        regs = [flat(name)]
-        deps("g", regs, [])
-        g.remote_dma(T[land][:], T[name][:], T.sem[rs], T.sem[ls], pid, rid, mask)
-        total[ls] = len(es)
-        note("rem", ls, len(es), regs, [])
+    def constants4():
+        ts(T.CV[:], T.CV[:], col(9), ALU.add, ["CV", "col"], ["CV"], 0.25, ALU.mult)
+        ts(T.DM8[:], T.DM[:], 256.0, ALU.mult, ["DM"], ["DM8"])
+        for i, c in enumerate((9, 14, 1)):
+            r = ("CP", 16 * i, 16 * i + 16)
+            ts(T.CP[:, r[1]:r[2]], T.CP[:, r[1]:r[2]], col(c), ALU.add, [r, "col"], [r], 1.0 / 128, ALU.mult)
+        ts(T.BLK[:], T.rowg[:], col(2), ALU.is_equal, ["rowg", "col"], ["BLK"])
+        fill("RSE", -1.0 / 8)
+        fill("RSE", BIG, T.RSE[:, 0::16])
+        op("v", lambda: g.vector.memset(T.X[:, 4096:4352], 0.0), [], [("X", 4096, 4352)])
 
     nxt = T.cores[(rank + 1) % n_ranks]
     prv = T.cores[(rank - 1) % n_ranks]
-    KB = 17 * 256
-    CN = 16 * SMF.index("cnt")
 
+    def engines(dst, part):
+        es = topo.engines(core, dst)
+        n = len(es) // 2
+        return es[part * n:part * n + n]
+
+    def landed(r, sem, n):
+        total[sem] = n
+        r = reg(r)
+        log.setdefault(r[0], []).append((r[1], r[2], "rem", sem, n, True))
+
+    def send(src, r, land, dst, tag, part):
+        rid, pid_, _ = topo.addr(dst)
+        es = engines(dst, part)
+        regs = [reg(r)]
+        deps("g", regs, [])
+        g.remote_dma(land, src, T.sem["r" + tag], T.sem["l" + tag], pid_, rid, sum(1 << e for e in es))
+        total["l" + tag] = len(es)
+        note("rem", "l" + tag, len(es), regs, [])
+
+    def phage_forms(t):
+        pw = "PW%d" % t
+        if t:
+            landed((pw, 0, 256), "rp%d" % t, len(engines(nxt, 0)))
+        cp(T.pu[:], T[pw][:, 0:256], [(pw, 0, 256)], ["pu"])
+        cp(T.Pf[:], T[pw][:, 0:256], [(pw, 0, 256)], ["Pf"])
+        for rl in range(4):
+            ts(T.Pm[:, :, rl], T.pu[:, rl::4], -2048.0, ALU.add, ["pu"], [("Pm", rl, rl + 1)], 0.125, ALU.mult)
+        dma("y", [(T.PS[0::16, 256:4352], T.Pf[:], ["PS"], ["Pf"])])
+        op("v", lambda: g.vector.transpose(T.PT[:], T.Pm[:]), ["Pm"], ["PT"])
+
+    def shifted(t, h):
+        kf = "kf%d" % t
+        a, b = 128 * h, 128 * h + 128
+        if t:
+            landed((kf, a, b), "rf%d%d" % (h, t), len(engines(prv, 1)))
+        mm(T.pa[:, 0, 2 * h:2 * h + 2], T.S15[:], T[kf][:, a:b], True, True, ["S15", (kf, a, b)], [("pa", a, b)])
+        act(T.k15[:, a:b], T.pa[:, 0, 2 * h:2 * h + 2], AF.Copy, [("pa", a, b)], [("k15", a, b)])
+        o = 40 * h
+        dma("y", [(T.kd[h, :, 1:17, :], T[kf][:, a:b], [("kd", o + 1, o + 17)], [(kf, a, b)]),
+                  (T.kd[h, :, 17:33, :], T.k15[:, a:b], [("kd", o + 17, o + 33)], [("k15", a, b)])])
+
+    def shifted_in(t, h):
+        kf = "kf%d" % t
+        a, b = 128 * h, 128 * h + 128
+        o = 40 * h
+        w = [("KS", 4 * h + 2, 4 * h + 3)]
+        dma("y", [(T.KS[j::16, KW * h:KW * h + 2048], T.kd[h, :, j + 1:j + 17, :], w, [("kd", o, o + 33)]) for j in range(1, 16)]
+            + [(T.KS[:, KW * h + 2048:KW * h + 2176], T.kd[h, :, 0:16, :], w, [("kd", o, o + 33)]),
+               (T.KS[:, KW * h + 2944:KW * h + 3072], T[kf][:, a:b], w, [(kf, a, b)])])
+
+    def sgather(t, c):
+        kl = "kl%d" % t
+        if t and c % 2 == 0:
+            landed((kl, 64 * c, 64 * c + 128), "ru%d%d" % (c // 2, t), len(engines(prv, 0)))
+        act(T.s[:, 1024 * c:1024 * c + 1024], T.X[:, 0:4096].indirect(T[kl][:, 64 * c:64 * c + 64]), AF.Copy,
+            [XT, (kl, 64 * c, 64 * c + 64)], [("s", c, c + 1)])
+
+    def dgather(c):
+        tt(T.d[:, 1024 * c:1024 * c + 1024], T.X[:, 0:4096].indirect(T.pu[:, 64 * c:64 * c + 64]), T.s[:, 1024 * c:1024 * c + 1024], ALU.subtract,
+           [XT, "pu", ("s", c, c + 1)], [("d", c, c + 1)])
+
+    def lanes(out, w, sel, src, c, first, final):
+        for q in range(16):
+            a = 1024 * c + 64 * q
+            rhs = T.ab[:, a // 16:a // 16 + 4, :] if src == "ab" else T[src][:, a:a + 64]
+            r = ("ab", 2 * c, 2 * c + 2) if src == "ab" else (src, c, c + 1)
+            mm(out, T[sel][:, q, :], rhs, first and q == 0, final and q == 15, [sel, r], [w])
+
+    def key(c, sel, src):
+        lanes(T.pk[:, 64 * c:64 * c + 64], ("pk", 64 * c, 64 * c + 64), sel, src, c, False, False)
+
+    def names(c, final=False):
+        for g2 in range(2):
+            mm(T.pk[:, 64 * c:64 * c + 64], T.PERM[:, 2 * (c % 2) + g2, :], T.PT[:, c // 2, :, g2, :], False, final and g2 == 1, ["PERM", "PT"],
+               [("pk", 64 * c, 64 * c + 64)])
+
+    def side(c):
+        lanes(T.ps[:, 64 * c:64 * c + 64], ("ps", 64 * c, 64 * c + 64), "SELN", "d", c, True, True)
+
+    def by_vector(c):
+        ts(T.rl[:, 1024 * c:1024 * c + 1024], T.d[:, 1024 * c:1024 * c + 1024], 0.0, ALU.max, [("d", c, c + 1)], [("rl", c, c + 1)])
+
+    def by_scalar(c):
+        act(T.rl[:, 1024 * c:1024 * c + 1024], T.d[:, 1024 * c:1024 * c + 1024], AF.Abs, [("d", c, c + 1)], [("rl", c, c + 1)])
+
+    def killed_names(t):
+        pw, kf = "PW%d" % t, "kf%d" % t
+        tt(T.t1[:], T[kf][:], T.pa[:, 1], ALU.mult, [kf, ("pa", 256, 512)], ["t1"])
+        ts(T.t2[:], T.t1[:], 5, ALU.arith_shift_right, ["t1"], ["t2"])
+        tt(T[pw][:, 256:512], T.t2[:], T.pa[:, 1], ALU.add, ["t2", ("pa", 256, 512)], [(pw, 256, 512)])
+
+    def load_s(b):
+        c, hj, db = b // 2, b % 2, "db%d" % (b % 4)
+        for jj in range(8):
+            mm(T[db][:, :, jj], T.ID[:], T.s[:, 1024 * c + 8 * hj + jj:1024 * c + 1024:16], jj == 0, False, ["ID", ("s", c, c + 1)], [db])
+
+    def second(b):
+        c, hj, db = b // 2, b % 2, "db%d" % (b % 4)
+        for jj in range(8):
+            mm(T[db][:, :, jj], T.IDN[:], T.xs[:, 64 * c:64 * c + 64], False, jj == 7, ["IDN", "xs"], [db])
+        act(T.ab[:, 64 * c:64 * c + 64, 8 * hj:8 * hj + 8], T[db][:], AF.Abs, [db], [("ab", b, b + 1)])
+
+    def esum(c):
+        if c < 2:
+            lanes(T.pk[:, 256 + 64 * c:320 + 64 * c], ("pk", 256 + 64 * c, 320 + 64 * c), "SEL", "ab", c, True, True)
+        else:
+            lanes(T.ps[:, 128 + 64 * c:192 + 64 * c], ("ps", 128 + 64 * c, 192 + 64 * c), "SEL", "ab", c, True, True)
+
+    def near(h):
+        src, r = (T.pk[:, 256:384], ("pk", 256, 384)) if h == 0 else (T.ps[:, 256:384], ("ps", 256, 384))
+        act(T.ns[:, 128 * h:128 * h + 128], src, AF.Sign, [r], [("ns", h, h + 1)], bias=-959.5)
+
+    def tail(t, h):
+        a, b = 128 * h, 128 * h + 128
+        scan(T.fs[:, a:b], T.RSE[:, a:b], T.ns[:, a:b], ALU.add, ALU.min, ["RSE", ("ns", h, h + 1)], [("fs", h, h + 1)])
+        tt(m("o1", 8, 8 * h), T.fs[:, a + 15:b:16], m("pr", 8, 8 * h), ALU.mult, [("fs", h, h + 1), "pr"], [("o1", 8 * h, 8 * h + 8)])
+        q2("o2", "o1", "CV", ALU.add, 8, 8 * h)
+        q1("offV", "o2", 4.0, ALU.mult, n=8, at=8 * h)
+        tt(T.kp[:, a:b], T.KS[:, KW * h:KW * h + KW].indirect(m("offV", 8, 8 * h)), T.a1[:, a:b], ALU.add,
+           [("KS", 4 * h, 4 * h + 4), ("offV", 8 * h, 8 * h + 8), "a1"], [("kp", a, b)])
+        if t == ROUNDS - 1:
+            dma("y", [(T.yk[:, a:b], T.kp[:, a:b], [], [("kp", a, b)])])
+        else:
+            cp(T.ku[:, a:b], T.kp[:, a:b], [("kp", a, b)], [("ku", a, b)])
+            send(T.ku[:, a:b], ("ku", a, b), T["kl%d" % (t + 1)][:, a:b], nxt, "u%d%d" % (h, t + 1), 0)
+            send(T.kp[:, a:b], ("kp", a, b), T["kf%d" % (t + 1)][:, a:b], nxt, "f%d%d" % (h, t + 1), 1)
+
+    def compare(rs):
+        for r in rs:
+            ts(T.NE[:, 64 * r:64 * r + 64], T.pb[:, r // 4, :], m("t32", 1, r), ALU.not_equal, [("pb", 0, 256), "t32"], [("NE", r, r + 1)])
+
+    def table_writes(t):
+        ts(T.nr[:], T.ak[:], 32.5, ALU.is_lt, ["ak"], ["nr"], 128.0, ALU.mult)
+        tt(T.e2[:], T.nr[:], T.pa[:, 1], ALU.mult, ["nr", ("pa", 256, 512)], ["e2"])
+        for c in (3, 2, 1, 0):
+            tt(T.X[:].indirect(m("offX", 4, 4 * c)), T.yv[:, 64 * c:64 * c + 64], T.e2[:, 64 * c:64 * c + 64], ALU.add, ["yv", "e2", "offX"], ["X"])
+
+    def column_parts():
+        act(T.yv[:], T.X[:, 0:4096].indirect(m("offY")), AF.Copy, [XT, "offY"], ["yv"])
+        act(T.ak[:], T.d[:].indirect(m("offK")), AF.Abs, ["d", "offK"], ["ak"])
+        act(T.pa[:, 1], T.yv[:], AF.Sign, ["yv"], [("pa", 256, 512)], scale=-1.0, bias=127.5)
+
+    def allowance(t):
+        mm(T.pb[:, 4, 0:16], T.BLK[:], m("kl"), True, True, ["BLK", "kl"], [("pb", 256, 272)])
+        act(T.kj[:], T.pb[:, 4, 0:16], AF.Copy, [("pb", 256, 272)], ["kj", ("kc", t, t + 1)], accum_out=T.kc[:, t:t + 1])
+        ts(T.Ai[:, 0:1], T.kc[:, t:t + 1], T.kc[:, 0:1] if t else 0.0, ALU.add, ["kc"], [("Ai", 0, 1)], 1.0 / 256, ALU.mult)
+        ts(T.Ai[:, 1:2], T.Ai[:, 0:1], 15, ALU.bitwise_and, [("Ai", 0, 1)], [("Ai", 1, 2)])
+        ts(T.thr[:, 0:1], T.Ai[:, 1:2], 4.0, ALU.mult, [("Ai", 1, 2)], ["thr"], 48.0, ALU.add)
+
+    phage_forms(0)
+    shifted(0, 0)
+    shifted(0, 1)
+    constants1()
     for t in range(ROUNDS):
         last = t == ROUNDS - 1
-        kl, pl = "kl%d" % t, "pl%d" % t
-        KL, PL = T[kl], T[pl]
+        pw = "PW%d" % t
+        sgather(t, 0)
+        mm(T.pk[:, 0:256], T.ID[:], T.CD[:], True, False, ["ID", "CD"], [("pk", 0, 256)])
+        mm(T.pk[:, 0:256], T.ID[:], T.JR[:], False, False, ["ID", "JR"], [("pk", 0, 256)])
         if t:
-            ne = len(topo.engines(core, nxt)[:8])
-            landed(kl, "rk%d" % t, ne)
-            landed(pl, "rp%d" % t, ne)
+            shifted(t, 0)
+        shifted_in(t, 0)
+        sgather(t, 1)
+        dgather(0)
+        sgather(t, 2)
+        by_vector(0)
+        side(0)
+        key(0, "SELN", "d")
+        key(0, "SEL2", "rl")
+        if t:
+            shifted(t, 1)
+        shifted_in(t, 1)
+        dgather(1)
+        sgather(t, 3)
+        side(1)
+        mm(T.pa[:, 1], T.IDF[:], T.Pf[:], True, True, ["IDF", "Pf"], [("pa", 256, 512)])
+        dgather(2)
+        by_scalar(1)
+        side(2)
+        key(1, "SEL", "rl")
         if t == 0:
-            fill("us", 0.0)
             constants2()
-        cp(T.y0[:], T.X[:, 0:4096].indirect(PL[:, 0:64]), [("X", 0, 4096), pl], ["y0"])
-        for c in (1, 2, 3):
-            act(T["y%d" % c][:], T.X[:, 0:4096].indirect(PL[:, 64 * c:64 * c + 64]), AF.Copy, [("X", 0, 4096), pl], ["y%d" % c])
-        cp(T.Pf[:], PL[:], [pl], ["Pf"])
-        ts(T.P4[:], PL[:], 4096.0, ALU.add, [pl], ["P4"])
-        cp(T.KS[:, KB:KB + 256], KL[:], [kl], [("KS", KB, KB + 256)])
-        mm(T.pn[:, 0:4], T.S15[:], T.KS[:, KB:KB + 256], True, True, ["S15", ("KS", KB, KB + 256)], [("pn", 0, 256)])
-        act(T["s3"][:], T.X[:, 0:4096].indirect(KL[:, 192:256]), AF.Copy, [("X", 0, 4096), kl], ["s3"])
-        act(T.k15[:], T.pn[:, 0:4], AF.Copy, [("pn", 0, 256)], ["k15"])
-        dma("y", [(T.kd[:, 1:17, :], T.KS[:, KB:KB + 256], [("kd", 1, 17)], [("KS", KB, KB + 256)]),
-                  (T.kd[:, 17:33, :], T.k15[:], [("kd", 17, 33)], ["k15"])])
-        dma("y", [(T.KS[j::16, 0:4096], T.kd[:, j + 1:j + 17, :], [("KS", 0, 4096)], [("kd", j + 1, j + 17)]) for j in range(1, 16)]
-            + [(T.KS[:, 4096:KB], T.kd[:, 0:16, :], [("KS", 4096, KB)], [("kd", 0, 16)])])
-        mm(T.pk[:, 0:256], T.ID[:], T.JR[:], True, False, ["ID", "JR"], [("pk", 0, 256)])
-
-        def fused(c):
-            tt(T["d%d" % c][:], T.X[:, 0:4096].indirect(KL[:, 64 * c:64 * c + 64]), T["y%d" % c][:], ALU.subtract, [("X", 0, 4096), kl, "y%d" % c], ["d%d" % c])
-
-        def relu(c):
-            ts(T["rl%d" % c][:], T["d%d" % c][:], 0.0, ALU.max, ["d%d" % c], ["rl%d" % c])
-
-        def pass_(bank, lo, sel, src, first, final, rev=False):
-            for q in range(16):
-                mm(T[bank][:, lo:lo + 64], T[sel][:, q, :], T[src][:, 64 * q:64 * q + 64], first and q == 0, final and q == 15,
-                   [sel, src], [(bank, lo, lo + 64)])
-
-        def dpass(c):
-            pass_("ps", 64 * c, "SELN", "d%d" % c, True, True)
-
-        def rpass(c):
-            pass_("pk", 64 * c, "SEL", "rl%d" % c, False, False)
-
-        def sgather(c):
-            act(T["s%d" % c][:], T.X[:, 0:4096].indirect(KL[:, 64 * c:64 * c + 64]), AF.Copy, [("X", 0, 4096), kl], ["s%d" % c])
-
-        for h, bank in ((0, "pone"), (1, "pg")):
-            mm(T[bank][:], T.ID[:], T.s3[:, 512 * h:512 * h + 512], True, False, ["ID", "s3"], [bank])
-            mm(T[bank][:], T.IDN[:], T.y3[:, 512 * h:512 * h + 512], False, True, ["IDN", "y3"], [bank])
-            act(T.rl3[:, 512 * h:512 * h + 512], T[bank][:], AF.Abs, [bank], [("rl3", 512 * h, 512 * h + 512)], scale=0.5)
-        sgather(0)
-        fused(0)
-        relu(0)
-        fused(1)
-        dpass(0)
-        rpass(0)
-        pass_("ps", 192, "SELN", "s3", True, False)
-        pass_("ps", 192, "SELP", "y3", False, True)
-        rpass(3)
-        relu(1)
-        fused(2)
-        dpass(1)
-        rpass(1)
-        relu(2)
-        dpass(2)
-        rpass(2)
-        tt(T.t1[:], T.KS[:, KB:KB + 256], T.Pf[:], ALU.mult, [("KS", KB, KB + 256), "Pf"], ["t1"])
-        ts(T.t2[:], T.t1[:], 5, ALU.arith_shift_right, ["t1"], ["t2"])
-        sgather(1)
-        act(T.sg[:], T.ps[:, 0:256], AF.Sign, [("ps", 0, 256)], ["sg"], scale=-1.0, bias=-0.25)
-        act(T.us[:, 0:192], T.ps[:, 0:192], AF.Copy, [("ps", 0, 192)], [("us", 0, 192)])
-        mm(T.pk[:, 0:256], T.IDW[:], T.sg[:], False, True, ["IDW", "sg"], [("pk", 0, 256)])
-        sgather(2)
+        names(0)
+        names(1)
+        dgather(3)
+        by_scalar(2)
+        side(3)
+        act(T.sg[:], T.ps[:, 0:256], AF.Sign, [("ps", 0, 256)], ["sg"], bias=-0.5)
+        by_vector(3)
+        key(3, "SELN", "d")
+        key(2, "SEL", "rl")
+        key(3, "SEL2", "rl")
+        mm(T.pk[:, 0:256], T.ID64[:], T.sg[:], False, False, ["ID64", "sg"], [("pk", 0, 256)])
+        names(2)
+        names(3, True)
         if t == 0:
-            act(T.SELW[:], T.SEL[:], AF.Copy, ["SEL", ("col", 6, 7)], ["SELW"], scale=T.col[:, 6:7])
-        mm(T.pe[:], T.ID[:], T.Z0[:], True, False, ["ID", "Z0"], ["pe"])
-        for c in (3, 0, 1, 2):
-            pass_("pe", 64 * c, "SELN", "s%d" % c, False, False)
-        tt(T.key[:], T.pk[:, 0:256], T.us[:], ALU.add, [("pk", 0, 256), "us"], ["key"])
-        scan(T.R[:], T.RST[:], T.key[:], ALU.max, ALU.min, ["RST", "key"], ["R"])
+            constants3()
+        killed_names(t)
+        for b in range(4):
+            load_s(b)
+        scan(T.R[:], T.RST[:], T.pk[:, 0:256], ALU.max, ALU.min, ["RST", ("pk", 0, 256)], ["R"])
         r = T.R[:, 15::16]
-        ts(m("ki"), r, 64.0, ALU.mult, ["R"], ["ki"])
-        ts(m("nk"), r, 440.0, ALU.is_ge, ["R"], ["nk"])
-        ts(m("plt"), r, T.thr[:, 0:1], ALU.is_lt, ["R", "thr"], ["plt"])
-        q1("ub", "ki", 1, ALU.bitwise_and)
-        q1("zm", "ki", 5, ALU.arith_shift_right, 3, ALU.bitwise_and)
-        q1("kk", "ki", 1, ALU.arith_shift_right, 15, ALU.bitwise_and)
-        q1("w", "ub", 2.0, ALU.mult, -1.0, ALU.add)
-        q2("pr", "plt", "nk", ALU.mult)
-        q2("h2", "zm", "w", ALU.mult)
-        q2("h1", "kk", "w", ALU.add)
-        q2("h3", "h1", "h2", ALU.add)
+        ts(m("ki"), r, 2.0 ** 17, ALU.mult, ["R"], ["ki"])
+        ts(m("kl"), r, -112.0, ALU.is_lt, ["R"], ["kl"], 256.0, ALU.mult)
+        q1("u2", "ki", 11, ALU.arith_shift_right, 2, ALU.bitwise_and)
+        q1("zm", "ki", 17, ALU.arith_shift_right, 3, ALU.bitwise_and)
+        q1("kk", "ki", 13, ALU.arith_shift_right, 15, ALU.bitwise_and)
+        q2("w", "u2", "CW", ALU.add, 32)
+        q1("nm", "ki", 4095, ALU.bitwise_and)
+        q2("h2", "w", "z1", ALU.mult)
+        ts(m("plt"), r, T.thr[:, 0:1], ALU.is_lt, ["R", "thr"], ["plt"], 256.0, ALU.mult)
+        q2("h3", "h2", "kk", ALU.add)
+        q1("t16", "nm", -2048.0, ALU.add, 1.0 / 16, ALU.mult)
         q1("fi", "h3", 15, ALU.bitwise_and)
-        q2("fo", "fi", "C16", ALU.add)
-        cp(T.offF[:], m("fo"), ["fo"], ["offF"])
-        for c in range(4):
-            cp(T.xn[:, c, :], T["y%d" % c][:].indirect(T.offF[:, 4 * c:4 * c + 4]), ["y%d" % c, "offF"], [("xn", 64 * c, 64 * c + 64)])
-        for rl in range(4):
-            mm(T.px[:, :, :, rl], T.ID[:], T.xn[:, :, 16 * rl:16 * rl + 16], True, True, ["ID", "xn"], ["px"])
-        q1("k1", "kk", 1.0, ALU.add)
-        q1("f1", "fi", 1.0, ALU.add)
-        q2("ko", "kk", "C16", ALU.add)
-        q2("k1b", "k1", "pr", ALU.mult)
-        q2("f1b", "f1", "pr", ALU.mult)
-        cp(T.offK[:], m("ko"), ["ko"], ["offK"])
-        ts(T.kill[:], r, 440.0, ALU.is_lt, ["R"], ["kill"])
-
-        def spread(b, src):
+        q2("pr", "plt", "kl", ALU.subtract)
+        q2("ko", "kk", "C16", ALU.add, 32)
+        q1("t32", "nm", 2048.0, ALU.add, 1.0 / 16, ALU.mult)
+        qc("offK", "ko", 32)
+        step = (1, 4, 16)[t]
+        for i, src in enumerate(("t16", "pr")):
             for q in range(16):
-                mm(T.pb[:, b:b + 4, q, :], T.SELT[:, q, :], T[src][:], True, True, ["SELT", src], [("pb", 64 * b, 64 * b + 256)])
-
-        spread(0, "k1b")
-        spread(4, "f1b")
-
-        def second(c):
-            for j in range(16):
-                tt(T["mx%d" % c][:, j::16], T["s%d" % c][:, j::16], T.px[:, c], ALU.max, ["s%d" % c, "px"], [("mx%d" % c, 64 * j, 64 * j + 64)])
-            pass_("pe", 64 * c, "SEL", "mx%d" % c, False, c == 3)
-
-        second(0)
-        ts(T.pone[:], T.pb[:], T.col[:, 3:4], ALU.is_equal, ["pb", ("col", 3, 4)], ["pone"])
-        tt(T.HPk[:], T.pone[:, 0:256], T.P4[:], ALU.mult, [("pone", 0, 256), "P4"], ["HPk"])
-        tt(T.HPf[:], T.pone[:, 256:512], T.P4[:], ALU.mult, [("pone", 256, 512), "P4"], ["HPf"])
-        for rl in range(4):
-            mm(T.pn[:, 0:4, rl, :], T.BLKF[:], T.HPk[:, :, :, rl], True, True, ["BLKF", "HPk"], [("pn", 0, 256)])
-        for q in range(16):
-            mm(T.ps[:, 256:272], T.SELN[:, q, :], T.xn[:, :, q::16], q == 0, q == 15, ["SELN", "xn"], [("ps", 256, 272)])
-        spread(0, "kill")
-        for c in range(4):
-            src = "d%d" % c if c < 3 else "rl3"
-            act(T.ak[:, 64 * c:64 * c + 64], T[src][:].indirect(T.offK[:, 4 * c:4 * c + 4]), AF.Abs, [src, "offK"], [("ak", 64 * c, 64 * c + 64)],
-                scale=1.0 if c < 3 else 2.0)
-        for c in range(4):
-            act(T.yk_[:, 64 * c:64 * c + 64], T["y%d" % c][:].indirect(T.offK[:, 4 * c:4 * c + 4]), AF.Copy, ["y%d" % c, "offK"], [("yk_", 64 * c, 64 * c + 64)])
-        act(T.sw[:], T.ak[:], AF.Sign, ["ak"], ["sw"], scale=-1.0, bias=32.5)
-        act(T.sy[:], T.yk_[:], AF.Sign, ["yk_"], ["sy"], scale=-1.0, bias=127.5)
-        second(1)
-        ts(T.b1[:], T.pn[:, 0:4], T.col[:, 5:6], ALU.mult, [("pn", 0, 256), ("col", 5, 6)], ["b1"])
-        ts(T.b2[:], T.b1[:], 4096, ALU.bitwise_and, ["b1"], ["b2"])
-        ts(T.FB[:], T.b2[:], 1.0 / 2048, ALU.mult, ["b2"], ["FB"], -1.0, ALU.add)
-        for i in range(8):
-            ts(T.BD[:, :, i, :], T.FB[:], T.GM[:, i:i + 1], ALU.mult, ["FB", "GM"], [("BD", 256 * i, 256 * i + 256)])
-        for rl in range(4):
-            mm(T.pn[:, 4:8, rl, :], T.BLK0[:], T.HPf[:, :, :, rl], True, True, ["BLK0", "HPf"], [("pn", 256, 512)])
-        act(T.a1[:], T.pn[:, 4:8], AF.Copy, [("pn", 256, 512)], ["a1"])
-        for q in range(16):
-            mm(T.ps[:, 272:288], T.SELW[:, q, :], T.FB[:, q::16], q == 0, q == 15, ["SELW", "FB"], [("ps", 272, 288)])
-        mm(T.ps[:, 288:304], T.BLK[:], T.kill[:], True, True, ["BLK", "kill"], [("ps", 288, 304)])
-        tt(T.pb[:, 4:8], T.t2[:], T.pb[:, 0:4], ALU.mult, ["t2", ("pb", 0, 256)], [("pb", 256, 512)])
-        tt(T.pw[:], T.pb[:, 4:8], T.Pf[:], ALU.add, [("pb", 256, 512), "Pf"], ["pw"])
-        ts(T.px_[:], T.pw[:], 4095, ALU.bitwise_and, ["pw"], ["px_"])
+                a = (4 * q, 16 * (q % 4) + q // 4, q)[t]
+                mm(T.pb[:, 0:4, a:a + 3 * step + 1:step], T.SELT[:, q, :], m(src), i + q == 0, i + q == 16, ["SELT", src], [("pb", 0, 256)])
+        act(T.sn[:], T.s[:].indirect(m("offF")), AF.Copy, ["s", "offF"], ["sn"])
+        q2("oP", "kl", "CB", ALU.add, 32)
+        cp(T.df[:], T.d[:].indirect(m("offF")), ["d", "offF"], ["df"])
+        for i, src in enumerate(("sn", "df")):
+            mm(T.pa[:, 0], T.ID[:], T[src][:], i == 0, i == 1, ["ID", src], [("pa", 0, 256)])
+        q2("fa", "fi", "pr", ALU.mult)
+        qc("offY", "nm")
+        q2("oN", "oN", "fa", ALU.add)
+        q2("w1", "nm", "DM", ALU.subtract)
+        qc("offP", "oP", 32)
+        q2("w1p", "w1", "pr", ALU.mult)
         if last:
-            cp(T.pout[:], T.px_[:], ["px_"], ["pout"])
+            column_parts()
+        for rl in range(4):
+            act(T.xs[:, rl::4], T.pa[:, 0, :, rl, :], AF.Copy, [("pa", 0, 256)], [("xs", rl, rl + 1)])
+        ts(T.po[:], T[pw][:].indirect(m("offP")), 4095, ALU.bitwise_and, [pw, "offP"], ["po"])
+        if not last:
+            send(T.po[:], "po", T["PW%d" % (t + 1)][:, 0:256], prv, "p%d" % (t + 1), 0)
+        if t == 0:
+            constants4()
+        second(0)
+        second(1)
+        compare(range(16))
+        load_s(4)
+        second(2)
+        esum(0)
+        load_s(5)
+        second(3)
+        act(T.a1[:], T.PS[:].indirect(m("offN")), AF.Copy, ["PS", "offN"], ["a1"])
+        scan(T.FE[:], T.RSD[:], T.NE[:], ALU.add, ALU.min, ["RSD", "NE"], ["FE"])
+        esum(1)
+        near(0)
+        tt(m("eq"), T.FE[:, 63::64], T.CP[:, 16 * t:16 * t + 16], ALU.is_equal, ["FE", "CP"], ["eq"])
+        q2("w2", "eq", "w1p", ALU.mult)
+        q2("w3", "w2", "DM8", ALU.add)
+        q1("offX", "w3", 1.0 / 256, ALU.mult)
+        if last:
+            table_writes(t)
+            dma("y", [(T.yx[:], T.X[:, 0:4096], [], [XT])])
+            cp(T.pout[:], T.po[:], ["po"], ["pout"])
             dma("y", [(T.yp[:], T.pout[:], [], ["pout"])])
         else:
-            cp(T.pu[:], T.px_[:], ["px_"], ["pu"])
-            send("pu", "pl%d" % (t + 1), prv, "rp%d" % (t + 1), "lp%d" % (t + 1))
-        for bank, rrs in (("pg", (12, 13)), ("pk", (14, 15)), ("pone", (8, 9)), ("pb", (10, 11)), ("pg", (4, 5, 6, 7)), ("pk", (0, 1, 2, 3))):
-            lo = 0
-            todo = []
-            for rr in rrs:
-                rh, rl = rr // 4, rr % 4
-                n = 64 * (rh + 1)
-                G = T[bank][:, lo // 64:(lo + n) // 64] if bank == "pb" else T[bank][:, lo:lo + n]
-                mm(G, T.BD[:, rr, :, :], T.FB[:, 0:n], True, False, ["BD", "FB"], [(bank, lo, lo + n)])
-                G2 = T[bank][:, (lo + n) // 64 - 1:(lo + n) // 64] if bank == "pb" else T[bank][:, lo + n - 64:lo + n]
-                mm(G2, T.ID[:], T.TRB[:, rl, :], False, True, ["ID", "TRB"], [(bank, lo, lo + n)])
-                todo.append((rr, n, lo, G))
-                lo += n
-            for rr, n, lo, G in todo:
-                act(T.junk[:, 256 * rr:256 * rr + n], G, AF.Relu, [(bank, lo, lo + n)], [("cnt", rr, rr + 1), ("junk", 256 * rr, 256 * rr + n)], bias=-15.0,
-                    accum_out=T.sf[:, CN + rr:CN + rr + 1])
-        ts(T.xz[:, 0::16], T.ps[:, 256:272], -1.0, ALU.mult, [("ps", 256, 272)], ["xz"], 480.0, ALU.add)
-        q1("pr4", "pr", 4096.0, ALU.mult)
-        q1("bs", "pr", -512.0, ALU.mult, 4352.0, ALU.add)
-        scan(T.xb[:], T.BC0[:], T.xz[:], ALU.mult, ALU.add, ["BC0", "xz"], ["xb"])
-        q2("bs2", "bs", "CB", ALU.add)
-        second(2)
+            column_parts()
+        tail(t, 0)
+        load_s(6)
+        second(4)
+        load_s(7)
+        second(5)
         if not last:
-            second(3)
-        ts(T.pn[:, 0:4], T.sw[:], 1.0, ALU.add, ["sw"], [("pn", 0, 256)], 64.0, ALU.mult)
-        tt(m("w1"), T.ps[:, 272:288], T.DMH[:], ALU.subtract, [("ps", 272, 288), "DMH"], ["w1"])
-        tt(T.e2[:], T.pn[:, 0:4], T.sy[:], ALU.mult, [("pn", 0, 256), "sy"], ["e2"])
-        q1("nd", "cnt", 0.5, ALU.is_lt)
-        q2("win", "nd", "pr", ALU.mult)
-        q2("w2", "w1", "win", ALU.mult)
-        q2("w3", "w2", "DM", ALU.add)
-        cp(T.offX[:], m("w3"), ["w3"], ["offX"])
-        tt(T.X[:].indirect(T.offX[:]), T.yk_[:], T.e2[:], ALU.add, ["yk_", "e2", "offX"], ["X"])
-        if last:
-            dma("y", [(T.yx[:], T.X[:, 0:4096], [], [("X", 0, 4096)])])
-            second(3)
-        tt(T.nn[:], T.pe[:], T.xb[:], ALU.is_ge, ["pe", "xb"], ["nn"])
-        scan(T.fs[:], T.RSE[:], T.nn[:], ALU.add, ALU.min, ["RSE", "nn"], ["fs"])
-        tt(m("o1"), T.fs[:, 15::16], m("pr4"), ALU.mult, ["fs", "pr4"], ["o1"])
-        q2("o2", "o1", "bs2", ALU.add)
-        cp(T.offV[:], m("o2"), ["o2"], ["offV"])
-        for c in range(4):
-            tt(T.kp[:, c, :], T.KS[:].indirect(T.offV[:, 4 * c:4 * c + 4]), T.a1[:, 64 * c:64 * c + 64], ALU.add, ["KS", "offV", "a1"], [("kp", 64 * c, 64 * c + 64)])
-        dst = "kout" if last else "ku"
-        for rl in range(4):
-            cp(T[dst][:, :, :, rl], T.kp[:, :, 16 * rl:16 * rl + 16], ["kp"], [(dst, 64 * rl, 64 * rl + 64)])
-        if last:
-            dma("y", [(T.yk[:], T.kout[:], [], ["kout"])])
-        else:
-            send("ku", "kl%d" % (t + 1), nxt, "rk%d" % (t + 1), "lk%d" % (t + 1))
+            table_writes(t)
+        second(6)
+        esum(2)
+        second(7)
+        esum(3)
+        near(1)
         if not last:
-            op("v", lambda: g.vector.tensor_reduce(T.A1[:, 0:1], T.ps[:, 288:304], AxisListType.X, ALU.add), [("ps", 288, 304)], ["A1"])
-            tt(T.A[:, 0:1], T.A[:, 0:1], T.A1[:, 0:1], ALU.add, ["A", "A1"], ["A"])
-            cp(T.Ai[:, 0:1], T.A[:, 0:1], ["A"], [("Ai", 0, 1)])
-            ts(T.Ai[:, 1:2], T.Ai[:, 0:1], 15, ALU.bitwise_and, [("Ai", 0, 1)], [("Ai", 1, 2)])
-            ts(T.thr[:, 0:1], T.Ai[:, 1:2], 2.0, ALU.mult, [("Ai", 1, 2)], ["thr"], 520.0, ALU.add)
+            phage_forms(t + 1)
+        tail(t, 1)
+        if not last:
+            allowance(t)
     for sem in sorted(total):
         if waited.get(("g", sem), 0) < total[sem]:
             g.wait_ge(T.sem[sem], total[sem])

@@ -1,15 +1,16 @@
 from concourse.mybir import AluOpType as ALU, ActivationFunctionType as AF
 
-BIG = 1.0e6
+BIG = 2.0 ** 30
+U = 2.0 ** 17
+KW = 18 * 128
 _B = "bfloat16"
 _F = "float32"
 _H = "float16"
 _I = "int32"
 _U = "uint16"
-KW = 24 * 128
 SCRATCH = {
-    "X": ("sbuf", [128, 4352], _B),
-    "s": ("sbuf", [128, 4096], _B), "d": ("sbuf", [128, 4096], _B), "rl": ("sbuf", [128, 4096], _B),
+    "X": ("sbuf", [128, 4160], _B),
+    "s": ("sbuf", [128, 4112], _B), "d": ("sbuf", [128, 4112], _B), "rl": ("sbuf", [128, 4096], _B),
     "ab": ("sbuf", [128, 256, 16], _B),
     "KS": ("sbuf", [128, 2 * KW], _F), "PS": ("sbuf", [128, 4352], _F),
     "kd": ("dram", [2, 8, 33, 128], _F),
@@ -25,14 +26,14 @@ SCRATCH = {
     "ID": ("sbuf", [128, 128], _B), "IDN": ("sbuf", [128, 128], _B), "ID64": ("sbuf", [128, 128], _B),
     "IDF": ("sbuf", [128, 128], _F), "S15": ("sbuf", [128, 128], _F),
     "JR": ("sbuf", [128, 256], _B), "CD": ("sbuf", [128, 256], _B),
-    "RST": ("sbuf", [128, 256], _F), "RSE": ("sbuf", [128, 256], _B), "RSD": ("sbuf", [128, 1024], _B),
+    "RST": ("sbuf", [128, 256], _F), "RC": ("sbuf", [128, 256], _F), "RSD": ("sbuf", [128, 1024], _B),
     "C16": ("sbuf", [128, 32], _F), "CB": ("sbuf", [128, 32], _F), "CV": ("sbuf", [128, 16], _F), "DM": ("sbuf", [128, 16], _F),
-    "DM8": ("sbuf", [128, 16], _F), "CW": ("sbuf", [128, 32], _F), "CP": ("sbuf", [128, 48], _F),
-    "R": ("sbuf", [128, 256], _F), "sg": ("sbuf", [128, 256], _B),
+    "CW": ("sbuf", [128, 32], _F), "CP": ("sbuf", [128, 48], _F),
+    "R": ("sbuf", [128, 256], _I), "sg": ("sbuf", [128, 256], _B),
     "sf": ("sbuf", [128, 320], _F), "si": ("sbuf", [128, 128], _I), "sh": ("sbuf", [128, 48], _H), "su": ("sbuf", [128, 128], _U),
     "kc": ("sbuf", [128, 4], _F), "kj": ("sbuf", [128, 16], _F), "Ai": ("sbuf", [128, 4], _I), "thr": ("sbuf", [128, 4], _F),
     "df": ("sbuf", [128, 256], _B), "sn": ("sbuf", [128, 256], _B), "xs": ("sbuf", [128, 256], _B),
-    "ns": ("sbuf", [128, 256], _B), "fs": ("sbuf", [128, 256], _B),
+    "ns": ("sbuf", [128, 256], _B), "fs": ("sbuf", [128, 256], _F),
     "NE": ("sbuf", [128, 1024], _B), "FE": ("sbuf", [128, 1024], _B),
     "ak": ("sbuf", [128, 256], _B), "yv": ("sbuf", [128, 256], _B), "nr": ("sbuf", [128, 256], _B), "e2": ("sbuf", [128, 256], _B),
     "pk": ("psum", [128, 512], _F), "ps": ("psum", [128, 512], _F), "pa": ("psum", [128, 2, 4, 4, 16], _F), "pb": ("psum", [128, 8, 64], _F),
@@ -47,8 +48,8 @@ for _t in range(ROUNDS):
 PSUM = ("pk", "ps", "pa", "pb", "db0", "db1", "db2", "db3")
 SEMAPHORES = (["qv", "qs", "qt", "qg"] + ["dm%d" % i for i in range(40)]
               + [a + b + str(t) for a in "rl" for b in ("p", "u0", "u1", "f0", "f1") for t in (1, 2)])
-SMALL = {"sf": ("w", "z1", "ko", "fo", "oP", "oN", "h2", "plt", "fa", "t32", "w1", "w1p", "eq", "w2", "w3", "o1", "o2"),
-         "si": ("ki", "nm", "kk", "fi", "u2", "zm", "h3"),
+SMALL = {"sf": ("w", "z1", "ko", "fo", "oP", "oN", "h2", "plt", "fa", "t32", "w1", "w1p", "w2", "w3", "un", "u8"),
+         "si": ("nm", "kk", "fi", "u2", "zm", "h3"),
          "sh": ("kl", "pr", "t16"),
          "su": ("offK", "offF", "offP", "offN", "offY", "offX", "offV")}
 WHERE = {n: (b, 16 * i) for b in SMALL for i, n in enumerate(SMALL[b])}
@@ -151,12 +152,12 @@ def rank_program(g, core, T, topo):
         else:
             op("v", lambda: g.vector.tensor_scalar(out, a, s1, s2, o1, o2), reads, writes)
 
-    def q1(out, a, s1, o1, s2=None, o2=None, n=16, at=0):
-        ts(m(out, n, at), m(a, n, at), s1, o1, [(a, at, at + n)], [(out, at, at + n)], s2, o2)
+    def q1(out, a, s1, o1, s2=None, o2=None, n=16):
+        ts(m(out, n), m(a, n), s1, o1, [(a, 0, n)], [(out, 0, n)], s2, o2)
 
     def q2(out, a, b, o, n=16, at=0):
-        bb = m(b, n, at) if b in WHERE else T[b][:, at:at + n]
-        tt(m(out, n, at), m(a, n, at), bb, o, [(a, at, at + n), (b, at, at + n)], [(out, at, at + n)])
+        bb = m(b, n) if b in WHERE else T[b][:, at:at + n]
+        tt(m(out, n), m(a, n), bb, o, [(a, 0, n), (b, at, at + n)], [(out, 0, n)])
 
     def cp(out, a, reads, writes):
         op("v", lambda: g.vector.tensor_copy(out, a), reads, writes)
@@ -164,8 +165,8 @@ def rank_program(g, core, T, topo):
     def qc(out, a, n=16):
         cp(m(out, n), m(a, n), [(a, 0, n)], [(out, 0, n)])
 
-    def fill(name, c, ap=None):
-        op("v", lambda: g.vector.memset(T[name][:] if ap is None else ap, c), [] if ap is None else [name], [name])
+    def fill(name, c, ap=None, w=None):
+        op("v", lambda: g.vector.memset(T[name][:] if ap is None else ap, c), [], [w or name])
 
     def act(out, a, f, reads, writes, **kw):
         op("s", lambda: g.scalar.activation(out, a, f, **kw), reads, writes)
@@ -173,8 +174,8 @@ def rank_program(g, core, T, topo):
     def mm(out, l, r, st, sp, reads, writes):
         op("t", lambda: g.tensor.matmul(out, l, r, st, sp), reads, writes)
 
-    def scan(out, a, b, o1, o2, reads, writes):
-        op("v", lambda: g.vector.tensor_tensor_scan(out, a, b, 0.0, o1, o2), reads, writes)
+    def scan(out, a, b, first, o1, o2, reads, writes):
+        op("v", lambda: g.vector.tensor_tensor_scan(out, a, b, first, o1, o2), reads, writes)
 
     def iota(name, pat, base, mult=0, ap=None, w=None):
         op("g", lambda: g.iota(T[name][:] if ap is None else ap, pat, base, mult, allow_small_or_imprecise_dtypes=True), [], [w or name])
@@ -182,26 +183,25 @@ def rank_program(g, core, T, topo):
     def col(i):
         return T.col[:, i:i + 1]
 
-    XT = ("X", 0, 4096)
+    XT = ("X", 64, 4160)
+    XW = T.X[:, 64:4160]
     dma("y", [(T.kin[:], T.ka[:], ["kin"], [])])
     dma("y", [(T.PW0[:, 0:256], T.ph[:], [("PW0", 0, 256)], [])])
-    dma("y", [(T.X[:, 0:4096], T.x0[:], [XT], [])])
+    dma("y", [(XW, T.x0[:], [XT], [])])
     iota("pid", [[0, 1]], 0, 1, T.pid[:, 0:1])
     iota("rowi", [[1, 128]], 0)
     iota("rowg", [[1, 8], [0, 16]], 0)
     iota("isel", [[-1, 16], [32, 8], [1, 16]], 0)
-    iota("JR", [[0, 16], [4, 16]], 2)
-    iota("C16", [[0, 2], [1024, 4], [16, 4]], 0)
+    iota("JR", [[0, 16], [8192, 16]], 4096)
+    iota("C16", [[1024, 4], [16, 4]], 0, 0, T.C16[:, 0:16], ("C16", 0, 16))
     iota("CB", [[0, 2], [64, 4], [1, 4]], 0)
-    iota("CV", [[0, 2], [64, 2], [1, 4]], 23 * 128)
-    iota("DM", [[16, 16]], 4096)
+    iota("CV", [[0, 2], [64, 2], [1, 4]], 4096 + 23 * 128)
+    iota("DM", [[0, 4], [4096, 4]], 0)
     iota("CW", [[2, 2], [0, 16]], -1)
     for i in range(3):
         iota("CP", [[0, 4], [4 ** i, 4]], -63, 0, T.CP[:, 16 * i:16 * i + 16], ("CP", 16 * i, 16 * i + 16))
     iota("iselt", [[1, 16], [32, 8], [0, 16]], 0)
-    for h in range(2):
-        iota("KS", [[0, 768]], 0, 0, T.KS[:, KW * h + 2176:KW * h + 2944], ("KS", 4 * h + 1, 4 * h + 2))
-    fill("RSD", -1.0 / 128)
+    fill("RSD", -2.0 ** 21)
     fill("RSD", BIG, T.RSD[:, 0::64])
     for a in range(0, 4352, 1024):
         n = min(1024, 4352 - a)
@@ -213,47 +213,47 @@ def rank_program(g, core, T, topo):
         ts(pid(i), pid(0), sh, ALU.arith_shift_right, [("pid", 0, 1)], [("pid", i, i + 1)], mk, ALU.bitwise_and)
     cp(T.col[:, 0:6], T.pid[:, 0:6], [("pid", 0, 6)], [("col", 0, 6)])
     for i, a, s1, s2 in ((6, 2, 32.0, 0.0), (7, 2, 32.0, col(1)), (8, 1, 64.0, 0.0), (9, 1, 4.0, 0.0), (10, 0, 1.0, -16.0), (11, 0, 1.0, 16.0),
-                         (12, 5, -2.0 ** -14, 2.0 ** -14), (13, 5, 2.0 ** -14, 0.0), (14, 3, 16.0, col(4))):
+                         (12, 5, -1.0, 1.0), (13, 5, 1.0, 0.0), (14, 3, 16.0, col(4)), (16, 1, 4.0, -4096.0), (17, 1, 256.0, 0.0)):
         ts(col(i), col(a), s1, ALU.mult, [("col", 0, 6)], [("col", i, i + 1)], s2, ALU.add)
     ts(col(15), col(1), 15.0, ALU.is_equal, [("col", 0, 6)], [("col", 15, 16)])
     ts(T.ID[:], T.rowi[:], col(0), ALU.is_equal, ["rowi", "col"], ["ID"])
     ts(T.IDF[:], T.rowi[:], col(0), ALU.is_equal, ["rowi", "col"], ["IDF"])
     ts(T.S15[:], T.rowg[:], col(2), ALU.is_equal, ["rowg", "col"], ["S15"], col(15), ALU.mult)
-    fill("CD", -992.0)
-    fill("thr", 48.0)
+    fill("CD", -992.0 * U)
+    fill("thr", 48.0 * U)
     cp(T.kl0[:], T.kin[:], ["kin"], ["kl0"])
     cp(T.kf0[:], T.kin[:], ["kin"], ["kf0"])
 
     def constants1():
-        ts(T.ID64[:], T.ID[:], 1.0 / 64, ALU.mult, ["ID"], ["ID64"])
+        ts(T.ID64[:], T.ID[:], U / 64, ALU.mult, ["ID"], ["ID64"])
         ts(T.IDN[:], T.ID[:], -1.0, ALU.mult, ["ID"], ["IDN"])
-        for name, w in (("SELN", -1.0), ("SEL2", 2.0), ("SEL", 1.0)):
-            ts(T[name][:], T.isel[:], col(6), ALU.is_equal, ["isel", "col"], [name], w, ALU.mult)
-        ts(T.JR[:], T.JR[:], 1.0 / 64, ALU.mult, ["JR"], ["JR"])
-
-    def constants2():
         for h in range(2):
             for g2 in range(2):
                 ts(T.PERM[:, 2 * h + g2, :], T.rowi[:], col((10, 0, 11)[g2 - h + 1]), ALU.is_equal, ["rowi", "col"], [("PERM", 2 * h + g2, 2 * h + g2 + 1)],
                    col(12 + h), ALU.mult)
         fill("RST", -BIG)
         fill("RST", BIG, T.RST[:, 0::16])
+        fill("RC", -1.0 / 8)
+        fill("s", 1024.0, T.s[:, 4096:4112], ("s", 8, 9))
+        fill("d", 0.0, T.d[:, 4096:4112], ("d", 8, 9))
+        fill("X", 0.0, T.X[:, 0:64], ("X", 0, 64))
+        ts(T.BLK[:], T.rowg[:], col(2), ALU.is_equal, ["rowg", "col"], ["BLK"])
+        for name, w in (("SELN", -U), ("SEL2", 2 * U)):
+            ts(T[name][:], T.isel[:], col(6), ALU.is_equal, ["isel", "col"], [name], w, ALU.mult)
+
+    def constants2():
+        ts(T.SEL[:], T.isel[:], col(6), ALU.is_equal, ["isel", "col"], ["SEL"], U, ALU.mult)
 
     def constants3():
-        for name, c in (("C16", 8), ("CB", 9), ("DM", 1)):
+        ts(T.C16[:, 0:16], T.C16[:, 0:16], col(8), ALU.add, [("C16", 0, 16), "col"], [("C16", 0, 16)])
+        for name, c in (("CB", 9), ("DM", 17)):
             ts(T[name][:], T[name][:], col(c), ALU.add, [name, "col"], [name])
-        ts(T.SELT[:], T.iselt[:], col(7), ALU.is_equal, ["iselt", "col"], ["SELT"])
-
-    def constants4():
-        ts(T.CV[:], T.CV[:], col(9), ALU.add, ["CV", "col"], ["CV"], 0.25, ALU.mult)
-        ts(T.DM8[:], T.DM[:], 256.0, ALU.mult, ["DM"], ["DM8"])
+        ts(T.CV[:], T.CV[:], 1.0 / 1024, ALU.mult, ["CV"], ["CV"])
         for i, c in enumerate((9, 14, 1)):
             r = ("CP", 16 * i, 16 * i + 16)
-            ts(T.CP[:, r[1]:r[2]], T.CP[:, r[1]:r[2]], col(c), ALU.add, [r, "col"], [r], 1.0 / 128, ALU.mult)
-        ts(T.BLK[:], T.rowg[:], col(2), ALU.is_equal, ["rowg", "col"], ["BLK"])
-        fill("RSE", -1.0 / 8)
-        fill("RSE", BIG, T.RSE[:, 0::16])
-        op("v", lambda: g.vector.memset(T.X[:, 4096:4352], 0.0), [], [("X", 4096, 4352)])
+            ts(T.CP[:, r[1]:r[2]], T.CP[:, r[1]:r[2]], col(c), ALU.add, [r, "col"], [r], -8192.0, ALU.mult)
+        ts(T.SELT[:], T.iselt[:], col(7), ALU.is_equal, ["iselt", "col"], ["SELT"])
+        ts(T.CP[:], T.CP[:], 64.0, ALU.add, ["CP"], ["CP"])
 
     nxt = T.cores[(rank + 1) % n_ranks]
     prv = T.cores[(rank - 1) % n_ranks]
@@ -261,7 +261,7 @@ def rank_program(g, core, T, topo):
     def engines(dst, part):
         es = topo.engines(core, dst)
         n = len(es) // 2
-        return es[part * n:part * n + n]
+        return es if part is None else es[part * n:part * n + n]
 
     def landed(r, sem, n):
         total[sem] = n
@@ -280,19 +280,21 @@ def rank_program(g, core, T, topo):
     def phage_forms(t):
         pw = "PW%d" % t
         if t:
-            landed((pw, 0, 256), "rp%d" % t, len(engines(nxt, 0)))
+            landed((pw, 0, 256), "rp%d" % t, len(engines(nxt, None)))
         cp(T.pu[:], T[pw][:, 0:256], [(pw, 0, 256)], ["pu"])
         cp(T.Pf[:], T[pw][:, 0:256], [(pw, 0, 256)], ["Pf"])
         for rl in range(4):
-            ts(T.Pm[:, :, rl], T.pu[:, rl::4], -2048.0, ALU.add, ["pu"], [("Pm", rl, rl + 1)], 0.125, ALU.mult)
+            ts(T.Pm[:, :, rl], T.pu[:, rl::4], -2048.0, ALU.add, ["pu"], [("Pm", rl, rl + 1)])
         dma("y", [(T.PS[0::16, 256:4352], T.Pf[:], ["PS"], ["Pf"])])
+
+    def phage_turn():
         op("v", lambda: g.vector.transpose(T.PT[:], T.Pm[:]), ["Pm"], ["PT"])
 
     def shifted(t, h):
         kf = "kf%d" % t
         a, b = 128 * h, 128 * h + 128
         if t:
-            landed((kf, a, b), "rf%d%d" % (h, t), len(engines(prv, 1)))
+            landed((kf, a, b), "rf%d%d" % (h, t), len(engines(prv, None)))
         mm(T.pa[:, 0, 2 * h:2 * h + 2], T.S15[:], T[kf][:, a:b], True, True, ["S15", (kf, a, b)], [("pa", a, b)])
         act(T.k15[:, a:b], T.pa[:, 0, 2 * h:2 * h + 2], AF.Copy, [("pa", a, b)], [("k15", a, b)])
         o = 40 * h
@@ -306,241 +308,275 @@ def rank_program(g, core, T, topo):
         w = [("KS", 4 * h + 2, 4 * h + 3)]
         dma("y", [(T.KS[j::16, KW * h:KW * h + 2048], T.kd[h, :, j + 1:j + 17, :], w, [("kd", o, o + 33)]) for j in range(1, 16)]
             + [(T.KS[:, KW * h + 2048:KW * h + 2176], T.kd[h, :, 0:16, :], w, [("kd", o, o + 33)]),
-               (T.KS[:, KW * h + 2944:KW * h + 3072], T[kf][:, a:b], w, [(kf, a, b)])])
+               (T.KS[:, KW * h + 2176:KW * h + 2304], T[kf][:, a:b], w, [(kf, a, b)])])
 
-    def sgather(t, c):
+    def sgather(t, lo, hi):
         kl = "kl%d" % t
-        if t and c % 2 == 0:
-            landed((kl, 64 * c, 64 * c + 128), "ru%d%d" % (c // 2, t), len(engines(prv, 0)))
-        act(T.s[:, 1024 * c:1024 * c + 1024], T.X[:, 0:4096].indirect(T[kl][:, 64 * c:64 * c + 64]), AF.Copy,
-            [XT, (kl, 64 * c, 64 * c + 64)], [("s", c, c + 1)])
+        if t and lo % 4 == 0:
+            landed((kl, 32 * lo, 32 * lo + 128), "ru%d%d" % (lo // 4, t), len(engines(prv, None)))
+        act(T.s[:, 512 * lo:512 * hi], XW.indirect(T[kl][:, 32 * lo:32 * hi]), AF.Copy, [XT, (kl, 32 * lo, 32 * hi)], [("s", lo, hi)])
 
-    def dgather(c):
-        tt(T.d[:, 1024 * c:1024 * c + 1024], T.X[:, 0:4096].indirect(T.pu[:, 64 * c:64 * c + 64]), T.s[:, 1024 * c:1024 * c + 1024], ALU.subtract,
-           [XT, "pu", ("s", c, c + 1)], [("d", c, c + 1)])
+    def dgather(lo, hi):
+        tt(T.d[:, 512 * lo:512 * hi], XW.indirect(T.pu[:, 32 * lo:32 * hi]), T.s[:, 512 * lo:512 * hi], ALU.subtract,
+           [XT, "pu", ("s", lo, hi)], [("d", lo, hi)])
 
-    def lanes(out, w, sel, src, c, first, final):
-        for q in range(16):
-            a = 1024 * c + 64 * q
-            rhs = T.ab[:, a // 16:a // 16 + 4, :] if src == "ab" else T[src][:, a:a + 64]
-            r = ("ab", 2 * c, 2 * c + 2) if src == "ab" else (src, c, c + 1)
-            mm(out, T[sel][:, q, :], rhs, first and q == 0, final and q == 15, [sel, r], [w])
+    def by_vector(lo, hi):
+        ts(T.rl[:, 512 * lo:512 * hi], T.d[:, 512 * lo:512 * hi], 0.0, ALU.max, [("d", lo, hi)], [("rl", lo, hi)])
 
-    def key(c, sel, src):
-        lanes(T.pk[:, 64 * c:64 * c + 64], ("pk", 64 * c, 64 * c + 64), sel, src, c, False, False)
+    def by_scalar(lo, hi):
+        act(T.rl[:, 512 * lo:512 * hi], T.d[:, 512 * lo:512 * hi], AF.Abs, [("d", lo, hi)], [("rl", lo, hi)])
+
+    def lanes(bank, base, sel, src, lo, hi, group):
+        for e in range(lo, hi):
+            c = e // 2
+            for q in range(8 * (e % 2), 8 * (e % 2) + 8):
+                a = 1024 * c + 64 * q
+                rhs = T.ab[:, a // 16:a // 16 + 4, :] if src == "ab" else T[src][:, a:a + 64]
+                r = ("ab", 2 * c, 2 * c + 2) if src == "ab" else (src, e, e + 1)
+                o = base + 64 * c
+                mm(T[bank][:, o:o + 64], T[sel][:, q, :], rhs, group and q == 0, group and q == 15, [sel, r], [(bank, o, o + 64)])
+
+    def key(lo, hi, sel, src):
+        lanes("pk", 0, sel, src, lo, hi, False)
+
+    def side(lo, hi):
+        lanes("ps", 0, "SELN", "d", lo, hi, True)
 
     def names(c, final=False):
         for g2 in range(2):
             mm(T.pk[:, 64 * c:64 * c + 64], T.PERM[:, 2 * (c % 2) + g2, :], T.PT[:, c // 2, :, g2, :], False, final and g2 == 1, ["PERM", "PT"],
                [("pk", 64 * c, 64 * c + 64)])
 
-    def side(c):
-        lanes(T.ps[:, 64 * c:64 * c + 64], ("ps", 64 * c, 64 * c + 64), "SELN", "d", c, True, True)
-
-    def by_vector(c):
-        ts(T.rl[:, 1024 * c:1024 * c + 1024], T.d[:, 1024 * c:1024 * c + 1024], 0.0, ALU.max, [("d", c, c + 1)], [("rl", c, c + 1)])
-
-    def by_scalar(c):
-        act(T.rl[:, 1024 * c:1024 * c + 1024], T.d[:, 1024 * c:1024 * c + 1024], AF.Abs, [("d", c, c + 1)], [("rl", c, c + 1)])
-
-    def killed_names(t):
+    def killed_names(t, part):
         pw, kf = "PW%d" % t, "kf%d" % t
-        tt(T.t1[:], T[kf][:], T.pa[:, 1], ALU.mult, [kf, ("pa", 256, 512)], ["t1"])
-        ts(T.t2[:], T.t1[:], 5, ALU.arith_shift_right, ["t1"], ["t2"])
-        tt(T[pw][:, 256:512], T.t2[:], T.pa[:, 1], ALU.add, ["t2", ("pa", 256, 512)], [(pw, 256, 512)])
+        if part == 0:
+            tt(T.t1[:], T[kf][:], T.pa[:, 1], ALU.mult, [kf, ("pa", 256, 512)], ["t1"])
+        if part == 1:
+            ts(T.t2[:], T.t1[:], 5, ALU.arith_shift_right, ["t1"], ["t2"])
+        if part == 2:
+            tt(T[pw][:, 256:512], T.t2[:], T.pa[:, 1], ALU.add, ["t2", ("pa", 256, 512)], [(pw, 256, 512)])
 
     def load_s(b):
         c, hj, db = b // 2, b % 2, "db%d" % (b % 4)
         for jj in range(8):
-            mm(T[db][:, :, jj], T.ID[:], T.s[:, 1024 * c + 8 * hj + jj:1024 * c + 1024:16], jj == 0, False, ["ID", ("s", c, c + 1)], [db])
+            mm(T[db][:, :, jj], T.ID[:], T.s[:, 1024 * c + 8 * hj + jj:1024 * c + 1024:16], jj == 0, False, ["ID", ("s", 2 * c, 2 * c + 2)], [db])
 
-    def second(b):
-        c, hj, db = b // 2, b % 2, "db%d" % (b % 4)
+    def minus_n(b):
+        c, db = b // 2, "db%d" % (b % 4)
         for jj in range(8):
             mm(T[db][:, :, jj], T.IDN[:], T.xs[:, 64 * c:64 * c + 64], False, jj == 7, ["IDN", "xs"], [db])
+
+    def size(b):
+        c, hj, db = b // 2, b % 2, "db%d" % (b % 4)
         act(T.ab[:, 64 * c:64 * c + 64, 8 * hj:8 * hj + 8], T[db][:], AF.Abs, [db], [("ab", b, b + 1)])
 
     def esum(c):
         if c < 2:
-            lanes(T.pk[:, 256 + 64 * c:320 + 64 * c], ("pk", 256 + 64 * c, 320 + 64 * c), "SEL", "ab", c, True, True)
+            lanes("pk", 256, "SEL", "ab", 2 * c, 2 * c + 2, True)
         else:
-            lanes(T.ps[:, 128 + 64 * c:192 + 64 * c], ("ps", 128 + 64 * c, 192 + 64 * c), "SEL", "ab", c, True, True)
+            lanes("ps", 128, "SEL", "ab", 2 * c, 2 * c + 2, True)
 
     def near(h):
-        src, r = (T.pk[:, 256:384], ("pk", 256, 384)) if h == 0 else (T.ps[:, 256:384], ("ps", 256, 384))
-        act(T.ns[:, 128 * h:128 * h + 128], src, AF.Sign, [r], [("ns", h, h + 1)], bias=-959.5)
+        bank = ("pk", "ps")[h]
+        act(T.ns[:, 128 * h:128 * h + 128], T[bank][:, 256:384], AF.Sign, [(bank, 256, 384)], [("ns", h, h + 1)], bias=-959.5 * U)
 
-    def tail(t, h):
+    def tail(t, h, part):
         a, b = 128 * h, 128 * h + 128
-        scan(T.fs[:, a:b], T.RSE[:, a:b], T.ns[:, a:b], ALU.add, ALU.min, ["RSE", ("ns", h, h + 1)], [("fs", h, h + 1)])
-        tt(m("o1", 8, 8 * h), T.fs[:, a + 15:b:16], m("pr", 8, 8 * h), ALU.mult, [("fs", h, h + 1), "pr"], [("o1", 8 * h, 8 * h + 8)])
-        q2("o2", "o1", "CV", ALU.add, 8, 8 * h)
-        q1("offV", "o2", 4.0, ALU.mult, n=8, at=8 * h)
-        tt(T.kp[:, a:b], T.KS[:, KW * h:KW * h + KW].indirect(m("offV", 8, 8 * h)), T.a1[:, a:b], ALU.add,
-           [("KS", 4 * h, 4 * h + 4), ("offV", 8 * h, 8 * h + 8), "a1"], [("kp", a, b)])
-        if t == ROUNDS - 1:
+        ov = ("offV", 8 * h, 8 * h + 8)
+        if part == 0:
+            scan(T.fs[:, a:b], T.ns[:, a:b], T.RC[:, a:b], BIG, ALU.min, ALU.add, ["RC", ("ns", h, h + 1)], [("fs", h, h + 1)])
+        if part == 1:
+            ts(m("offV", 8, 8 * h), T.fs[:, a + 15:b:16], 1024.0, ALU.mult, [("fs", h, h + 1), "col"], [ov], col(16), ALU.add)
+        if part == 2:
+            tt(T.kp[:, a:b], T.KS[:, KW * h:KW * h + KW].indirect(m("offV", 8, 8 * h)), T.a1[:, a:b], ALU.add,
+               [("KS", 4 * h, 4 * h + 4), ov, "a1"], [("kp", a, b)])
+        if part == 3 and t == ROUNDS - 1:
             dma("y", [(T.yk[:, a:b], T.kp[:, a:b], [], [("kp", a, b)])])
-        else:
+        if part == 3 and t < ROUNDS - 1:
             cp(T.ku[:, a:b], T.kp[:, a:b], [("kp", a, b)], [("ku", a, b)])
-            send(T.ku[:, a:b], ("ku", a, b), T["kl%d" % (t + 1)][:, a:b], nxt, "u%d%d" % (h, t + 1), 0)
-            send(T.kp[:, a:b], ("kp", a, b), T["kf%d" % (t + 1)][:, a:b], nxt, "f%d%d" % (h, t + 1), 1)
+            send(T.ku[:, a:b], ("ku", a, b), T["kl%d" % (t + 1)][:, a:b], nxt, "u%d%d" % (h, t + 1), None)
+            send(T.kp[:, a:b], ("kp", a, b), T["kf%d" % (t + 1)][:, a:b], nxt, "f%d%d" % (h, t + 1), None)
 
     def compare(rs):
         for r in rs:
-            ts(T.NE[:, 64 * r:64 * r + 64], T.pb[:, r // 4, :], m("t32", 1, r), ALU.not_equal, [("pb", 0, 256), "t32"], [("NE", r, r + 1)])
+            ts(T.NE[:, 64 * r:64 * r + 64], T.pb[:, r // 4, :], m("t32", 1, r), ALU.not_equal, [("pb", 0, 256), "t32"], [("NE", r, r + 1)],
+               2.0 ** 28, ALU.mult)
 
-    def table_writes(t):
-        ts(T.nr[:], T.ak[:], 32.5, ALU.is_lt, ["ak"], ["nr"], 128.0, ALU.mult)
-        tt(T.e2[:], T.nr[:], T.pa[:, 1], ALU.mult, ["nr", ("pa", 256, 512)], ["e2"])
+    def table_writes():
         for c in (3, 2, 1, 0):
             tt(T.X[:].indirect(m("offX", 4, 4 * c)), T.yv[:, 64 * c:64 * c + 64], T.e2[:, 64 * c:64 * c + 64], ALU.add, ["yv", "e2", "offX"], ["X"])
 
-    def column_parts():
-        act(T.yv[:], T.X[:, 0:4096].indirect(m("offY")), AF.Copy, [XT, "offY"], ["yv"])
-        act(T.ak[:], T.d[:].indirect(m("offK")), AF.Abs, ["d", "offK"], ["ak"])
-        act(T.pa[:, 1], T.yv[:], AF.Sign, ["yv"], [("pa", 256, 512)], scale=-1.0, bias=127.5)
-
-    def allowance(t):
-        mm(T.pb[:, 4, 0:16], T.BLK[:], m("kl"), True, True, ["BLK", "kl"], [("pb", 256, 272)])
-        act(T.kj[:], T.pb[:, 4, 0:16], AF.Copy, [("pb", 256, 272)], ["kj", ("kc", t, t + 1)], accum_out=T.kc[:, t:t + 1])
-        ts(T.Ai[:, 0:1], T.kc[:, t:t + 1], T.kc[:, 0:1] if t else 0.0, ALU.add, ["kc"], [("Ai", 0, 1)], 1.0 / 256, ALU.mult)
-        ts(T.Ai[:, 1:2], T.Ai[:, 0:1], 15, ALU.bitwise_and, [("Ai", 0, 1)], [("Ai", 1, 2)])
-        ts(T.thr[:, 0:1], T.Ai[:, 1:2], 4.0, ALU.mult, [("Ai", 1, 2)], ["thr"], 48.0, ALU.add)
+    def allowance(t, part):
+        if part == 0:
+            mm(T.pb[:, 4, 0:16], T.BLK[:], m("kl"), True, True, ["BLK", "kl"], [("pb", 256, 272)])
+            act(T.kj[:], T.pb[:, 4, 0:16], AF.Copy, [("pb", 256, 272)], ["kj", ("kc", t, t + 1)], accum_out=T.kc[:, t:t + 1])
+        if part == 1:
+            ts(T.Ai[:, 0:1], T.kc[:, t:t + 1], T.kc[:, 0:1] if t else 0.0, ALU.add, ["kc"], [("Ai", 0, 1)], 1.0 / 256, ALU.mult)
+        if part == 2:
+            ts(T.Ai[:, 1:2], T.Ai[:, 0:1], 15, ALU.bitwise_and, [("Ai", 0, 1)], [("Ai", 1, 2)])
+        if part == 3:
+            ts(T.thr[:, 0:1], T.Ai[:, 1:2], 4.0 * U, ALU.mult, [("Ai", 1, 2)], ["thr"], 48.0 * U, ALU.add)
 
     phage_forms(0)
+    phage_turn()
     shifted(0, 0)
     shifted(0, 1)
     constants1()
     for t in range(ROUNDS):
         last = t == ROUNDS - 1
         pw = "PW%d" % t
-        sgather(t, 0)
+        sgather(t, 0, 1)
         mm(T.pk[:, 0:256], T.ID[:], T.CD[:], True, False, ["ID", "CD"], [("pk", 0, 256)])
         mm(T.pk[:, 0:256], T.ID[:], T.JR[:], False, False, ["ID", "JR"], [("pk", 0, 256)])
+        sgather(t, 1, 2)
         if t:
             shifted(t, 0)
         shifted_in(t, 0)
-        sgather(t, 1)
-        dgather(0)
-        sgather(t, 2)
-        by_vector(0)
-        side(0)
-        key(0, "SELN", "d")
-        key(0, "SEL2", "rl")
+        sgather(t, 2, 4)
+        dgather(0, 1)
+        if t:
+            allowance(t - 1, 1)
+        dgather(1, 2)
+        if t:
+            allowance(t - 1, 2)
+        else:
+            constants2()
+        sgather(t, 4, 6)
+        by_vector(0, 2)
+        if t:
+            allowance(t - 1, 3)
+        side(0, 2)
+        key(0, 2, "SELN", "d")
+        key(0, 2, "SEL2", "rl")
+        names(0)
         if t:
             shifted(t, 1)
         shifted_in(t, 1)
-        dgather(1)
-        sgather(t, 3)
-        side(1)
+        dgather(2, 4)
+        sgather(t, 6, 8)
         mm(T.pa[:, 1], T.IDF[:], T.Pf[:], True, True, ["IDF", "Pf"], [("pa", 256, 512)])
-        dgather(2)
-        by_scalar(1)
-        side(2)
-        key(1, "SEL", "rl")
-        if t == 0:
-            constants2()
-        names(0)
+        side(2, 4)
+        key(2, 4, "SELN", "d")
+        dgather(4, 6)
+        by_vector(2, 4)
+        by_scalar(4, 6)
+        side(4, 6)
+        key(2, 4, "SEL2", "rl")
         names(1)
-        dgather(3)
-        by_scalar(2)
-        side(3)
-        act(T.sg[:], T.ps[:, 0:256], AF.Sign, [("ps", 0, 256)], ["sg"], bias=-0.5)
-        by_vector(3)
-        key(3, "SELN", "d")
-        key(2, "SEL", "rl")
-        key(3, "SEL2", "rl")
-        mm(T.pk[:, 0:256], T.ID64[:], T.sg[:], False, False, ["ID64", "sg"], [("pk", 0, 256)])
+        dgather(6, 7)
+        side(6, 7)
+        key(6, 7, "SELN", "d")
+        dgather(7, 8)
+        by_vector(6, 7)
+        key(4, 6, "SEL", "rl")
         names(2)
+        side(7, 8)
+        act(T.sg[:], T.ps[:, 0:256], AF.Sign, [("ps", 0, 256)], ["sg"], bias=-0.5 * U)
+        by_vector(7, 8)
+        key(6, 7, "SEL2", "rl")
+        key(7, 8, "SELN", "d")
+        key(7, 8, "SEL2", "rl")
+        mm(T.pk[:, 0:256], T.ID64[:], T.sg[:], False, False, ["ID64", "sg"], [("pk", 0, 256)])
         names(3, True)
         if t == 0:
             constants3()
-        killed_names(t)
+        killed_names(t, 0)
+        killed_names(t, 1)
         for b in range(4):
             load_s(b)
-        scan(T.R[:], T.RST[:], T.pk[:, 0:256], ALU.max, ALU.min, ["RST", ("pk", 0, 256)], ["R"])
+        scan(T.R[:], T.RST[:], T.pk[:, 0:256], 0.0, ALU.max, ALU.min, ["RST", ("pk", 0, 256)], ["R"])
+        killed_names(t, 2)
         r = T.R[:, 15::16]
-        ts(m("ki"), r, 2.0 ** 17, ALU.mult, ["R"], ["ki"])
-        ts(m("kl"), r, -112.0, ALU.is_lt, ["R"], ["kl"], 256.0, ALU.mult)
-        q1("u2", "ki", 11, ALU.arith_shift_right, 2, ALU.bitwise_and)
-        q1("zm", "ki", 17, ALU.arith_shift_right, 3, ALU.bitwise_and)
-        q1("kk", "ki", 13, ALU.arith_shift_right, 15, ALU.bitwise_and)
-        q2("w", "u2", "CW", ALU.add, 32)
-        q1("nm", "ki", 4095, ALU.bitwise_and)
-        q2("h2", "w", "z1", ALU.mult)
+        for out, sh, mk in (("u2", 11, 2), ("zm", 17, 3), ("kk", 13, 15)):
+            ts(m(out), r, sh, ALU.arith_shift_right, ["R"], [out], mk, ALU.bitwise_and)
+        ts(m("kl"), r, -112.0 * U, ALU.is_lt, ["R"], ["kl"], 256.0, ALU.mult)
         ts(m("plt"), r, T.thr[:, 0:1], ALU.is_lt, ["R", "thr"], ["plt"], 256.0, ALU.mult)
-        q2("h3", "h2", "kk", ALU.add)
-        q1("t16", "nm", -2048.0, ALU.add, 1.0 / 16, ALU.mult)
-        q1("fi", "h3", 15, ALU.bitwise_and)
+        q2("w", "u2", "CW", ALU.add, 32)
+        ts(m("nm"), r, 4095, ALU.bitwise_and, ["R"], ["nm"])
         q2("pr", "plt", "kl", ALU.subtract)
+        q2("h2", "w", "z1", ALU.mult)
+        q1("t16", "nm", -2048.0, ALU.add, 1.0 / 16, ALU.mult)
+        q1("un", "pr", -16.0, ALU.mult, 4096.0, ALU.add)
+        qc("offY", "nm")
+        q2("h3", "h2", "kk", ALU.add)
+        q2("t32", "t16", "pr", ALU.add)
+        tt(T.C16[:, 16:32], m("un"), T.C16[:, 0:16], ALU.max, ["un", ("C16", 0, 16)], [("C16", 16, 32)])
+        q2("oP", "kl", "CB", ALU.add, 32)
+        q1("fi", "h3", 15, ALU.bitwise_and)
+        q2("w1", "nm", "CP", ALU.add, 16, 16 * t)
+        q1("u8", "pr", -1.0 / 2048, ALU.mult, 1.0 / 8, ALU.add)
         q2("ko", "kk", "C16", ALU.add, 32)
-        q1("t32", "nm", 2048.0, ALU.add, 1.0 / 16, ALU.mult)
+        q2("fa", "fi", "pr", ALU.mult)
+        q2("w1p", "w1", "pr", ALU.mult)
+        tt(T.RC[:, 15::16], m("u8"), T.CV[:], ALU.add, ["u8", "CV"], ["RC"])
         qc("offK", "ko", 32)
+        q2("oN", "oN", "fa", ALU.add)
         step = (1, 4, 16)[t]
         for i, src in enumerate(("t16", "pr")):
             for q in range(16):
                 a = (4 * q, 16 * (q % 4) + q // 4, q)[t]
                 mm(T.pb[:, 0:4, a:a + 3 * step + 1:step], T.SELT[:, q, :], m(src), i + q == 0, i + q == 16, ["SELT", src], [("pb", 0, 256)])
+        act(T.yv[:], XW.indirect(m("offY")), AF.Copy, [XT, "offY"], ["yv"])
         act(T.sn[:], T.s[:].indirect(m("offF")), AF.Copy, ["s", "offF"], ["sn"])
-        q2("oP", "kl", "CB", ALU.add, 32)
         cp(T.df[:], T.d[:].indirect(m("offF")), ["d", "offF"], ["df"])
         for i, src in enumerate(("sn", "df")):
             mm(T.pa[:, 0], T.ID[:], T[src][:], i == 0, i == 1, ["ID", src], [("pa", 0, 256)])
-        q2("fa", "fi", "pr", ALU.mult)
-        qc("offY", "nm")
-        q2("oN", "oN", "fa", ALU.add)
-        q2("w1", "nm", "DM", ALU.subtract)
         qc("offP", "oP", 32)
-        q2("w1p", "w1", "pr", ALU.mult)
-        if last:
-            column_parts()
+        act(T.ak[:], T.d[:].indirect(m("offK")), AF.Abs, ["d", "offK"], ["ak"])
         for rl in range(4):
             act(T.xs[:, rl::4], T.pa[:, 0, :, rl, :], AF.Copy, [("pa", 0, 256)], [("xs", rl, rl + 1)])
+        compare(range(16))
         ts(T.po[:], T[pw][:].indirect(m("offP")), 4095, ALU.bitwise_and, [pw, "offP"], ["po"])
         if not last:
-            send(T.po[:], "po", T["PW%d" % (t + 1)][:, 0:256], prv, "p%d" % (t + 1), 0)
-        if t == 0:
-            constants4()
-        second(0)
-        second(1)
-        compare(range(16))
+            send(T.po[:], "po", T["PW%d" % (t + 1)][:, 0:256], prv, "p%d" % (t + 1), None)
+        for b in range(4):
+            minus_n(b)
+        act(T.pa[:, 1], T.yv[:], AF.Sign, ["yv"], [("pa", 256, 512)], scale=-1.0, bias=127.5)
+        size(0)
+        size(1)
         load_s(4)
-        second(2)
+        minus_n(4)
+        size(2)
         esum(0)
+        size(3)
         load_s(5)
-        second(3)
+        minus_n(5)
         act(T.a1[:], T.PS[:].indirect(m("offN")), AF.Copy, ["PS", "offN"], ["a1"])
-        scan(T.FE[:], T.RSD[:], T.NE[:], ALU.add, ALU.min, ["RSD", "NE"], ["FE"])
         esum(1)
-        near(0)
-        tt(m("eq"), T.FE[:, 63::64], T.CP[:, 16 * t:16 * t + 16], ALU.is_equal, ["FE", "CP"], ["eq"])
-        q2("w2", "eq", "w1p", ALU.mult)
-        q2("w3", "w2", "DM8", ALU.add)
+        scan(T.FE[:], T.RSD[:], T.NE[:], 0.0, ALU.add, ALU.min, ["RSD", "NE"], ["FE"])
+        ts(T.nr[:], T.ak[:], 32.5, ALU.is_lt, ["ak"], ["nr"], 128.0, ALU.mult)
+        tt(m("w2"), T.FE[:, 63::64], m("w1p"), ALU.add, ["FE", "w1p"], ["w2"])
+        tt(T.e2[:], T.nr[:], T.pa[:, 1], ALU.mult, ["nr", ("pa", 256, 512)], ["e2"])
+        q2("w3", "w2", "DM", ALU.max)
         q1("offX", "w3", 1.0 / 256, ALU.mult)
+        size(4)
+        near(0)
+        load_s(6)
+        minus_n(6)
+        size(5)
+        load_s(7)
+        minus_n(7)
+        table_writes()
         if last:
-            table_writes(t)
-            dma("y", [(T.yx[:], T.X[:, 0:4096], [], [XT])])
+            dma("y", [(T.yx[:], XW, [], [XT])])
+        size(6)
+        esum(2)
+        size(7)
+        esum(3)
+        near(1)
+        for part in range(4):
+            tail(t, 0, part)
+        if last:
             cp(T.pout[:], T.po[:], ["po"], ["pout"])
             dma("y", [(T.yp[:], T.pout[:], [], ["pout"])])
         else:
-            column_parts()
-        tail(t, 0)
-        load_s(6)
-        second(4)
-        load_s(7)
-        second(5)
-        if not last:
-            table_writes(t)
-        second(6)
-        esum(2)
-        second(7)
-        esum(3)
-        near(1)
-        if not last:
             phage_forms(t + 1)
-        tail(t, 1)
+            allowance(t, 0)
+        tail(t, 1, 0)
         if not last:
-            allowance(t)
+            phage_turn()
+        for part in range(1, 4):
+            tail(t, 1, part)
     for sem in sorted(total):
         if waited.get(("g", sem), 0) < total[sem]:
             g.wait_ge(T.sem[sem], total[sem])

@@ -10,7 +10,7 @@ _I = "int32"
 _U = "uint16"
 SCRATCH = {
     "X": ("sbuf", [128, 4160], _B),
-    "s": ("sbuf", [128, 4112], _B), "d": ("sbuf", [128, 4112], _B), "rl": ("sbuf", [128, 4096], _B),
+    "yg": ("sbuf", [128, 4112], _B), "d": ("sbuf", [128, 4096], _B), "s": ("sbuf", [128, 4096], _B), "rl": ("sbuf", [128, 4096], _B),
     "ab": ("sbuf", [128, 256, 16], _B),
     "KS": ("sbuf", [128, 2 * KW], _F), "PS": ("sbuf", [128, 4352], _F),
     "kd": ("dram", [2, 8, 33, 128], _F),
@@ -20,25 +20,27 @@ SCRATCH = {
     "Pm": ("sbuf", [128, 2, 4, 2, 16], _H), "PT": ("sbuf", [128, 2, 4, 2, 16], _H),
     "t1": ("sbuf", [128, 256], _I), "t2": ("sbuf", [128, 256], _I),
     "pid": ("sbuf", [128, 8], _I), "col": ("sbuf", [128, 24], _F), "rowi": ("sbuf", [128, 128], _F), "rowg": ("sbuf", [128, 128], _F),
-    "isel": ("sbuf", [128, 2048], _B), "iselt": ("sbuf", [128, 2048], _B),
-    "SEL": ("sbuf", [128, 16, 128], _B), "SEL2": ("sbuf", [128, 16, 128], _B), "SELN": ("sbuf", [128, 16, 128], _B),
+    "rowq": ("sbuf", [128, 128], _B), "r16": ("sbuf", [128, 16], _F), "OH": ("sbuf", [128, 16], _F),
+    "SEL": ("sbuf", [128, 16, 128], _B), "SELN": ("sbuf", [128, 16, 128], _B),
     "SELT": ("sbuf", [128, 16, 128], _H), "PERM": ("sbuf", [128, 4, 128], _H), "BLK": ("sbuf", [128, 128], _H),
     "ID": ("sbuf", [128, 128], _B), "IDN": ("sbuf", [128, 128], _B), "ID64": ("sbuf", [128, 128], _B),
     "IDF": ("sbuf", [128, 128], _F), "S15": ("sbuf", [128, 128], _F),
     "JR": ("sbuf", [128, 256], _B), "CD": ("sbuf", [128, 256], _B),
     "RST": ("sbuf", [128, 256], _F), "RC": ("sbuf", [128, 256], _F), "RSD": ("sbuf", [128, 1024], _B),
     "C16": ("sbuf", [128, 32], _F), "CB": ("sbuf", [128, 32], _F), "CV": ("sbuf", [128, 16], _F), "DM": ("sbuf", [128, 16], _F),
-    "CW": ("sbuf", [128, 32], _F), "CP": ("sbuf", [128, 48], _F),
+    "CW": ("sbuf", [128, 64], _F), "zi": ("sbuf", [128, 64], _I), "zf": ("sbuf", [128, 64], _F), "zs": ("sbuf", [128, 32], _I), "CP": ("sbuf", [128, 48], _F),
     "R": ("sbuf", [128, 256], _I), "sg": ("sbuf", [128, 256], _B),
     "sf": ("sbuf", [128, 320], _F), "si": ("sbuf", [128, 128], _I), "sh": ("sbuf", [128, 48], _H), "su": ("sbuf", [128, 128], _U),
     "kc": ("sbuf", [128, 4], _F), "kj": ("sbuf", [128, 16], _F), "Ai": ("sbuf", [128, 4], _I), "thr": ("sbuf", [128, 4], _F),
-    "df": ("sbuf", [128, 256], _B), "sn": ("sbuf", [128, 256], _B), "xs": ("sbuf", [128, 256], _B),
-    "ns": ("sbuf", [128, 256], _B), "fs": ("sbuf", [128, 256], _F),
+    "xs": ("sbuf", [128, 256], _B), "ns": ("sbuf", [128, 256], _B), "fs": ("sbuf", [128, 256], _F),
     "NE": ("sbuf", [128, 1024], _B), "FE": ("sbuf", [128, 1024], _B),
     "ak": ("sbuf", [128, 256], _B), "yv": ("sbuf", [128, 256], _B), "nr": ("sbuf", [128, 256], _B), "e2": ("sbuf", [128, 256], _B),
     "pk": ("psum", [128, 512], _F), "ps": ("psum", [128, 512], _F), "pa": ("psum", [128, 2, 4, 4, 16], _F), "pb": ("psum", [128, 8, 64], _F),
 }
 ROUNDS = 3
+MODE = ("vv", "vv", "ss", "ss", "vv", "vv", "ss", "ss")
+YQ = ("vsssvsss", "vsssvsss", "vsssvsss")
+BANKS = ("db0", "db1", "db2", "db3", "pa", "db0", "db1", "db2")
 for _c in range(4):
     SCRATCH["db%d" % _c] = ("psum", [128, 64, 8], _F)
 for _t in range(ROUNDS):
@@ -47,12 +49,90 @@ for _t in range(ROUNDS):
     SCRATCH["kf%d" % _t] = ("sbuf", [128, 256], _F)
 PSUM = ("pk", "ps", "pa", "pb", "db0", "db1", "db2", "db3")
 SEMAPHORES = (["qv", "qs", "qt", "qg"] + ["dm%d" % i for i in range(40)]
-              + [a + b + str(t) for a in "rl" for b in ("p", "u0", "u1", "f0", "f1") for t in (1, 2)])
-SMALL = {"sf": ("w", "z1", "ko", "fo", "oP", "oN", "h2", "plt", "fa", "t32", "w1", "w1p", "w2", "w3", "un", "u8"),
-         "si": ("nm", "kk", "fi", "u2", "zm", "h3"),
+              + [a + b + str(t) for a in "rl" for b in ("p", "u0", "u1") for t in (1, 2)])
+SMALL = {"sf": ("ko", "fo", "oP", "oN", "far", "np", "nq", "fa", "t32", "w1", "w1p", "w2", "w3", "un", "u8"),
+         "si": ("nm", "fi"),
          "sh": ("kl", "pr", "t16"),
-         "su": ("offK", "offF", "offP", "offN", "offY", "offX", "offV")}
+         "su": ("offK", "offF", "offP", "offN", "offX", "offV")}
 WHERE = {n: (b, 16 * i) for b in SMALL for i, n in enumerate(SMALL[b])}
+
+CYCLE, TCYCLE, GATHER, SCATTER = 0.00085, 0.00043, 1.56, 3.5
+PASSES = 400
+CASES = ({"compute": 1.0, "index": 1.0, "tensor": 1.0, "remote": 1.0, "local": 1.0, "wake": 0.2},
+         {"compute": 1.2, "index": 1.2, "tensor": 2.4, "remote": 1.2, "local": 1.2, "wake": 0.22},
+         {"compute": 1.3, "index": 1.6, "tensor": 1.8, "remote": 1.5, "local": 1.5, "wake": 0.25})
+ORDER = []
+
+
+def issue_order(calls):
+    n = len(calls)
+    cases = []
+    for case in CASES:
+        busy = [c["busy"] * case[c["kind"]] for c in calls]
+        late = [c["late"] * case[c["kind"]] for c in calls]
+        fwd = [[] for _ in range(n)]
+        bwd = [[] for _ in range(n)]
+        for j, c in enumerate(calls):
+            for i, how in c["pre"].items():
+                gap = busy[i] + (0.0 if how == "order" else late[i] + case["wake"])
+                fwd[i].append((j, gap))
+                bwd[j].append((i, gap + busy[j] - busy[i]))
+        cases.append((busy, late, fwd, bwd))
+
+    def play(order, busy, late, fwd):
+        can = [0.0] * n
+        free = {}
+        end = 0.0
+        for j in order:
+            at = max(can[j], free.get(calls[j]["q"], 0.0))
+            free[calls[j]["q"]] = at + busy[j]
+            end = max(end, at + busy[j] + late[j])
+            for k, gap in fwd[j]:
+                can[k] = max(can[k], at + gap)
+        return end
+
+    def place(rank, busy, nxt, prev, can):
+        left = [len(p) for p in prev]
+        ready = [j for j in range(n) if left[j] == 0]
+        taken = {}
+        start = [0.0] * n
+        while ready:
+            j = min(ready, key=lambda j: rank[j])
+            ready.remove(j)
+            at = can[j]
+            line = taken.setdefault(calls[j]["q"], [])
+            i = len(line)
+            while i and line[i - 1][1] > at:
+                i -= 1
+            while i < len(line) and line[i][0] < at + busy[j]:
+                at = max(at, line[i][1])
+                i += 1
+            line.insert(i, (at, at + busy[j]))
+            start[j] = at
+            for k, gap in nxt[j]:
+                can[k] = max(can[k], at + gap)
+                left[k] -= 1
+                if left[k] == 0:
+                    ready.append(k)
+        return start
+
+    best = None
+    rank = list(range(n))
+    for turn in range(PASSES):
+        busy, late, fwd, bwd = cases[turn // 2 % len(cases)]
+        start = place(rank, busy, fwd, bwd, [0.0] * n)
+        order = sorted(range(n), key=lambda j: (start[j], j))
+        score = sum(play(order, c[0], c[1], c[2]) / case["compute"] for c, case in zip(cases, CASES))
+        if best is None or score < best[0]:
+            best = (score, order, start)
+        if turn % 2:
+            lo = max(best[2]) * (turn * 7717 % 997) / 997
+            amp = (0.3, 0.8, 1.6)[turn // 2 % 7 % 3]
+            rank = [x + (amp * ((j * 7919 + turn * 104729) ** 2 % 1009) / 1009 if lo < x < lo + 8 else 0) for j, x in enumerate(best[2])]
+        else:
+            back = place([-(start[j] + busy[j]) for j in range(n)], busy, bwd, fwd, list(late))
+            rank = [-(back[j] + busy[j]) for j in range(n)]
+    return best[1]
 
 
 def rank_program(g, core, T, topo):
@@ -61,43 +141,10 @@ def rank_program(g, core, T, topo):
         return
     n_ranks = len(T.cores)
     eng = {"v": g.vector, "s": g.scalar, "t": g.tensor, "g": g, "y": g.sync}
-    count = {"v": 0, "s": 0, "t": 0, "g": 0}
-    total = {}
-    waited = {}
+    calls = []
     log = {}
+    banks = {}
     dmas = [0]
-
-    def deps(q, reads, writes):
-        need = {}
-        for is_w, regs in ((False, reads), (True, writes)):
-            for name, lo, hi in regs:
-                bank = name in PSUM
-                for (l, h, oq, sem, val, ow) in log.get(name, []):
-                    apart = h <= lo or hi <= l
-                    if not bank and apart:
-                        continue
-                    if oq == q:
-                        if q == "t" or (not ow) or apart:
-                            continue
-                    elif not bank and not ow and not is_w:
-                        continue
-                    if val > need.get(sem, 0):
-                        need[sem] = val
-        for sem in sorted(need):
-            if waited.get((q, sem), 0) < need[sem]:
-                waited[(q, sem)] = need[sem]
-                eng[q].wait_ge(T.sem[sem], need[sem])
-
-    def note(q, sem, val, reads, writes):
-        for is_w, regs in ((False, reads), (True, writes)):
-            for name, lo, hi in regs:
-                old = log.get(name, [])
-                if is_w:
-                    old = [e for e in old if not (lo <= e[0] and e[1] <= hi)]
-                else:
-                    old = [e for e in old if not (e[2] == q and not e[5] and e[3] == sem and lo <= e[0] and e[1] <= hi)]
-                old.append((lo, hi, q, sem, val, is_w))
-                log[name] = old
 
     def m(name, n=16, at=0):
         b, i = WHERE[name]
@@ -114,43 +161,61 @@ def rank_program(g, core, T, topo):
             return (b, i, i + 16)
         return (r, 0, 1 << 20)
 
-    def op(q, fn, reads, writes):
-        reads = [reg(r) for r in reads]
-        writes = [reg(r) for r in writes]
-        deps(q, reads, writes)
-        count[q] += 1
-        sem = "q" + q
-        total[sem] = count[q]
-        fn().then_inc(T.sem[sem], 1)
-        note(q, sem, count[q], reads, writes)
+    def call(q, emit, busy, reads, writes, late=0.0, group=None, after=(), told=("done", "done"), kind="compute"):
+        j = len(calls)
+        pre = {i: "order" for i in after}
+        own = q in "vstg" and told[0] == "done"
 
-    def dma(q, pairs):
+        def follow(i, how):
+            if how != "order" or i not in pre:
+                pre[i] = how
+
+        for is_w, regs in ((False, reads), (True, writes)):
+            for name, lo, hi in [reg(r) for r in regs]:
+                if name in PSUM:
+                    b = banks.setdefault(name, [None, [], []])
+                    if b[0] != (q, group):
+                        b[0], b[1], b[2] = (q, group), [], b[1]
+                    for i, _l, _h, _w in b[2]:
+                        follow(i, "order" if calls[i]["q"] == q == "t" else "done")
+                    for i, l, h, w in b[1]:
+                        if q != "t" and i != j and l < hi and lo < h and (w or is_w):
+                            follow(i, "done" if w else "order")
+                    b[1].append((j, lo, hi, is_w))
+                    continue
+                old = log.setdefault(name, [])
+                for l, h, i, w, how in old:
+                    if i != j and l < hi and lo < h and (w or is_w):
+                        follow(i, "order" if (not w and own and calls[i]["own"] and calls[i]["q"] == q) else how)
+                if is_w:
+                    old[:] = [e for e in old if e[2] == j or not (lo <= e[0] and e[1] <= hi)]
+                old.append((lo, hi, j, is_w, told[is_w]))
+        calls.append({"q": q, "emit": emit, "busy": busy, "late": late, "pre": pre, "group": group, "own": own, "kind": kind})
+        return j
+
+    def vector(fn, reads, writes, c, q="v"):
+        return call(q, fn, max(64, abs(c)) * CYCLE, reads, writes, kind="index" if c < 0 else "compute")
+
+    def dma(pairs, kb, after=()):
         sem = "dm%d" % dmas[0]
         dmas[0] += 1
-        val = 16 * len(pairs)
-        total[sem] = val
-        done = []
-        for out, in_, w, r in pairs:
-            r = [reg(x) for x in r]
-            w = [reg(x) for x in w]
-            deps(q, r, w)
-            eng[q].dma_start(out, in_).then_inc(T.sem[sem], 16)
-            done.append((r, w))
-        for r, w in done:
-            note("dma", sem, val, r, [])
-        for r, w in done:
-            for x in w:
-                log[x[0]] = [e for e in log.get(x[0], []) if e[3] == sem or not (x[1] <= e[0] and e[1] <= x[2])]
-                log[x[0]].append((x[1], x[2], "dma", sem, val, True))
 
-    def tt(out, a, b, o, reads, writes):
-        op("v", lambda: g.vector.tensor_tensor(out, a, b, o), reads, writes)
+        def emit():
+            for out, in_, _w, _r in pairs:
+                g.sync.dma_start(out, in_).then_inc(T.sem[sem], 16)
+            return {sem: 16 * len(pairs)}
 
-    def ts(out, a, s1, o1, reads, writes, s2=None, o2=None):
+        return call("y", emit, 0.05 * len(pairs), [x for p in pairs for x in p[3]], [x for p in pairs for x in p[2]], 2.0 + kb / 400.0,
+                    after=after, told=(sem, sem), kind="local")
+
+    def tt(out, a, b, o, reads, writes, c=0):
+        vector(lambda: g.vector.tensor_tensor(out, a, b, o), reads, writes, c)
+
+    def ts(out, a, s1, o1, reads, writes, s2=None, o2=None, c=0):
         if o2 is None:
-            op("v", lambda: g.vector.tensor_scalar(out, a, s1, None, o1), reads, writes)
+            vector(lambda: g.vector.tensor_scalar(out, a, s1, None, o1), reads, writes, c)
         else:
-            op("v", lambda: g.vector.tensor_scalar(out, a, s1, s2, o1, o2), reads, writes)
+            vector(lambda: g.vector.tensor_scalar(out, a, s1, s2, o1, o2), reads, writes, c)
 
     def q1(out, a, s1, o1, s2=None, o2=None, n=16):
         ts(m(out, n), m(a, n), s1, o1, [(a, 0, n)], [(out, 0, n)], s2, o2)
@@ -159,424 +224,344 @@ def rank_program(g, core, T, topo):
         bb = m(b, n) if b in WHERE else T[b][:, at:at + n]
         tt(m(out, n), m(a, n), bb, o, [(a, 0, n), (b, at, at + n)], [(out, 0, n)])
 
-    def cp(out, a, reads, writes):
-        op("v", lambda: g.vector.tensor_copy(out, a), reads, writes)
+    def cp(out, a, reads, writes, c=0):
+        vector(lambda: g.vector.tensor_copy(out, a), reads, writes, c)
 
     def qc(out, a, n=16):
         cp(m(out, n), m(a, n), [(a, 0, n)], [(out, 0, n)])
 
-    def fill(name, c, ap=None, w=None):
-        op("v", lambda: g.vector.memset(T[name][:] if ap is None else ap, c), [], [w or name])
+    def fill(name, x, ap=None, w=None, c=0):
+        vector(lambda: g.vector.memset(T[name][:] if ap is None else ap, x), [], [w or name], c)
 
-    def act(out, a, f, reads, writes, **kw):
-        op("s", lambda: g.scalar.activation(out, a, f, **kw), reads, writes)
+    def act(out, a, f, reads, writes, c, **kw):
+        vector(lambda: g.scalar.activation(out, a, f, **kw), reads, writes, c, "s")
 
-    def mm(out, l, r, st, sp, reads, writes):
-        op("t", lambda: g.tensor.matmul(out, l, r, st, sp), reads, writes)
+    def mms(each, group, reads, bank, c=64, after=()):
+        def emit(st, sp):
+            for k, (out, l, r) in enumerate(each):
+                g.tensor.matmul(out, l, r, st and k == 0, sp and k == len(each) - 1).then_inc(T.sem.qt, 1)
+            return len(each)
 
-    def scan(out, a, b, first, o1, o2, reads, writes):
-        op("v", lambda: g.vector.tensor_tensor_scan(out, a, b, first, o1, o2), reads, writes)
+        return call("t", emit, len(each) * max(64, c) * TCYCLE, reads, [bank], group=(bank, group), after=after, kind="tensor")
+
+    def mm(out, l, r, group, reads, bank, c=64):
+        mms([(out, l, r)], group, reads, bank, c)
+
+    def scan(out, a, b, first, o1, o2, reads, writes, c):
+        vector(lambda: g.vector.tensor_tensor_scan(out, a, b, first, o1, o2), reads, writes, c)
 
     def iota(name, pat, base, mult=0, ap=None, w=None):
-        op("g", lambda: g.iota(T[name][:] if ap is None else ap, pat, base, mult, allow_small_or_imprecise_dtypes=True), [], [w or name])
+        n = 1
+        for _s, k in pat:
+            n *= k
+        call("g", lambda: g.iota(T[name][:] if ap is None else ap, pat, base, mult, allow_small_or_imprecise_dtypes=True),
+             0.13 + 2 * n * CYCLE, [], [w or name])
+
+    def gath(n):
+        return -70 - GATHER * n
 
     def col(i):
         return T.col[:, i:i + 1]
 
+    def rc(i):
+        return ("col", i, i + 1)
+
     XT = ("X", 64, 4160)
     XW = T.X[:, 64:4160]
-    dma("y", [(T.kin[:], T.ka[:], ["kin"], [])])
-    dma("y", [(T.PW0[:, 0:256], T.ph[:], [("PW0", 0, 256)], [])])
-    dma("y", [(XW, T.x0[:], [XT], [])])
+    lists = dma([(T.PW0[:, 0:256], T.ph[:], [("PW0", 0, 256)], []), (T.kin[:], T.ka[:], ["kin"], [])], 128)
+    dma([(XW, T.x0[:], [XT], [])], 800, [lists])
     iota("pid", [[0, 1]], 0, 1, T.pid[:, 0:1])
     iota("rowi", [[1, 128]], 0)
     iota("rowg", [[1, 8], [0, 16]], 0)
-    iota("isel", [[-1, 16], [32, 8], [1, 16]], 0)
+    iota("r16", [[1, 16]], 0)
+    iota("PS", [[0, 4352]], 0)
     iota("JR", [[0, 16], [8192, 16]], 4096)
     iota("C16", [[1024, 4], [16, 4]], 0, 0, T.C16[:, 0:16], ("C16", 0, 16))
     iota("CB", [[0, 2], [64, 4], [1, 4]], 0)
     iota("CV", [[0, 2], [64, 2], [1, 4]], 4096 + 23 * 128)
     iota("DM", [[0, 4], [4096, 4]], 0)
-    iota("CW", [[2, 2], [0, 16]], -1)
+    iota("CW", [[1, 2], [0, 16], [-1, 2]], 0)
+    iota("zi", [[0, 64]], 0)
     for i in range(3):
         iota("CP", [[0, 4], [4 ** i, 4]], -63, 0, T.CP[:, 16 * i:16 * i + 16], ("CP", 16 * i, 16 * i + 16))
-    iota("iselt", [[1, 16], [32, 8], [0, 16]], 0)
-    fill("RSD", -2.0 ** 21)
+    fill("RSD", -2.0 ** 21, c=512)
     fill("RSD", BIG, T.RSD[:, 0::64])
-    for a in range(0, 4352, 1024):
-        n = min(1024, 4352 - a)
-        act(T.PS[:, a:a + n], T.RSD[:, 0:n], AF.Copy, ["RSD"], [("PS", a, a + n)], scale=0.0)
-    dma("y", [(T.KS[0::16, KW * h:KW * h + 2048], T.PS[1::16, 0:2048], [("KS", 4 * h, 4 * h + 1)], [("PS", 0, 2048)]) for h in range(2)]
-        + [(T.kd[h, :, 0, :], T.PS[1::16, 0:128], [("kd", 40 * h, 40 * h + 1)], [("PS", 0, 128)]) for h in range(2)])
+    dma([(T.KS[0::16, KW * h:KW * h + 2048], T.PS[1::16, 0:2048], [("KS", 4 * h, 4 * h + 1)], [("PS", 0, 2048)]) for h in range(2)]
+        + [(T.kd[h, :, 0, :], T.PS[1::16, 0:128], [("kd", 40 * h, 40 * h + 1)], [("PS", 0, 128)]) for h in range(2)], 128)
     pid = lambda i: T.pid[:, i:i + 1]
     for i, sh, mk in ((1, 0, 15), (2, 4, 7), (3, 0, 3), (4, 2, 3), (5, 4, 1)):
         ts(pid(i), pid(0), sh, ALU.arith_shift_right, [("pid", 0, 1)], [("pid", i, i + 1)], mk, ALU.bitwise_and)
     cp(T.col[:, 0:6], T.pid[:, 0:6], [("pid", 0, 6)], [("col", 0, 6)])
-    for i, a, s1, s2 in ((6, 2, 32.0, 0.0), (7, 2, 32.0, col(1)), (8, 1, 64.0, 0.0), (9, 1, 4.0, 0.0), (10, 0, 1.0, -16.0), (11, 0, 1.0, 16.0),
+    for i, a, s1, s2 in ((6, 2, 16.0, 0.0), (8, 1, 64.0, 0.0), (9, 1, 4.0, 0.0), (10, 0, 1.0, -16.0), (11, 0, 1.0, 16.0),
                          (12, 5, -1.0, 1.0), (13, 5, 1.0, 0.0), (14, 3, 16.0, col(4)), (16, 1, 4.0, -4096.0), (17, 1, 256.0, 0.0)):
-        ts(col(i), col(a), s1, ALU.mult, [("col", 0, 6)], [("col", i, i + 1)], s2, ALU.add)
-    ts(col(15), col(1), 15.0, ALU.is_equal, [("col", 0, 6)], [("col", 15, 16)])
-    ts(T.ID[:], T.rowi[:], col(0), ALU.is_equal, ["rowi", "col"], ["ID"])
-    ts(T.IDF[:], T.rowi[:], col(0), ALU.is_equal, ["rowi", "col"], ["IDF"])
-    ts(T.S15[:], T.rowg[:], col(2), ALU.is_equal, ["rowg", "col"], ["S15"], col(15), ALU.mult)
-    fill("CD", -992.0 * U)
+        ts(col(i), col(a), s1, ALU.mult, [("col", 0, 6)], [rc(i)], s2, ALU.add)
+    ts(col(15), col(1), 15.0, ALU.is_equal, [("col", 0, 6)], [rc(15)])
+    ts(T.ID[:], T.rowi[:], col(0), ALU.is_equal, ["rowi", rc(0)], ["ID"], c=128)
+    ts(T.IDF[:], T.rowi[:], col(0), ALU.is_equal, ["rowi", rc(0)], ["IDF"], c=128)
+    ts(T.S15[:], T.rowg[:], col(2), ALU.is_equal, ["rowg", rc(2), rc(15)], ["S15"], col(15), ALU.mult, c=128)
+    fill("CD", -992.0 * U, c=128)
     fill("thr", 48.0 * U)
-    cp(T.kl0[:], T.kin[:], ["kin"], ["kl0"])
-    cp(T.kf0[:], T.kin[:], ["kin"], ["kf0"])
-
-    def constants1():
-        ts(T.ID64[:], T.ID[:], U / 64, ALU.mult, ["ID"], ["ID64"])
-        ts(T.IDN[:], T.ID[:], -1.0, ALU.mult, ["ID"], ["IDN"])
-        for h in range(2):
-            for g2 in range(2):
-                ts(T.PERM[:, 2 * h + g2, :], T.rowi[:], col((10, 0, 11)[g2 - h + 1]), ALU.is_equal, ["rowi", "col"], [("PERM", 2 * h + g2, 2 * h + g2 + 1)],
-                   col(12 + h), ALU.mult)
-        fill("RST", -BIG)
-        fill("RST", BIG, T.RST[:, 0::16])
-        fill("RC", -1.0 / 8)
-        fill("s", 1024.0, T.s[:, 4096:4112], ("s", 8, 9))
-        fill("d", 0.0, T.d[:, 4096:4112], ("d", 8, 9))
-        fill("X", 0.0, T.X[:, 0:64], ("X", 0, 64))
-        ts(T.BLK[:], T.rowg[:], col(2), ALU.is_equal, ["rowg", "col"], ["BLK"])
-        for name, w in (("SELN", -U), ("SEL2", 2 * U)):
-            ts(T[name][:], T.isel[:], col(6), ALU.is_equal, ["isel", "col"], [name], w, ALU.mult)
-
-    def constants2():
-        ts(T.SEL[:], T.isel[:], col(6), ALU.is_equal, ["isel", "col"], ["SEL"], U, ALU.mult)
-
-    def constants3():
-        ts(T.C16[:, 0:16], T.C16[:, 0:16], col(8), ALU.add, [("C16", 0, 16), "col"], [("C16", 0, 16)])
-        for name, c in (("CB", 9), ("DM", 17)):
-            ts(T[name][:], T[name][:], col(c), ALU.add, [name, "col"], [name])
-        ts(T.CV[:], T.CV[:], 1.0 / 1024, ALU.mult, ["CV"], ["CV"])
-        for i, c in enumerate((9, 14, 1)):
-            r = ("CP", 16 * i, 16 * i + 16)
-            ts(T.CP[:, r[1]:r[2]], T.CP[:, r[1]:r[2]], col(c), ALU.add, [r, "col"], [r], -8192.0, ALU.mult)
-        ts(T.SELT[:], T.iselt[:], col(7), ALU.is_equal, ["iselt", "col"], ["SELT"])
-        ts(T.CP[:], T.CP[:], 64.0, ALU.add, ["CP"], ["CP"])
+    cp(T.kl0[:], T.kin[:], ["kin"], ["kl0"], 256)
+    ts(T.ID64[:], T.ID[:], U / 64, ALU.mult, ["ID"], ["ID64"])
+    ts(T.IDN[:], T.ID[:], -1.0, ALU.mult, ["ID"], ["IDN"])
+    for h in range(2):
+        for g2 in range(2):
+            i = (10, 0, 11)[g2 - h + 1]
+            ts(T.PERM[:, 2 * h + g2, :], T.rowi[:], col(i), ALU.is_equal, ["rowi", rc(i), rc(12 + h)], [("PERM", 2 * h + g2, 2 * h + g2 + 1)],
+               col(12 + h), ALU.mult, c=128)
+    fill("RST", -BIG, c=256)
+    fill("RST", BIG, T.RST[:, 0::16])
+    fill("RC", -1.0 / 8, c=256)
+    fill("yg", 1024.0, T.yg[:, 4096:4112], ("yg", 8, 9))
+    fill("X", 0.0, T.X[:, 0:64], ("X", 0, 64))
+    ts(T.BLK[:], T.rowg[:], col(2), ALU.is_equal, ["rowg", rc(2)], ["BLK"], c=128)
+    ts(T.rowq[:], T.rowi[:], col(6), ALU.subtract, ["rowi", rc(6)], ["rowq"], c=128)
+    ts(T.OH[:], T.r16[:], col(1), ALU.is_equal, ["r16", rc(1)], ["OH"])
+    for q in range(16):
+        ts(T.SELN[:, q, :], T.rowq[:], float(q), ALU.is_equal, ["rowq"], [("SELN", q, q + 1)], -U, ALU.mult)
+        ts(T.SELT[:, q, :], T.BLK[:], T.OH[:, q:q + 1], ALU.mult, ["BLK", "OH"], [("SELT", q, q + 1)])
+    act(T.SEL[:], T.SELN[:], AF.Copy, ["SELN"], ["SEL"], 2048, scale=-1.0)
+    ts(T.C16[:, 0:16], T.C16[:, 0:16], col(8), ALU.add, [("C16", 0, 16), rc(8)], [("C16", 0, 16)])
+    for name, c in (("CB", 9), ("DM", 17)):
+        ts(T[name][:], T[name][:], col(c), ALU.add, [name, rc(c)], [name])
+    ts(T.CV[:], T.CV[:], 1.0 / 1024, ALU.mult, ["CV"], ["CV"])
+    for i, c in enumerate((9, 14, 1)):
+        r = ("CP", 16 * i, 16 * i + 16)
+        ts(T.CP[:, r[1]:r[2]], T.CP[:, r[1]:r[2]], col(c), ALU.add, [r, rc(c)], [r], -8192.0, ALU.mult)
+    ts(T.CP[:], T.CP[:], 64.0, ALU.add, ["CP"], ["CP"])
 
     nxt = T.cores[(rank + 1) % n_ranks]
     prv = T.cores[(rank - 1) % n_ranks]
 
-    def engines(dst, part):
-        es = topo.engines(core, dst)
-        n = len(es) // 2
-        return es if part is None else es[part * n:part * n + n]
-
-    def landed(r, sem, n):
-        total[sem] = n
-        r = reg(r)
-        log.setdefault(r[0], []).append((r[1], r[2], "rem", sem, n, True))
-
-    def send(src, r, land, dst, tag, part):
+    def send(src, r, land, w, dst, tag):
         rid, pid_, _ = topo.addr(dst)
-        es = engines(dst, part)
-        regs = [reg(r)]
-        deps("g", regs, [])
-        g.remote_dma(land, src, T.sem["r" + tag], T.sem["l" + tag], pid_, rid, sum(1 << e for e in es))
-        total["l" + tag] = len(es)
-        note("rem", "l" + tag, len(es), regs, [])
+        es = topo.engines(core, dst)
+        other = prv if dst == nxt else nxt
+
+        def emit():
+            g.remote_dma(land, src, T.sem["r" + tag], T.sem["l" + tag], pid_, rid, sum(1 << e for e in es))
+            return {"l" + tag: len(es), "r" + tag: len(topo.engines(other, core))}
+
+        call("g", emit, 0.5, [r], [w], 4.6 if tag == "p1" else 2.6, told=("l" + tag, "r" + tag), kind="remote")
 
     def phage_forms(t):
         pw = "PW%d" % t
-        if t:
-            landed((pw, 0, 256), "rp%d" % t, len(engines(nxt, None)))
-        cp(T.pu[:], T[pw][:, 0:256], [(pw, 0, 256)], ["pu"])
-        cp(T.Pf[:], T[pw][:, 0:256], [(pw, 0, 256)], ["Pf"])
+        cp(T.pu[:], T[pw][:, 0:256], [(pw, 0, 256)], ["pu"], 256)
+        cp(T.Pf[:], T[pw][:, 0:256], [(pw, 0, 256)], ["Pf"], 256)
+        dma([(T.PS[0::16, 256:4352], T.Pf[:], ["PS"], ["Pf"])], 128)
         for rl in range(4):
             ts(T.Pm[:, :, rl], T.pu[:, rl::4], -2048.0, ALU.add, ["pu"], [("Pm", rl, rl + 1)])
-        dma("y", [(T.PS[0::16, 256:4352], T.Pf[:], ["PS"], ["Pf"])])
-
-    def phage_turn():
-        op("v", lambda: g.vector.transpose(T.PT[:], T.Pm[:]), ["Pm"], ["PT"])
+        vector(lambda: g.vector.transpose(T.PT[:], T.Pm[:]), ["Pm"], ["PT"], 128)
 
     def shifted(t, h):
         kf = "kf%d" % t
         a, b = 128 * h, 128 * h + 128
-        if t:
-            landed((kf, a, b), "rf%d%d" % (h, t), len(engines(prv, None)))
-        mm(T.pa[:, 0, 2 * h:2 * h + 2], T.S15[:], T[kf][:, a:b], True, True, ["S15", (kf, a, b)], [("pa", a, b)])
-        act(T.k15[:, a:b], T.pa[:, 0, 2 * h:2 * h + 2], AF.Copy, [("pa", a, b)], [("k15", a, b)])
+        cp(T[kf][:, a:b], T["kl%d" % t][:, a:b], [("kl%d" % t, a, b)], [(kf, a, b)], 128)
         o = 40 * h
-        dma("y", [(T.kd[h, :, 1:17, :], T[kf][:, a:b], [("kd", o + 1, o + 17)], [(kf, a, b)]),
-                  (T.kd[h, :, 17:33, :], T.k15[:, a:b], [("kd", o + 17, o + 33)], [("k15", a, b)])])
-
-    def shifted_in(t, h):
-        kf = "kf%d" % t
-        a, b = 128 * h, 128 * h + 128
-        o = 40 * h
+        dma([(T.kd[h, :, 1:17, :], T[kf][:, a:b], [("kd", o + 1, o + 17)], [(kf, a, b)])]
+            + [(T.kd[h, :, i, :], T[kf][15::16, a:b], [("kd", o + i, o + i + 1)], [(kf, a, b)]) for i in range(17, 32)], 128)
         w = [("KS", 4 * h + 2, 4 * h + 3)]
-        dma("y", [(T.KS[j::16, KW * h:KW * h + 2048], T.kd[h, :, j + 1:j + 17, :], w, [("kd", o, o + 33)]) for j in range(1, 16)]
+        dma([(T.KS[j::16, KW * h:KW * h + 2048], T.kd[h, :, j + 1:j + 17, :], w, [("kd", o, o + 33)]) for j in range(1, 16)]
             + [(T.KS[:, KW * h + 2048:KW * h + 2176], T.kd[h, :, 0:16, :], w, [("kd", o, o + 33)]),
-               (T.KS[:, KW * h + 2176:KW * h + 2304], T[kf][:, a:b], w, [(kf, a, b)])])
+               (T.KS[:, KW * h + 2176:KW * h + 2304], T[kf][:, a:b], w, [(kf, a, b)])], 1152)
 
-    def sgather(t, lo, hi):
-        kl = "kl%d" % t
-        if t and lo % 4 == 0:
-            landed((kl, 32 * lo, 32 * lo + 128), "ru%d%d" % (lo // 4, t), len(engines(prv, None)))
-        act(T.s[:, 512 * lo:512 * hi], XW.indirect(T[kl][:, 32 * lo:32 * hi]), AF.Copy, [XT, (kl, 32 * lo, 32 * hi)], [("s", lo, hi)])
-
-    def dgather(lo, hi):
-        tt(T.d[:, 512 * lo:512 * hi], XW.indirect(T.pu[:, 32 * lo:32 * hi]), T.s[:, 512 * lo:512 * hi], ALU.subtract,
-           [XT, "pu", ("s", lo, hi)], [("d", lo, hi)])
-
-    def by_vector(lo, hi):
-        ts(T.rl[:, 512 * lo:512 * hi], T.d[:, 512 * lo:512 * hi], 0.0, ALU.max, [("d", lo, hi)], [("rl", lo, hi)])
-
-    def by_scalar(lo, hi):
-        act(T.rl[:, 512 * lo:512 * hi], T.d[:, 512 * lo:512 * hi], AF.Abs, [("d", lo, hi)], [("rl", lo, hi)])
-
-    def lanes(bank, base, sel, src, lo, hi, group):
-        for e in range(lo, hi):
-            c = e // 2
-            for q in range(8 * (e % 2), 8 * (e % 2) + 8):
-                a = 1024 * c + 64 * q
-                rhs = T.ab[:, a // 16:a // 16 + 4, :] if src == "ab" else T[src][:, a:a + 64]
-                r = ("ab", 2 * c, 2 * c + 2) if src == "ab" else (src, e, e + 1)
-                o = base + 64 * c
-                mm(T[bank][:, o:o + 64], T[sel][:, q, :], rhs, group and q == 0, group and q == 15, [sel, r], [(bank, o, o + 64)])
-
-    def key(lo, hi, sel, src):
-        lanes("pk", 0, sel, src, lo, hi, False)
-
-    def side(lo, hi):
-        lanes("ps", 0, "SELN", "d", lo, hi, True)
-
-    def names(c, final=False):
-        for g2 in range(2):
-            mm(T.pk[:, 64 * c:64 * c + 64], T.PERM[:, 2 * (c % 2) + g2, :], T.PT[:, c // 2, :, g2, :], False, final and g2 == 1, ["PERM", "PT"],
-               [("pk", 64 * c, 64 * c + 64)])
-
-    def killed_names(t, part):
-        pw, kf = "PW%d" % t, "kf%d" % t
-        if part == 0:
-            tt(T.t1[:], T[kf][:], T.pa[:, 1], ALU.mult, [kf, ("pa", 256, 512)], ["t1"])
-        if part == 1:
-            ts(T.t2[:], T.t1[:], 5, ALU.arith_shift_right, ["t1"], ["t2"])
-        if part == 2:
-            tt(T[pw][:, 256:512], T.t2[:], T.pa[:, 1], ALU.add, ["t2", ("pa", 256, 512)], [(pw, 256, 512)])
-
-    def load_s(b):
-        c, hj, db = b // 2, b % 2, "db%d" % (b % 4)
-        for jj in range(8):
-            mm(T[db][:, :, jj], T.ID[:], T.s[:, 1024 * c + 8 * hj + jj:1024 * c + 1024:16], jj == 0, False, ["ID", ("s", 2 * c, 2 * c + 2)], [db])
-
-    def minus_n(b):
-        c, db = b // 2, "db%d" % (b % 4)
-        for jj in range(8):
-            mm(T[db][:, :, jj], T.IDN[:], T.xs[:, 64 * c:64 * c + 64], False, jj == 7, ["IDN", "xs"], [db])
-
-    def size(b):
-        c, hj, db = b // 2, b % 2, "db%d" % (b % 4)
-        act(T.ab[:, 64 * c:64 * c + 64, 8 * hj:8 * hj + 8], T[db][:], AF.Abs, [db], [("ab", b, b + 1)])
-
-    def esum(c):
-        if c < 2:
-            lanes("pk", 256, "SEL", "ab", 2 * c, 2 * c + 2, True)
+    def ygather(q, e):
+        out, a = T.yg[:, 512 * e:512 * e + 512], XW.indirect(T.pu[:, 32 * e:32 * e + 32])
+        if q == "v":
+            cp(out, a, [XT, "pu"], [("yg", e, e + 1)], gath(512))
         else:
-            lanes("ps", 128, "SEL", "ab", 2 * c, 2 * c + 2, True)
+            act(out, a, AF.Copy, [XT, "pu"], [("yg", e, e + 1)], gath(512))
 
-    def near(h):
-        bank = ("pk", "ps")[h]
-        act(T.ns[:, 128 * h:128 * h + 128], T[bank][:, 256:384], AF.Sign, [(bank, 256, 384)], [("ns", h, h + 1)], bias=-959.5 * U)
+    def lanes(bank, base, sel, src, e, group):
+        c = e // 2
+        each = []
+        for q in range(8 * (e % 2), 8 * (e % 2) + 8):
+            a = 1024 * c + 64 * q
+            rhs = T.ab[:, a // 16:a // 16 + 4, :] if src == "ab" else T[src][:, a:a + 64]
+            each.append((T[bank][:, base + 64 * c:base + 64 * c + 64], T[sel][:, q, :], rhs))
+        return [mms(each, group, [sel, ("ab", 2 * c, 2 * c + 2) if src == "ab" else (src, e, e + 1)], bank)]
 
-    def tail(t, h, part):
+    def first(t, e):
+        kl, a, b, r = "kl%d" % t, 512 * e, 512 * e + 512, (e, e + 1)
+        s = XW.indirect(T[kl][:, 32 * e:32 * e + 32])
+        if MODE[e][0] == "v":
+            tt(T.d[:, a:b], s, T.yg[:, a:b], ALU.subtract, [XT, (kl, 32 * e, 32 * e + 32), ("yg",) + r], [("d",) + r], gath(512))
+        else:
+            act(T.s[:, a:b], s, AF.Copy, [XT, (kl, 32 * e, 32 * e + 32)], [("s",) + r], gath(512))
+            tt(T.d[:, a:b], T.s[:, a:b], T.yg[:, a:b], ALU.subtract, [("s",) + r, ("yg",) + r], [("d",) + r], 512)
+        lanes("ps", 0, "SEL", "d", e, ("side", t))
+        if MODE[e][1] == "s":
+            act(T.rl[:, a:b], T.d[:, a:b], AF.Abs, [("d",) + r], [("rl",) + r], 512)
+            return lanes("pk", 0, "SEL", "rl", e, ("key", t))
+        ts(T.rl[:, a:b], T.d[:, a:b], 0.0, ALU.max, [("d",) + r], [("rl",) + r], 2.0, ALU.mult, c=256)
+        return lanes("pk", 0, "SELN", "d", e, ("key", t)) + lanes("pk", 0, "SEL", "rl", e, ("key", t))
+
+    def names(t, c, sums):
+        mms([(T.pk[:, 64 * c:64 * c + 64], T.PERM[:, 2 * (c % 2) + g2, :], T.PT[:, c // 2, :, g2, :]) for g2 in range(2)],
+            ("key", t), ["PERM", "PT"], "pk", after=sums)
+
+    def killed_names(t, h):
+        pw, kf = "PW%d" % t, "kf%d" % t
         a, b = 128 * h, 128 * h + 128
+        p = T.pa[:, 1, 2 * h:2 * h + 2]
+        tt(T.t1[:, a:b], T[kf][:, a:b], p, ALU.mult, [(kf, a, b), "pa"], [("t1", a, b)], 128)
+        ts(T.t2[:, a:b], T.t1[:, a:b], 5, ALU.arith_shift_right, [("t1", a, b)], [("t2", a, b)], c=128)
+        tt(T[pw][:, 256 + a:256 + b], T.t2[:, a:b], p, ALU.add, [("t2", a, b), "pa"], [(pw, 256 + a, 256 + b)], 128)
+
+    def second(t, b):
+        c, hj, db = b // 2, b % 2, BANKS[b]
+        out = [T.pa[:, :, :, :, jj::8] if db == "pa" else T[db][:, :, jj] for jj in range(8)]
+        for src in ("s",) if MODE[2 * c][0] == "s" else ("d", "yg"):
+            mms([(out[jj], T.ID[:], T[src][:, 1024 * c + 8 * hj + jj:1024 * c + 1024:16]) for jj in range(8)], ("second", t, b),
+                ["ID", (src, 2 * c, 2 * c + 2)], db)
+        mms([(out[jj], T.IDN[:], T.xs[:, 64 * c:64 * c + 64]) for jj in range(8)], ("second", t, b), ["IDN", "xs"], db)
+        act(T.ab[:, 64 * c:64 * c + 64, 8 * hj:8 * hj + 8], T[db][:], AF.Abs, [db], [("ab", b, b + 1)], 512)
+
+    def tail(t, h):
+        a, b = 128 * h, 128 * h + 128
+        bank = ("pk", "ps")[h]
+        for e in range(4 * h, 4 * h + 4):
+            lanes(bank, 256 - 128 * h, "SEL", "ab", e, ("near", t))
+        act(T.ns[:, a:b], T[bank][:, 256:384], AF.Sign, [bank], [("ns", h, h + 1)], 128, bias=-959.5 * U)
         ov = ("offV", 8 * h, 8 * h + 8)
-        if part == 0:
-            scan(T.fs[:, a:b], T.ns[:, a:b], T.RC[:, a:b], BIG, ALU.min, ALU.add, ["RC", ("ns", h, h + 1)], [("fs", h, h + 1)])
-        if part == 1:
-            ts(m("offV", 8, 8 * h), T.fs[:, a + 15:b:16], 1024.0, ALU.mult, [("fs", h, h + 1), "col"], [ov], col(16), ALU.add)
-        if part == 2:
-            tt(T.kp[:, a:b], T.KS[:, KW * h:KW * h + KW].indirect(m("offV", 8, 8 * h)), T.a1[:, a:b], ALU.add,
-               [("KS", 4 * h, 4 * h + 4), ov, "a1"], [("kp", a, b)])
-        if part == 3 and t == ROUNDS - 1:
-            dma("y", [(T.yk[:, a:b], T.kp[:, a:b], [], [("kp", a, b)])])
-        if part == 3 and t < ROUNDS - 1:
-            cp(T.ku[:, a:b], T.kp[:, a:b], [("kp", a, b)], [("ku", a, b)])
-            send(T.ku[:, a:b], ("ku", a, b), T["kl%d" % (t + 1)][:, a:b], nxt, "u%d%d" % (h, t + 1), None)
-            send(T.kp[:, a:b], ("kp", a, b), T["kf%d" % (t + 1)][:, a:b], nxt, "f%d%d" % (h, t + 1), None)
+        scan(T.fs[:, a:b], T.ns[:, a:b], T.RC[:, a:b], BIG, ALU.min, ALU.add, ["RC", ("ns", h, h + 1)], [("fs", h, h + 1)], 128)
+        ts(m("offV", 8, 8 * h), T.fs[:, a + 15:b:16], 1024.0, ALU.mult, [("fs", h, h + 1), rc(16)], [ov], col(16), ALU.add)
+        tt(T.kp[:, a:b], T.KS[:, KW * h:KW * h + KW].indirect(m("offV", 8, 8 * h)), T.a1[:, a:b], ALU.add,
+           [("KS", 4 * h, 4 * h + 4), ov, "a1"], [("kp", a, b)], gath(128))
+        if t == ROUNDS - 1:
+            dma([(T.yk[:, a:b], T.kp[:, a:b], [], [("kp", a, b)])], 64)
+        else:
+            cp(T.ku[:, a:b], T.kp[:, a:b], [("kp", a, b)], [("ku", a, b)], 128)
+            kl = "kl%d" % (t + 1)
+            send(T.ku[:, a:b], ("ku", a, b), T[kl][:, a:b], (kl, a, b), nxt, "u%d%d" % (h, t + 1))
 
-    def compare(rs):
-        for r in rs:
-            ts(T.NE[:, 64 * r:64 * r + 64], T.pb[:, r // 4, :], m("t32", 1, r), ALU.not_equal, [("pb", 0, 256), "t32"], [("NE", r, r + 1)],
-               2.0 ** 28, ALU.mult)
+    def allowance(t):
+        mm(T.pb[:, 4, 0:16], T.BLK[:], m("kl"), ("kills", t), ["BLK", "kl"], "pb")
+        act(T.kj[:], T.pb[:, 4, 0:16], AF.Copy, ["pb"], ["kj", ("kc", t, t + 1)], 200, accum_out=T.kc[:, t:t + 1])
+        ts(T.Ai[:, 0:1], T.kc[:, t:t + 1], T.kc[:, 0:1] if t else 0.0, ALU.add, ["kc"], [("Ai", 0, 1)], 1.0 / 256, ALU.mult)
+        ts(T.Ai[:, 1:2], T.Ai[:, 0:1], 15, ALU.bitwise_and, [("Ai", 0, 1)], [("Ai", 1, 2)])
+        ts(T.thr[:, 0:1], T.Ai[:, 1:2], 4.0 * U, ALU.mult, [("Ai", 1, 2)], ["thr"], 48.0 * U, ALU.add)
 
-    def table_writes():
-        for c in (3, 2, 1, 0):
-            tt(T.X[:].indirect(m("offX", 4, 4 * c)), T.yv[:, 64 * c:64 * c + 64], T.e2[:, 64 * c:64 * c + 64], ALU.add, ["yv", "e2", "offX"], ["X"])
-
-    def allowance(t, part):
-        if part == 0:
-            mm(T.pb[:, 4, 0:16], T.BLK[:], m("kl"), True, True, ["BLK", "kl"], [("pb", 256, 272)])
-            act(T.kj[:], T.pb[:, 4, 0:16], AF.Copy, [("pb", 256, 272)], ["kj", ("kc", t, t + 1)], accum_out=T.kc[:, t:t + 1])
-        if part == 1:
-            ts(T.Ai[:, 0:1], T.kc[:, t:t + 1], T.kc[:, 0:1] if t else 0.0, ALU.add, ["kc"], [("Ai", 0, 1)], 1.0 / 256, ALU.mult)
-        if part == 2:
-            ts(T.Ai[:, 1:2], T.Ai[:, 0:1], 15, ALU.bitwise_and, [("Ai", 0, 1)], [("Ai", 1, 2)])
-        if part == 3:
-            ts(T.thr[:, 0:1], T.Ai[:, 1:2], 4.0 * U, ALU.mult, [("Ai", 1, 2)], ["thr"], 48.0 * U, ALU.add)
-
-    phage_forms(0)
-    phage_turn()
-    shifted(0, 0)
-    shifted(0, 1)
-    constants1()
     for t in range(ROUNDS):
         last = t == ROUNDS - 1
         pw = "PW%d" % t
-        sgather(t, 0, 1)
-        mm(T.pk[:, 0:256], T.ID[:], T.CD[:], True, False, ["ID", "CD"], [("pk", 0, 256)])
-        mm(T.pk[:, 0:256], T.ID[:], T.JR[:], False, False, ["ID", "JR"], [("pk", 0, 256)])
-        sgather(t, 1, 2)
-        if t:
-            shifted(t, 0)
-        shifted_in(t, 0)
-        sgather(t, 2, 4)
-        dgather(0, 1)
-        if t:
-            allowance(t - 1, 1)
-        dgather(1, 2)
-        if t:
-            allowance(t - 1, 2)
-        else:
-            constants2()
-        sgather(t, 4, 6)
-        by_vector(0, 2)
-        if t:
-            allowance(t - 1, 3)
-        side(0, 2)
-        key(0, 2, "SELN", "d")
-        key(0, 2, "SEL2", "rl")
-        names(0)
-        if t:
-            shifted(t, 1)
-        shifted_in(t, 1)
-        dgather(2, 4)
-        sgather(t, 6, 8)
-        mm(T.pa[:, 1], T.IDF[:], T.Pf[:], True, True, ["IDF", "Pf"], [("pa", 256, 512)])
-        side(2, 4)
-        key(2, 4, "SELN", "d")
-        dgather(4, 6)
-        by_vector(2, 4)
-        by_scalar(4, 6)
-        side(4, 6)
-        key(2, 4, "SEL2", "rl")
-        names(1)
-        dgather(6, 7)
-        side(6, 7)
-        key(6, 7, "SELN", "d")
-        dgather(7, 8)
-        by_vector(6, 7)
-        key(4, 6, "SEL", "rl")
-        names(2)
-        side(7, 8)
-        act(T.sg[:], T.ps[:, 0:256], AF.Sign, [("ps", 0, 256)], ["sg"], bias=-0.5 * U)
-        by_vector(7, 8)
-        key(6, 7, "SEL2", "rl")
-        key(7, 8, "SELN", "d")
-        key(7, 8, "SEL2", "rl")
-        mm(T.pk[:, 0:256], T.ID64[:], T.sg[:], False, False, ["ID64", "sg"], [("pk", 0, 256)])
-        names(3, True)
-        if t == 0:
-            constants3()
-        killed_names(t, 0)
-        killed_names(t, 1)
-        for b in range(4):
-            load_s(b)
-        scan(T.R[:], T.RST[:], T.pk[:, 0:256], 0.0, ALU.max, ALU.min, ["RST", ("pk", 0, 256)], ["R"])
-        killed_names(t, 2)
+        phage_forms(t)
+        mm(T.pk[:, 0:256], T.ID[:], T.CD[:], ("key", t), ["ID", "CD"], "pk", 256)
+        mm(T.pk[:, 0:256], T.ID[:], T.JR[:], ("key", t), ["ID", "JR"], "pk", 256)
+        act(T.pa[:, 1], T.Pf[:], AF.Copy, ["Pf"], ["pa"], 256)
+        for h in range(2):
+            for e in range(4 * h, 4 * h + 4):
+                ygather(YQ[t][e], e)
+            for c in (2 * h + 1, 2 * h):
+                names(t, c, first(t, 2 * c) + first(t, 2 * c + 1))
+            shifted(t, h)
+            killed_names(t, h)
+        act(T.sg[:], T.ps[:, 0:256], AF.Sign, ["ps"], ["sg"], 256, bias=-0.5 * U)
+        mm(T.pk[:, 0:256], T.ID64[:], T.sg[:], ("key", t), ["ID64", "sg"], "pk", 256)
+        scan(T.R[:], T.RST[:], T.pk[:, 0:256], 0.0, ALU.max, ALU.min, ["RST", "pk"], ["R"], 256)
         r = T.R[:, 15::16]
-        for out, sh, mk in (("u2", 11, 2), ("zm", 17, 3), ("kk", 13, 15)):
-            ts(m(out), r, sh, ALU.arith_shift_right, ["R"], [out], mk, ALU.bitwise_and)
-        ts(m("kl"), r, -112.0 * U, ALU.is_lt, ["R"], ["kl"], 256.0, ALU.mult)
-        ts(m("plt"), r, T.thr[:, 0:1], ALU.is_lt, ["R", "thr"], ["plt"], 256.0, ALU.mult)
-        q2("w", "u2", "CW", ALU.add, 32)
+        for i, (at, sh, mk) in enumerate(((1, 11, 2), (32, 17, 3), (33, 13, 15))):
+            ts(T.zi[:, at:at + 31:2], r, sh, ALU.arith_shift_right, ["R"], [("zi", i, i + 1)], mk, ALU.bitwise_and)
         ts(m("nm"), r, 4095, ALU.bitwise_and, ["R"], ["nm"])
-        q2("pr", "plt", "kl", ALU.subtract)
-        q2("h2", "w", "z1", ALU.mult)
-        q1("t16", "nm", -2048.0, ALU.add, 1.0 / 16, ALU.mult)
-        q1("un", "pr", -16.0, ALU.mult, 4096.0, ALU.add)
-        qc("offY", "nm")
-        q2("h3", "h2", "kk", ALU.add)
-        q2("t32", "t16", "pr", ALU.add)
+        ts(m("kl"), r, -112.0 * U, ALU.is_lt, ["R"], ["kl"], 256.0, ALU.mult)
+        ts(m("far"), r, T.thr[:, 0:1], ALU.is_ge, ["R", "thr"], ["far"], 256.0, ALU.mult)
+        q2("np", "far", "kl", ALU.add)
+        q1("pr", "np", -1.0, ALU.mult, 256.0, ALU.add)
+        tt(T.zf[:], T.zi[:], T.CW[:], ALU.add, ["zi", "CW"], ["zf"])
+        scan(T.zs[:], T.zf[:, 0:32], T.zf[:, 32:64], 0.0, ALU.mult, ALU.add, ["zf"], ["zs"], 32)
+        ts(m("fi"), T.zs[:, 1::2], 15, ALU.bitwise_and, ["zs"], ["fi"])
+        q1("un", "np", 16.0, ALU.mult)
         tt(T.C16[:, 16:32], m("un"), T.C16[:, 0:16], ALU.max, ["un", ("C16", 0, 16)], [("C16", 16, 32)])
-        q2("oP", "kl", "CB", ALU.add, 32)
-        q1("fi", "h3", 15, ALU.bitwise_and)
-        q2("w1", "nm", "CP", ALU.add, 16, 16 * t)
-        q1("u8", "pr", -1.0 / 2048, ALU.mult, 1.0 / 8, ALU.add)
-        q2("ko", "kk", "C16", ALU.add, 32)
-        q2("fa", "fi", "pr", ALU.mult)
-        q2("w1p", "w1", "pr", ALU.mult)
-        tt(T.RC[:, 15::16], m("u8"), T.CV[:], ALU.add, ["u8", "CV"], ["RC"])
-        qc("offK", "ko", 32)
-        q2("oN", "oN", "fa", ALU.add)
-        step = (1, 4, 16)[t]
-        for i, src in enumerate(("t16", "pr")):
-            for q in range(16):
-                a = (4 * q, 16 * (q % 4) + q // 4, q)[t]
-                mm(T.pb[:, 0:4, a:a + 3 * step + 1:step], T.SELT[:, q, :], m(src), i + q == 0, i + q == 16, ["SELT", src], [("pb", 0, 256)])
-        act(T.yv[:], XW.indirect(m("offY")), AF.Copy, [XT, "offY"], ["yv"])
-        act(T.sn[:], T.s[:].indirect(m("offF")), AF.Copy, ["s", "offF"], ["sn"])
-        cp(T.df[:], T.d[:].indirect(m("offF")), ["d", "offF"], ["df"])
-        for i, src in enumerate(("sn", "df")):
-            mm(T.pa[:, 0], T.ID[:], T[src][:], i == 0, i == 1, ["ID", src], [("pa", 0, 256)])
-        qc("offP", "oP", 32)
-        act(T.ak[:], T.d[:].indirect(m("offK")), AF.Abs, ["d", "offK"], ["ak"])
+        tt(m("ko"), T.zi[:, 33::2], T.C16[:, 0:16], ALU.add, [("zi", 2, 3), ("C16", 0, 16)], ["ko"])
+        q2("fo", "fi", "C16", ALU.add, 16, 16)
+        qc("offK", "ko")
         for rl in range(4):
-            act(T.xs[:, rl::4], T.pa[:, 0, :, rl, :], AF.Copy, [("pa", 0, 256)], [("xs", rl, rl + 1)])
-        compare(range(16))
-        ts(T.po[:], T[pw][:].indirect(m("offP")), 4095, ALU.bitwise_and, [pw, "offP"], ["po"])
-        if not last:
-            send(T.po[:], "po", T["PW%d" % (t + 1)][:, 0:256], prv, "p%d" % (t + 1), None)
-        for b in range(4):
-            minus_n(b)
-        act(T.pa[:, 1], T.yv[:], AF.Sign, ["yv"], [("pa", 256, 512)], scale=-1.0, bias=127.5)
-        size(0)
-        size(1)
-        load_s(4)
-        minus_n(4)
-        size(2)
-        esum(0)
-        size(3)
-        load_s(5)
-        minus_n(5)
-        act(T.a1[:], T.PS[:].indirect(m("offN")), AF.Copy, ["PS", "offN"], ["a1"])
-        esum(1)
-        scan(T.FE[:], T.RSD[:], T.NE[:], 0.0, ALU.add, ALU.min, ["RSD", "NE"], ["FE"])
-        ts(T.nr[:], T.ak[:], 32.5, ALU.is_lt, ["ak"], ["nr"], 128.0, ALU.mult)
-        tt(m("w2"), T.FE[:, 63::64], m("w1p"), ALU.add, ["FE", "w1p"], ["w2"])
-        tt(T.e2[:], T.nr[:], T.pa[:, 1], ALU.mult, ["nr", ("pa", 256, 512)], ["e2"])
-        q2("w3", "w2", "DM", ALU.max)
-        q1("offX", "w3", 1.0 / 256, ALU.mult)
-        size(4)
-        near(0)
-        load_s(6)
-        minus_n(6)
-        size(5)
-        load_s(7)
-        minus_n(7)
-        table_writes()
+            r4 = ("offF", 4 * rl, 4 * rl + 4)
+            cp(m("offF", 4, 4 * rl), T.sf[:, WHERE["fo"][1] + rl:WHERE["fo"][1] + 16:4], ["fo"], [r4])
+            out, a = T.xs[:, rl::4], T.yg[:].indirect(m("offF", 4, 4 * rl))
+            if rl % 2:
+                cp(out, a, ["yg", r4], [("xs", rl, rl + 1)], gath(64))
+            else:
+                act(out, a, AF.Copy, ["yg", r4], [("xs", rl, rl + 1)], gath(64))
+        q2("oP", "kl", "CB", ALU.add, 32)
+        q2("fa", "fi", "pr", ALU.mult)
+        q2("oN", "oN", "fa", ALU.add)
+        qc("offP", "oP")
+        qc("offN", "oN")
+        ts(T.po[:], T[pw][:].indirect(m("offP")), 4095, ALU.bitwise_and, [pw, "offP"], ["po"], c=gath(256))
         if last:
-            dma("y", [(T.yx[:], XW, [], [XT])])
-        size(6)
-        esum(2)
-        size(7)
-        esum(3)
-        near(1)
-        for part in range(4):
-            tail(t, 0, part)
-        if last:
-            cp(T.pout[:], T.po[:], ["po"], ["pout"])
-            dma("y", [(T.yp[:], T.pout[:], [], ["pout"])])
+            cp(T.pout[:], T.po[:], ["po"], ["pout"], 256)
+            dma([(T.yp[:], T.pout[:], [], ["pout"])], 128)
         else:
-            phage_forms(t + 1)
-            allowance(t, 0)
-        tail(t, 1, 0)
-        if not last:
-            phage_turn()
-        for part in range(1, 4):
-            tail(t, 1, part)
+            send(T.po[:], "po", T["PW%d" % (t + 1)][:, 0:256], ("PW%d" % (t + 1), 0, 256), prv, "p%d" % (t + 1))
+        act(T.a1[:], T.PS[:].indirect(m("offN")), AF.Copy, ["PS", "offN"], ["a1"], gath(256))
+        q1("nq", "nm", -2048.0, ALU.add, 1.0 / 16, ALU.mult)
+        q2("t16", "nq", "np", ALU.add)
+        qc("t32", "t16")
+        step = (1, 4, 16)[t]
+        at = [(4 * q, 16 * (q % 4) + q // 4, q)[t] for q in range(16)]
+        mms([(T.pb[:, 0:4, at[q]:at[q] + 3 * step + 1:step], T.SELT[:, q, :], m("t16")) for q in range(16)], ("spread", t), ["SELT", "t16"], "pb")
+        q2("w1", "nm", "CP", ALU.add, 16, 16 * t)
+        q2("w1p", "w1", "pr", ALU.mult)
+        for a, b in ((8, 16), (0, 8)):
+            for i in range(a, b):
+                ts(T.NE[:, 64 * i:64 * i + 64], T.pb[:, i // 4, :], m("t32", 1, i), ALU.not_equal, ["pb", "t32"], [("NE", i, i + 1)], 2.0 ** 28, ALU.mult)
+            scan(T.FE[:, 64 * a:64 * b], T.RSD[:, 64 * a:64 * b], T.NE[:, 64 * a:64 * b], 0.0, ALU.add, ALU.min, ["RSD", ("NE", a, b)], [("FE", a, b)], 256)
+            tt(m("w2", 8, a), T.FE[:, 64 * a + 63:64 * b:64], m("w1p", 8, a), ALU.add, [("FE", a, b), "w1p"], [("w2", a, b)])
+            tt(m("w3", 8, a), m("w2", 8, a), T.DM[:, a:b], ALU.max, [("w2", a, b), "DM"], [("w3", a, b)])
+            ts(m("offX", 8, a), m("w3", 8, a), 1.0 / 256, ALU.mult, [("w3", a, b)], [("offX", a, b)])
+        act(T.yv[:], T.yg[:].indirect(m("offK")), AF.Copy, ["yg", "offK"], ["yv"], gath(256))
+        act(T.ak[:], T.d[:].indirect(m("offK")), AF.Abs, ["d", "offK"], ["ak"], gath(256))
+        act(T.pk[:, 0:256], T.yv[:], AF.Sign, ["yv"], ["pk"], 256, scale=-1.0, bias=127.5)
+        ts(T.nr[:], T.ak[:], 32.5, ALU.is_lt, ["ak"], ["nr"], 128.0, ALU.mult, c=128)
+        tt(T.e2[:], T.nr[:], T.pk[:, 0:256], ALU.mult, ["nr", "pk"], ["e2"], 256)
+        for c in (3, 2, 1, 0):
+            tt(T.X[:].indirect(m("offX", 4, 4 * c)), T.yv[:, 64 * c:64 * c + 64], T.e2[:, 64 * c:64 * c + 64], ALU.add,
+               ["yv", "e2", ("offX", 4 * c, 4 * c + 4)], ["X"], -60 - 64 * SCATTER)
+        if last:
+            dma([(T.yx[:], XW, [], [XT])], 1024)
+        else:
+            allowance(t)
+        q1("u8", "np", 1.0 / 2048, ALU.mult)
+        tt(T.RC[:, 15::16], m("u8"), T.CV[:], ALU.add, ["u8", "CV"], ["RC"])
+        for h in range(2):
+            for b in range(4 * h, 4 * h + 4):
+                second(t, b)
+            tail(t, h)
+
+    if not ORDER:
+        ORDER.extend(issue_order(calls))
+    size = {}
+    for c in calls:
+        size[c["group"]] = size.get(c["group"], 0) + 1
+    seen = {}
+    told = {}
+    total = {}
+    waited = {}
+    for j in ORDER:
+        c = calls[j]
+        q = c["q"]
+        need = {}
+        for i, how in c["pre"].items():
+            if how != "order":
+                sem = "q" + calls[i]["q"] if how == "done" else how
+                need[sem] = max(need.get(sem, 0), told[i][sem])
+        for sem in sorted(need):
+            if waited.get((q, sem), 0) < need[sem]:
+                waited[(q, sem)] = need[sem]
+                eng[q].wait_ge(T.sem[sem], need[sem])
+        if c["own"]:
+            sem = "q" + q
+            if q == "t":
+                seen[c["group"]] = seen.get(c["group"], 0) + 1
+                total[sem] = total.get(sem, 0) + c["emit"](seen[c["group"]] == 1, seen[c["group"]] == size[c["group"]])
+            else:
+                c["emit"]().then_inc(T.sem[sem], 1)
+                total[sem] = total.get(sem, 0) + 1
+            told[j] = {sem: total[sem]}
+        else:
+            told[j] = c["emit"]()
+            total.update(told[j])
     for sem in sorted(total):
         if waited.get(("g", sem), 0) < total[sem]:
             g.wait_ge(T.sem[sem], total[sem])

@@ -10,57 +10,60 @@ _I = "int32"
 _U = "uint16"
 SCRATCH = {
     "X": ("sbuf", [128, 4160], _B),
-    "yg": ("sbuf", [128, 4112], _B), "d": ("sbuf", [128, 4096], _B), "s": ("sbuf", [128, 4096], _B), "rl": ("sbuf", [128, 4096], _B),
-    "ab": ("sbuf", [128, 256, 16], _B),
+    "yg": ("sbuf", [128, 4096], _B), "d": ("sbuf", [128, 4096], _B), "s": ("sbuf", [128, 4096], _B), "rl": ("sbuf", [128, 4096], _B),
+    "df": ("sbuf", [128, 4096], _B), "ab": ("sbuf", [128, 256, 16], _B),
     "KS": ("sbuf", [128, 2 * KW], _F), "PS": ("sbuf", [128, 4352], _F),
     "kd": ("dram", [2, 8, 33, 128], _F),
-    "k15": ("sbuf", [128, 256], _F), "kin": ("sbuf", [128, 256], _I),
-    "ku": ("sbuf", [128, 256], _U), "kp": ("sbuf", [128, 256], _F), "a1": ("sbuf", [128, 256], _F),
+    "kin": ("sbuf", [128, 256], _I), "kp": ("sbuf", [128, 256], _F), "ku": ("sbuf", [128, 256], _U), "a1": ("sbuf", [128, 256], _F),
     "pu": ("sbuf", [128, 256], _U), "Pf": ("sbuf", [128, 256], _F), "po": ("sbuf", [128, 256], _I), "pout": ("sbuf", [128, 256], _F),
     "Pm": ("sbuf", [128, 2, 4, 2, 16], _H), "PT": ("sbuf", [128, 2, 4, 2, 16], _H),
     "t1": ("sbuf", [128, 256], _I), "t2": ("sbuf", [128, 256], _I),
-    "pid": ("sbuf", [128, 8], _I), "col": ("sbuf", [128, 24], _F), "rowi": ("sbuf", [128, 128], _F), "rowg": ("sbuf", [128, 128], _F),
-    "rowq": ("sbuf", [128, 128], _B), "r16": ("sbuf", [128, 16], _F), "OH": ("sbuf", [128, 16], _F),
-    "SEL": ("sbuf", [128, 16, 128], _B), "SELN": ("sbuf", [128, 16, 128], _B),
-    "SELT": ("sbuf", [128, 16, 128], _H), "PERM": ("sbuf", [128, 4, 128], _H), "BLK": ("sbuf", [128, 128], _H),
-    "ID": ("sbuf", [128, 128], _B), "IDN": ("sbuf", [128, 128], _B), "ID64": ("sbuf", [128, 128], _B),
-    "IDF": ("sbuf", [128, 128], _F), "S15": ("sbuf", [128, 128], _F),
-    "JR": ("sbuf", [128, 256], _B), "CD": ("sbuf", [128, 256], _B),
+    "pid": ("sbuf", [128, 8], _I), "col": ("sbuf", [128, 24], _F), "rowi": ("sbuf", [128, 160], _F), "rowg": ("sbuf", [128, 128], _F),
+    "r16": ("sbuf", [128, 16], _F), "OH": ("sbuf", [128, 16], _F),
+    "SEL": ("sbuf", [128, 144], _B), "SELT": ("sbuf", [128, 16, 128], _B), "PERM": ("sbuf", [128, 2, 160], _H), "BLK": ("sbuf", [128, 128], _B),
+    "ID": ("sbuf", [128, 128], _B), "IDN": ("sbuf", [128, 128], _B), "ID64": ("sbuf", [128, 128], _B), "IDH": ("sbuf", [128, 128], _B),
+    "JR": ("sbuf", [128, 256], _B), "TWO": ("sbuf", [128, 128], _B),
     "RST": ("sbuf", [128, 256], _F), "RC": ("sbuf", [128, 256], _F), "RSD": ("sbuf", [128, 1024], _B),
-    "C16": ("sbuf", [128, 32], _F), "CB": ("sbuf", [128, 32], _F), "CV": ("sbuf", [128, 16], _F), "DM": ("sbuf", [128, 16], _F),
-    "CW": ("sbuf", [128, 64], _F), "zi": ("sbuf", [128, 64], _I), "zf": ("sbuf", [128, 64], _F), "zs": ("sbuf", [128, 32], _I), "CP": ("sbuf", [128, 48], _F),
-    "R": ("sbuf", [128, 256], _I), "sg": ("sbuf", [128, 256], _B),
+    "C16": ("sbuf", [128, 16], _F), "CB": ("sbuf", [128, 16], _F), "CV": ("sbuf", [128, 16], _F), "DM": ("sbuf", [128, 16], _F),
+    "CQ": ("sbuf", [128, 16], _F), "CW": ("sbuf", [128, 64], _F), "CP": ("sbuf", [128, 48], _F),
+    "R": ("sbuf", [128, 256], _I), "sg": ("sbuf", [128, 256], _B), "us": ("sbuf", [128, 256], _H),
+    "zi": ("sbuf", [128, 64], _I), "zf": ("sbuf", [128, 64], _F), "zs": ("sbuf", [128, 32], _I),
     "sf": ("sbuf", [128, 320], _F), "si": ("sbuf", [128, 128], _I), "sh": ("sbuf", [128, 48], _H), "su": ("sbuf", [128, 128], _U),
     "kc": ("sbuf", [128, 4], _F), "kj": ("sbuf", [128, 16], _F), "Ai": ("sbuf", [128, 4], _I), "thr": ("sbuf", [128, 4], _F),
     "xs": ("sbuf", [128, 256], _B), "ns": ("sbuf", [128, 256], _B), "fs": ("sbuf", [128, 256], _F),
     "NE": ("sbuf", [128, 1024], _B), "FE": ("sbuf", [128, 1024], _B),
-    "ak": ("sbuf", [128, 256], _B), "yv": ("sbuf", [128, 256], _B), "nr": ("sbuf", [128, 256], _B), "e2": ("sbuf", [128, 256], _B),
-    "pk": ("psum", [128, 512], _F), "ps": ("psum", [128, 512], _F), "pa": ("psum", [128, 2, 4, 4, 16], _F), "pb": ("psum", [128, 8, 64], _F),
+    "ak": ("sbuf", [128, 256], _B), "yv": ("sbuf", [128, 256], _B), "sy": ("sbuf", [128, 256], _B),
+    "nr": ("sbuf", [128, 256], _B), "e2": ("sbuf", [128, 256], _B),
+    "pk": ("psum", [128, 512], _F), "ps": ("psum", [128, 512], _F), "pb": ("psum", [128, 8, 64], _F),
 }
 ROUNDS = 3
-MODE = ("vv", "vv", "ss", "ss", "vv", "vv", "ss", "ss")
-YQ = ("vsssvsss", "vsssvsss", "vsssvsss")
-BANKS = ("db0", "db1", "db2", "db3", "pa", "db0", "db1", "db2")
-for _c in range(4):
+YQ = ("vsssssvs", "vsssssss", "vsssssss")
+MODE = ("vvvvvvss", "vvvvvvss", "vvvvvvss")
+SIZE = ("ccssccss", "ccssccss", "ccssccss")
+SECOND = ("ttts", "ttts", "ttts")
+XQ = ("ssss",)
+BANKS = ("db0", "db1", "db2", "db3", "db4", "db0", "db1", "db2")
+for _c in range(5):
     SCRATCH["db%d" % _c] = ("psum", [128, 64, 8], _F)
 for _t in range(ROUNDS):
     SCRATCH["PW%d" % _t] = ("sbuf", [128, 512], _I)
     SCRATCH["kl%d" % _t] = ("sbuf", [128, 256], _U)
     SCRATCH["kf%d" % _t] = ("sbuf", [128, 256], _F)
-PSUM = ("pk", "ps", "pa", "pb", "db0", "db1", "db2", "db3")
+PSUM = ("pk", "ps", "pb", "db0", "db1", "db2", "db3", "db4")
 SEMAPHORES = (["qv", "qs", "qt", "qg"] + ["dm%d" % i for i in range(40)]
               + [a + b + str(t) for a in "rl" for b in ("p", "u0", "u1") for t in (1, 2)])
-SMALL = {"sf": ("ko", "fo", "oP", "oN", "far", "np", "nq", "fa", "t32", "w1", "w1p", "w2", "w3", "un", "u8"),
-         "si": ("nm", "fi"),
+SMALL = {"sf": ("ko", "oP", "oN", "far", "np", "nq", "f1", "fa", "t32", "w1", "w1p", "w2", "w3", "u8"),
+         "si": ("nm", "fo"),
          "sh": ("kl", "pr", "t16"),
-         "su": ("offK", "offF", "offP", "offN", "offX", "offV")}
+         "su": ("offK", "offP", "offF", "offN", "offX", "offV")}
 WHERE = {n: (b, 16 * i) for b in SMALL for i, n in enumerate(SMALL[b])}
 
 CYCLE, TCYCLE, GATHER, SCATTER = 0.00085, 0.00043, 1.56, 3.5
-PASSES = 400
-CASES = ({"compute": 1.0, "index": 1.0, "tensor": 1.0, "remote": 1.0, "local": 1.0, "wake": 0.2},
-         {"compute": 1.2, "index": 1.2, "tensor": 2.4, "remote": 1.2, "local": 1.2, "wake": 0.22},
-         {"compute": 1.3, "index": 1.6, "tensor": 1.8, "remote": 1.5, "local": 1.5, "wake": 0.25})
+PASSES = 100
+SWAPS = 8000
+CASES = ({"compute": 1.0, "index": 1.0, "tensor": 1.0, "remote": 1.0, "local": 1.0, "wake": 0.2, "all": 0.8},
+         {"compute": 1.1, "index": 1.1, "tensor": 2.2, "remote": 1.1, "local": 1.2, "wake": 0.22, "all": 1.4},
+         {"compute": 1.3, "index": 1.6, "tensor": 1.7, "remote": 1.4, "local": 1.5, "wake": 0.25, "all": 1.4})
 ORDER = []
 
 
@@ -78,18 +81,35 @@ def issue_order(calls):
                 fwd[i].append((j, gap))
                 bwd[j].append((i, gap + busy[j] - busy[i]))
         cases.append((busy, late, fwd, bwd))
+    queue = [c["q"] for c in calls]
 
-    def play(order, busy, late, fwd):
+    def play(order, case):
+        busy, late, fwd, _b = case
         can = [0.0] * n
+        by = [-1] * n
+        held = [False] * n
         free = {}
-        end = 0.0
+        end, j1 = 0.0, 0
         for j in order:
-            at = max(can[j], free.get(calls[j]["q"], 0.0))
-            free[calls[j]["q"]] = at + busy[j]
-            end = max(end, at + busy[j] + late[j])
+            at = can[j]
+            f = free.get(queue[j])
+            if f and f[0] > at:
+                at, by[j], held[j] = f[0], f[1], True
+            free[queue[j]] = (at + busy[j], j)
+            if at + busy[j] + late[j] > end:
+                end, j1 = at + busy[j] + late[j], j
             for k, gap in fwd[j]:
-                can[k] = max(can[k], at + gap)
-        return end
+                if at + gap > can[k]:
+                    can[k], by[k] = at + gap, j
+        path = []
+        while j1 >= 0:
+            if held[j1]:
+                path.append((j1, by[j1]))
+            j1 = by[j1]
+        return end, path
+
+    def score(order):
+        return sum(play(order, c)[0] / case["all"] for c, case in zip(cases, CASES))
 
     def place(rank, busy, nxt, prev, can):
         left = [len(p) for p in prev]
@@ -100,7 +120,7 @@ def issue_order(calls):
             j = min(ready, key=lambda j: rank[j])
             ready.remove(j)
             at = can[j]
-            line = taken.setdefault(calls[j]["q"], [])
+            line = taken.setdefault(queue[j], [])
             i = len(line)
             while i and line[i - 1][1] > at:
                 i -= 1
@@ -122,9 +142,9 @@ def issue_order(calls):
         busy, late, fwd, bwd = cases[turn // 2 % len(cases)]
         start = place(rank, busy, fwd, bwd, [0.0] * n)
         order = sorted(range(n), key=lambda j: (start[j], j))
-        score = sum(play(order, c[0], c[1], c[2]) / case["compute"] for c, case in zip(cases, CASES))
-        if best is None or score < best[0]:
-            best = (score, order, start)
+        s = score(order)
+        if best is None or s < best[0]:
+            best = (s, order, start)
         if turn % 2:
             lo = max(best[2]) * (turn * 7717 % 997) / 997
             amp = (0.3, 0.8, 1.6)[turn // 2 % 7 % 3]
@@ -132,6 +152,41 @@ def issue_order(calls):
         else:
             back = place([-(start[j] + busy[j]) for j in range(n)], busy, bwd, fwd, list(late))
             rank = [-(back[j] + busy[j]) for j in range(n)]
+    now, order = best[0], best[1]
+    best = (now, order)
+    pre = [set(c["pre"]) for c in calls]
+    for turn in range(SWAPS):
+        path = play(order, cases[turn % len(cases)])[1]
+        pick = (turn * 7919 + 13) ** 2 % 1000003
+        j, p = path[pick % len(path)]
+        a, b, more = order.index(p), order.index(j), pick // 1000 % 3
+        if pick // 100 % 2:
+            while more and a > 0:
+                a -= 1
+                more -= queue[order[a]] == queue[j]
+            move, want = {j}, set(pre[j])
+            for x in reversed(order[a:b]):
+                if x in want:
+                    move.add(x)
+                    want |= pre[x]
+            ahead = move
+        else:
+            while more and b < n - 1:
+                b += 1
+                more -= queue[order[b]] == queue[j]
+            move = {p}
+            for x in order[a + 1:b + 1]:
+                if pre[x] & move:
+                    move.add(x)
+            ahead = set(order[a:b + 1]) - move
+        if p in ahead or j not in ahead:
+            continue
+        new = order[:a] + [x for x in order[a:b + 1] if x in ahead] + [x for x in order[a:b + 1] if x not in ahead] + order[b + 1:]
+        s = score(new)
+        if s <= now + 0.5 * (1 - turn / SWAPS) ** 2 * (pick % 97) / 97:
+            now, order = s, new
+            if s < best[0]:
+                best = (s, new)
     return best[1]
 
 
@@ -145,6 +200,7 @@ def rank_program(g, core, T, topo):
     log = {}
     banks = {}
     dmas = [0]
+    opened = {}
 
     def m(name, n=16, at=0):
         b, i = WHERE[name]
@@ -217,18 +273,17 @@ def rank_program(g, core, T, topo):
         else:
             vector(lambda: g.vector.tensor_scalar(out, a, s1, s2, o1, o2), reads, writes, c)
 
-    def q1(out, a, s1, o1, s2=None, o2=None, n=16):
-        ts(m(out, n), m(a, n), s1, o1, [(a, 0, n)], [(out, 0, n)], s2, o2)
+    def q1(out, a, s1, o1, s2=None, o2=None):
+        ts(m(out), m(a), s1, o1, [a], [out], s2, o2)
 
-    def q2(out, a, b, o, n=16, at=0):
-        bb = m(b, n) if b in WHERE else T[b][:, at:at + n]
-        tt(m(out, n), m(a, n), bb, o, [(a, 0, n), (b, at, at + n)], [(out, 0, n)])
+    def q2(out, a, b, o, at=0):
+        tt(m(out), m(a), m(b) if b in WHERE else T[b][:, at:at + 16], o, [a, b], [out])
 
     def cp(out, a, reads, writes, c=0):
         vector(lambda: g.vector.tensor_copy(out, a), reads, writes, c)
 
-    def qc(out, a, n=16):
-        cp(m(out, n), m(a, n), [(a, 0, n)], [(out, 0, n)])
+    def qc(out, a):
+        cp(m(out), m(a), [a], [out])
 
     def fill(name, x, ap=None, w=None, c=0):
         vector(lambda: g.vector.memset(T[name][:] if ap is None else ap, x), [], [w or name], c)
@@ -242,20 +297,25 @@ def rank_program(g, core, T, topo):
                 g.tensor.matmul(out, l, r, st and k == 0, sp and k == len(each) - 1).then_inc(T.sem.qt, 1)
             return len(each)
 
-        return call("t", emit, len(each) * max(64, c) * TCYCLE, reads, [bank], group=(bank, group), after=after, kind="tensor")
+        if group[0] == "key":
+            after = list(after) + opened.setdefault(group, [])
+        j = call("t", emit, len(each) * max(64, c) * TCYCLE, reads, [bank], group=(bank, group), after=after, kind="tensor")
+        if group[0] == "key" and not opened[group]:
+            opened[group].append(j)
+        return j
 
     def mm(out, l, r, group, reads, bank, c=64):
-        mms([(out, l, r)], group, reads, bank, c)
+        return mms([(out, l, r)], group, reads, bank, c)
 
     def scan(out, a, b, first, o1, o2, reads, writes, c):
         vector(lambda: g.vector.tensor_tensor_scan(out, a, b, first, o1, o2), reads, writes, c)
 
-    def iota(name, pat, base, mult=0, ap=None, w=None):
+    def iota(name, pat, base, mult=0, ap=None, w=None, after=()):
         n = 1
         for _s, k in pat:
             n *= k
         call("g", lambda: g.iota(T[name][:] if ap is None else ap, pat, base, mult, allow_small_or_imprecise_dtypes=True),
-             0.13 + 2 * n * CYCLE, [], [w or name])
+             0.13 + 2 * n * CYCLE, [], [w or name], after=after)
 
     def gath(n):
         return -70 - GATHER * n
@@ -271,19 +331,22 @@ def rank_program(g, core, T, topo):
     lists = dma([(T.PW0[:, 0:256], T.ph[:], [("PW0", 0, 256)], []), (T.kin[:], T.ka[:], ["kin"], [])], 128)
     dma([(XW, T.x0[:], [XT], [])], 800, [lists])
     iota("pid", [[0, 1]], 0, 1, T.pid[:, 0:1])
-    iota("rowi", [[1, 128]], 0)
+    iota("rowi", [[1, 160]], 0)
     iota("rowg", [[1, 8], [0, 16]], 0)
     iota("r16", [[1, 16]], 0)
-    iota("PS", [[0, 4352]], 0)
     iota("JR", [[0, 16], [8192, 16]], 4096)
-    iota("C16", [[1024, 4], [16, 4]], 0, 0, T.C16[:, 0:16], ("C16", 0, 16))
-    iota("CB", [[0, 2], [64, 4], [1, 4]], 0)
+    iota("C16", [[1024, 4], [16, 4]], 0)
+    iota("CB", [[64, 4], [1, 4]], 0)
     iota("CV", [[0, 2], [64, 2], [1, 4]], 4096 + 23 * 128)
     iota("DM", [[0, 4], [4096, 4]], 0)
-    iota("CW", [[1, 2], [0, 16], [-1, 2]], 0)
+    iota("CQ", [[-1024, 4], [0, 4]], 1)
+    iota("CW", [[0, 16], [-1, 2]], 0, 0, T.CW[:, 0:32], ("CW", 0, 1))
+    iota("CW", [[0, 16]], 1, 0, T.CW[:, 32::2], ("CW", 1, 2))
+    iota("CW", [[1024, 4], [0, 4]], 16, 0, T.CW[:, 33::2], ("CW", 2, 3))
     iota("zi", [[0, 64]], 0)
     for i in range(3):
         iota("CP", [[0, 4], [4 ** i, 4]], -63, 0, T.CP[:, 16 * i:16 * i + 16], ("CP", 16 * i, 16 * i + 16))
+    iota("PS", [[0, 4352]], 0, after=[j for j, c in enumerate(calls) if c["q"] == "g"])
     fill("RSD", -2.0 ** 21, c=512)
     fill("RSD", BIG, T.RSD[:, 0::64])
     dma([(T.KS[0::16, KW * h:KW * h + 2048], T.PS[1::16, 0:2048], [("KS", 4 * h, 4 * h + 1)], [("PS", 0, 2048)]) for h in range(2)]
@@ -292,37 +355,28 @@ def rank_program(g, core, T, topo):
     for i, sh, mk in ((1, 0, 15), (2, 4, 7), (3, 0, 3), (4, 2, 3), (5, 4, 1)):
         ts(pid(i), pid(0), sh, ALU.arith_shift_right, [("pid", 0, 1)], [("pid", i, i + 1)], mk, ALU.bitwise_and)
     cp(T.col[:, 0:6], T.pid[:, 0:6], [("pid", 0, 6)], [("col", 0, 6)])
-    for i, a, s1, s2 in ((6, 2, 16.0, 0.0), (8, 1, 64.0, 0.0), (9, 1, 4.0, 0.0), (10, 0, 1.0, -16.0), (11, 0, 1.0, 16.0),
+    for i, a, s1, s2 in ((6, 2, 16.0, 15.0), (8, 1, 64.0, 0.0), (9, 1, 4.0, 0.0), (11, 0, 1.0, 16.0),
                          (12, 5, -1.0, 1.0), (13, 5, 1.0, 0.0), (14, 3, 16.0, col(4)), (16, 1, 4.0, -4096.0), (17, 1, 256.0, 0.0)):
         ts(col(i), col(a), s1, ALU.mult, [("col", 0, 6)], [rc(i)], s2, ALU.add)
-    ts(col(15), col(1), 15.0, ALU.is_equal, [("col", 0, 6)], [rc(15)])
-    ts(T.ID[:], T.rowi[:], col(0), ALU.is_equal, ["rowi", rc(0)], ["ID"], c=128)
-    ts(T.IDF[:], T.rowi[:], col(0), ALU.is_equal, ["rowi", rc(0)], ["IDF"], c=128)
-    ts(T.S15[:], T.rowg[:], col(2), ALU.is_equal, ["rowg", rc(2), rc(15)], ["S15"], col(15), ALU.mult, c=128)
-    fill("CD", -992.0 * U, c=128)
+    ts(T.ID[:], T.rowi[:, 0:128], col(0), ALU.is_equal, ["rowi", rc(0)], ["ID"], c=128)
+    fill("JR", -992.0 * U, T.JR[32:64, :], c=128)
+    fill("TWO", 1.0 / 32)
     fill("thr", 48.0 * U)
     cp(T.kl0[:], T.kin[:], ["kin"], ["kl0"], 256)
-    ts(T.ID64[:], T.ID[:], U / 64, ALU.mult, ["ID"], ["ID64"])
-    ts(T.IDN[:], T.ID[:], -1.0, ALU.mult, ["ID"], ["IDN"])
+    for name, w in (("ID64", U / 64), ("IDN", -1.0), ("IDH", U / 4)):
+        act(T[name][:], T.ID[:], AF.Copy, ["ID"], [name], 128, scale=w)
     for h in range(2):
-        for g2 in range(2):
-            i = (10, 0, 11)[g2 - h + 1]
-            ts(T.PERM[:, 2 * h + g2, :], T.rowi[:], col(i), ALU.is_equal, ["rowi", rc(i), rc(12 + h)], [("PERM", 2 * h + g2, 2 * h + g2 + 1)],
-               col(12 + h), ALU.mult, c=128)
-    fill("RST", -BIG, c=256)
+        ts(T.PERM[:, h, :], T.rowi[:], col(11), ALU.is_equal, ["rowi", rc(11), rc(12 + h)], [("PERM", h, h + 1)], col(12 + h), ALU.mult, c=160)
+        for name, x in (("RST", -BIG), ("RC", -1.0 / 8)):
+            act(T[name][:, 128 * h:128 * h + 128], T.rowg[:], AF.Identity, ["rowg"], [(name, 8 + h, 9 + h)], 128, scale=0.0, bias=x)
     fill("RST", BIG, T.RST[:, 0::16])
-    fill("RC", -1.0 / 8, c=256)
-    fill("yg", 1024.0, T.yg[:, 4096:4112], ("yg", 8, 9))
     fill("X", 0.0, T.X[:, 0:64], ("X", 0, 64))
     ts(T.BLK[:], T.rowg[:], col(2), ALU.is_equal, ["rowg", rc(2)], ["BLK"], c=128)
-    ts(T.rowq[:], T.rowi[:], col(6), ALU.subtract, ["rowi", rc(6)], ["rowq"], c=128)
+    ts(T.SEL[:], T.rowi[:, 0:144], col(6), ALU.is_equal, ["rowi", rc(6)], ["SEL"], U, ALU.mult, c=144)
     ts(T.OH[:], T.r16[:], col(1), ALU.is_equal, ["r16", rc(1)], ["OH"])
     for q in range(16):
-        ts(T.SELN[:, q, :], T.rowq[:], float(q), ALU.is_equal, ["rowq"], [("SELN", q, q + 1)], -U, ALU.mult)
-        ts(T.SELT[:, q, :], T.BLK[:], T.OH[:, q:q + 1], ALU.mult, ["BLK", "OH"], [("SELT", q, q + 1)])
-    act(T.SEL[:], T.SELN[:], AF.Copy, ["SELN"], ["SEL"], 2048, scale=-1.0)
-    ts(T.C16[:, 0:16], T.C16[:, 0:16], col(8), ALU.add, [("C16", 0, 16), rc(8)], [("C16", 0, 16)])
-    for name, c in (("CB", 9), ("DM", 17)):
+        act(T.SELT[:, q, :], T.BLK[:], AF.Copy, ["BLK", "OH"], [("SELT", q, q + 1)], 128, scale=T.OH[:, q:q + 1])
+    for name, c in (("C16", 8), ("CB", 9), ("DM", 17)):
         ts(T[name][:], T[name][:], col(c), ALU.add, [name, rc(c)], [name])
     ts(T.CV[:], T.CV[:], 1.0 / 1024, ALU.mult, ["CV"], ["CV"])
     for i, c in enumerate((9, 14, 1)):
@@ -342,7 +396,7 @@ def rank_program(g, core, T, topo):
             g.remote_dma(land, src, T.sem["r" + tag], T.sem["l" + tag], pid_, rid, sum(1 << e for e in es))
             return {"l" + tag: len(es), "r" + tag: len(topo.engines(other, core))}
 
-        call("g", emit, 0.5, [r], [w], 4.6 if tag == "p1" else 2.6, told=("l" + tag, "r" + tag), kind="remote")
+        call("g", emit, 0.5, [r], [w], 5.6 if tag == "p1" else 2.6, told=("l" + tag, "r" + tag), kind="remote")
 
     def phage_forms(t):
         pw = "PW%d" % t
@@ -352,11 +406,11 @@ def rank_program(g, core, T, topo):
         for rl in range(4):
             ts(T.Pm[:, :, rl], T.pu[:, rl::4], -2048.0, ALU.add, ["pu"], [("Pm", rl, rl + 1)])
         vector(lambda: g.vector.transpose(T.PT[:], T.Pm[:]), ["Pm"], ["PT"], 128)
+        act(T.pb[:, 4:8], T.Pf[:], AF.Copy, ["Pf"], ["pb"], 256)
 
     def shifted(t, h):
         kf = "kf%d" % t
         a, b = 128 * h, 128 * h + 128
-        cp(T[kf][:, a:b], T["kl%d" % t][:, a:b], [("kl%d" % t, a, b)], [(kf, a, b)], 128)
         o = 40 * h
         dma([(T.kd[h, :, 1:17, :], T[kf][:, a:b], [("kd", o + 1, o + 17)], [(kf, a, b)])]
             + [(T.kd[h, :, i, :], T[kf][15::16, a:b], [("kd", o + i, o + i + 1)], [(kf, a, b)]) for i in range(17, 32)], 128)
@@ -365,79 +419,85 @@ def rank_program(g, core, T, topo):
             + [(T.KS[:, KW * h + 2048:KW * h + 2176], T.kd[h, :, 0:16, :], w, [("kd", o, o + 33)]),
                (T.KS[:, KW * h + 2176:KW * h + 2304], T[kf][:, a:b], w, [(kf, a, b)])], 1152)
 
-    def ygather(q, e):
-        out, a = T.yg[:, 512 * e:512 * e + 512], XW.indirect(T.pu[:, 32 * e:32 * e + 32])
+    def gather(q, out, a, reads, writes, n):
         if q == "v":
-            cp(out, a, [XT, "pu"], [("yg", e, e + 1)], gath(512))
+            cp(out, a, reads, writes, gath(n))
         else:
-            act(out, a, AF.Copy, [XT, "pu"], [("yg", e, e + 1)], gath(512))
+            act(out, a, AF.Copy, reads, writes, gath(n))
 
-    def lanes(bank, base, sel, src, e, group):
+    def lanes(bank, base, src, e, group):
         c = e // 2
         each = []
         for q in range(8 * (e % 2), 8 * (e % 2) + 8):
             a = 1024 * c + 64 * q
             rhs = T.ab[:, a // 16:a // 16 + 4, :] if src == "ab" else T[src][:, a:a + 64]
-            each.append((T[bank][:, base + 64 * c:base + 64 * c + 64], T[sel][:, q, :], rhs))
-        return [mms(each, group, [sel, ("ab", 2 * c, 2 * c + 2) if src == "ab" else (src, e, e + 1)], bank)]
+            each.append((T[bank][:, base + 64 * c:base + 64 * c + 64], T.SEL[:, 15 - q:143 - q], rhs))
+        return mms(each, group, ["SEL", ("ab", 2 * c, 2 * c + 2) if src == "ab" else (src, e, e + 1)], bank)
 
     def first(t, e):
         kl, a, b, r = "kl%d" % t, 512 * e, 512 * e + 512, (e, e + 1)
         s = XW.indirect(T[kl][:, 32 * e:32 * e + 32])
-        if MODE[e][0] == "v":
+        if MODE[t][e] == "v":
             tt(T.d[:, a:b], s, T.yg[:, a:b], ALU.subtract, [XT, (kl, 32 * e, 32 * e + 32), ("yg",) + r], [("d",) + r], gath(512))
         else:
-            act(T.s[:, a:b], s, AF.Copy, [XT, (kl, 32 * e, 32 * e + 32)], [("s",) + r], gath(512))
+            gather("s", T.s[:, a:b], s, [XT, (kl, 32 * e, 32 * e + 32)], [("s",) + r], 512)
             tt(T.d[:, a:b], T.s[:, a:b], T.yg[:, a:b], ALU.subtract, [("s",) + r, ("yg",) + r], [("d",) + r], 512)
-        lanes("ps", 0, "SEL", "d", e, ("side", t))
-        if MODE[e][1] == "s":
+        lanes("ps", 0, "d", e, ("side", t, e // 2))
+        if SIZE[t][e] == "s":
             act(T.rl[:, a:b], T.d[:, a:b], AF.Abs, [("d",) + r], [("rl",) + r], 512)
-            return lanes("pk", 0, "SEL", "rl", e, ("key", t))
-        ts(T.rl[:, a:b], T.d[:, a:b], 0.0, ALU.max, [("d",) + r], [("rl",) + r], 2.0, ALU.mult, c=256)
-        return lanes("pk", 0, "SELN", "d", e, ("key", t)) + lanes("pk", 0, "SEL", "rl", e, ("key", t))
+        else:
+            ts(T.rl[:, a:b], T.d[:, a:b], 0.0, ALU.max, [("d",) + r], [("rl",) + r], 2.0, ALU.mult, c=256)
+        return lanes("pk", 0, "rl", e, ("key", t))
 
     def names(t, c, sums):
-        mms([(T.pk[:, 64 * c:64 * c + 64], T.PERM[:, 2 * (c % 2) + g2, :], T.PT[:, c // 2, :, g2, :]) for g2 in range(2)],
+        h = c % 2
+        mms([(T.pk[:, 64 * c:64 * c + 64], T.PERM[:, h, 16 * (1 + h - g2):16 * (9 + h - g2)], T.PT[:, c // 2, :, g2, :]) for g2 in range(2)],
             ("key", t), ["PERM", "PT"], "pk", after=sums)
 
     def killed_names(t, h):
         pw, kf = "PW%d" % t, "kf%d" % t
         a, b = 128 * h, 128 * h + 128
-        p = T.pa[:, 1, 2 * h:2 * h + 2]
-        tt(T.t1[:, a:b], T[kf][:, a:b], p, ALU.mult, [(kf, a, b), "pa"], [("t1", a, b)], 128)
+        p, r = T.pb[:, 4 + 2 * h:6 + 2 * h], ("pb", 256 + a, 256 + b)
+        tt(T.t1[:, a:b], T[kf][:, a:b], p, ALU.mult, [(kf, a, b), r], [("t1", a, b)], 128)
         ts(T.t2[:, a:b], T.t1[:, a:b], 5, ALU.arith_shift_right, [("t1", a, b)], [("t2", a, b)], c=128)
-        tt(T[pw][:, 256 + a:256 + b], T.t2[:, a:b], p, ALU.add, [("t2", a, b), "pa"], [(pw, 256 + a, 256 + b)], 128)
+        tt(T[pw][:, 256 + a:256 + b], T.t2[:, a:b], p, ALU.add, [("t2", a, b), r], [(pw, 256 + a, 256 + b)], 128)
 
     def second(t, b):
         c, hj, db = b // 2, b % 2, BANKS[b]
-        out = [T.pa[:, :, :, :, jj::8] if db == "pa" else T[db][:, :, jj] for jj in range(8)]
-        for src in ("s",) if MODE[2 * c][0] == "s" else ("d", "yg"):
-            mms([(out[jj], T.ID[:], T[src][:, 1024 * c + 8 * hj + jj:1024 * c + 1024:16]) for jj in range(8)], ("second", t, b),
-                ["ID", (src, 2 * c, 2 * c + 2)], db)
-        mms([(out[jj], T.IDN[:], T.xs[:, 64 * c:64 * c + 64]) for jj in range(8)], ("second", t, b), ["IDN", "xs"], db)
-        act(T.ab[:, 64 * c:64 * c + 64, 8 * hj:8 * hj + 8], T[db][:], AF.Abs, [db], [("ab", b, b + 1)], 512)
+        a, r = 1024 * c + 8 * hj, (2 * c, 2 * c + 2)
+        out = T.ab[:, 64 * c:64 * c + 64, 8 * hj:8 * hj + 8]
+        if SECOND[t][c] == "s":
+            if hj == 0:
+                for j in range(16):
+                    tt(T.df[:, a + j:a + 1024:16], T.s[:, a + j:a + 1024:16], T.xs[:, 64 * c:64 * c + 64], ALU.subtract,
+                       [("s",) + r, "xs"], [("df", 16 * c + j, 16 * c + j + 1)])
+                act(T.ab[:, 64 * c:64 * c + 64, :], T.df[:, a:a + 1024], AF.Abs, [("df", 16 * c, 16 * c + 16)], [("ab",) + r], 1024)
+            return
+        for src in ("s",) if MODE[t][2 * c] == "s" else ("d", "yg"):
+            mms([(T[db][:, :, jj], T.ID[:], T[src][:, a + jj:1024 * c + 1024:16]) for jj in range(8)], ("second", t, b), ["ID", (src,) + r], db)
+        mms([(T[db][:, :, jj], T.IDN[:], T.xs[:, 64 * c:64 * c + 64]) for jj in range(8)], ("second", t, b), ["IDN", "xs"], db)
+        act(out, T[db][:], AF.Abs, [db], [("ab", b, b + 1)], 512)
 
     def tail(t, h):
-        a, b = 128 * h, 128 * h + 128
+        a, b, i, j = 128 * h, 128 * h + 128, 8 * h, 8 * h + 8
         bank = ("pk", "ps")[h]
         for e in range(4 * h, 4 * h + 4):
-            lanes(bank, 256 - 128 * h, "SEL", "ab", e, ("near", t))
-        act(T.ns[:, a:b], T[bank][:, 256:384], AF.Sign, [bank], [("ns", h, h + 1)], 128, bias=-959.5 * U)
-        ov = ("offV", 8 * h, 8 * h + 8)
-        scan(T.fs[:, a:b], T.ns[:, a:b], T.RC[:, a:b], BIG, ALU.min, ALU.add, ["RC", ("ns", h, h + 1)], [("fs", h, h + 1)], 128)
-        ts(m("offV", 8, 8 * h), T.fs[:, a + 15:b:16], 1024.0, ALU.mult, [("fs", h, h + 1), rc(16)], [ov], col(16), ALU.add)
-        tt(T.kp[:, a:b], T.KS[:, KW * h:KW * h + KW].indirect(m("offV", 8, 8 * h)), T.a1[:, a:b], ALU.add,
-           [("KS", 4 * h, 4 * h + 4), ov, "a1"], [("kp", a, b)], gath(128))
+            lanes(bank, 256 - 128 * h, "ab", e, ("near", t))
+        act(T.ns[:, a:b], T[bank][:, 256:384], AF.Sign, [bank], [("ns", a, b)], 128, bias=-959.5 * U)
+        scan(T.fs[:, a:b], T.ns[:, a:b], T.RC[:, a:b], BIG, ALU.min, ALU.add, ["RC", ("ns", a, b)], [("fs", a, b)], 128)
+        ts(m("offV", 8, i), T.fs[:, a + 15:b:16], 1024.0, ALU.mult, [("fs", a, b), rc(16)], [("offV", i, j)], col(16), ALU.add)
+        tt(T.kp[:, a:b], T.KS[:, KW * h:KW * h + KW].indirect(m("offV", 8, i)), T.a1[:, a:b], ALU.add,
+           [("KS", 4 * h, 4 * h + 4), ("offV", i, j), "a1"], [("kp", a, b)], gath(128))
         if t == ROUNDS - 1:
             dma([(T.yk[:, a:b], T.kp[:, a:b], [], [("kp", a, b)])], 64)
         else:
-            cp(T.ku[:, a:b], T.kp[:, a:b], [("kp", a, b)], [("ku", a, b)], 128)
             kl = "kl%d" % (t + 1)
+            cp(T.ku[:, a:b], T.kp[:, a:b], [("kp", a, b)], [("ku", a, b)], 128)
             send(T.ku[:, a:b], ("ku", a, b), T[kl][:, a:b], (kl, a, b), nxt, "u%d%d" % (h, t + 1))
 
     def allowance(t):
         mm(T.pb[:, 4, 0:16], T.BLK[:], m("kl"), ("kills", t), ["BLK", "kl"], "pb")
-        act(T.kj[:], T.pb[:, 4, 0:16], AF.Copy, ["pb"], ["kj", ("kc", t, t + 1)], 200, accum_out=T.kc[:, t:t + 1])
+        act(T.kj[:], T.pb[:, 4, 0:16], AF.Copy, ["pb"], ["kj", ("kc", t, t + 1)], 90, accum_out=T.kc[:, t:t + 1])
         ts(T.Ai[:, 0:1], T.kc[:, t:t + 1], T.kc[:, 0:1] if t else 0.0, ALU.add, ["kc"], [("Ai", 0, 1)], 1.0 / 256, ALU.mult)
         ts(T.Ai[:, 1:2], T.Ai[:, 0:1], 15, ALU.bitwise_and, [("Ai", 0, 1)], [("Ai", 1, 2)])
         ts(T.thr[:, 0:1], T.Ai[:, 1:2], 4.0 * U, ALU.mult, [("Ai", 1, 2)], ["thr"], 48.0 * U, ALU.add)
@@ -446,18 +506,23 @@ def rank_program(g, core, T, topo):
         last = t == ROUNDS - 1
         pw = "PW%d" % t
         phage_forms(t)
-        mm(T.pk[:, 0:256], T.ID[:], T.CD[:], ("key", t), ["ID", "CD"], "pk", 256)
-        mm(T.pk[:, 0:256], T.ID[:], T.JR[:], ("key", t), ["ID", "JR"], "pk", 256)
-        act(T.pa[:, 1], T.Pf[:], AF.Copy, ["Pf"], ["pa"], 256)
+        mm(T.pk[:, 0:256], T.TWO[0:64, :], T.JR[0:64, :], ("key", t), ["TWO", "JR"], "pk", 256)
         for h in range(2):
+            a, b, kl, kf = 128 * h, 128 * h + 128, "kl%d" % t, "kf%d" % t
+            cp(T[kf][:, a:b], T[kl][:, a:b], [(kl, a, b)], [(kf, a, b)], 128)
             for e in range(4 * h, 4 * h + 4):
-                ygather(YQ[t][e], e)
-            for c in (2 * h + 1, 2 * h):
-                names(t, c, first(t, 2 * c) + first(t, 2 * c + 1))
+                gather(YQ[t][e], T.yg[:, 512 * e:512 * e + 512], XW.indirect(T.pu[:, 32 * e:32 * e + 32]), [XT, "pu"], [("yg", e, e + 1)], 512)
+            for c in (2 * h, 2 * h + 1):
+                a, b = 64 * c, 64 * c + 64
+                sums = [first(t, 2 * c), first(t, 2 * c + 1)]
+                if SIZE[t][2 * c] == "c":
+                    ts(T.us[:, a:b], T.ps[:, a:b], -4.0 / U, ALU.mult, [("ps", a, b)], [("us", a, b)])
+                    sums.append(mm(T.pk[:, a:b], T.IDH[:], T.us[:, a:b], ("key", t), ["IDH", ("us", a, b)], "pk"))
+                act(T.sg[:, a:b], T.ps[:, a:b], AF.Sign, [("ps", a, b)], [("sg", a, b)], 64, bias=-0.5 * U)
+                mm(T.pk[:, a:b], T.ID64[:], T.sg[:, a:b], ("key", t), ["ID64", ("sg", a, b)], "pk")
+                names(t, c, sums)
             shifted(t, h)
             killed_names(t, h)
-        act(T.sg[:], T.ps[:, 0:256], AF.Sign, ["ps"], ["sg"], 256, bias=-0.5 * U)
-        mm(T.pk[:, 0:256], T.ID64[:], T.sg[:], ("key", t), ["ID64", "sg"], "pk", 256)
         scan(T.R[:], T.RST[:], T.pk[:, 0:256], 0.0, ALU.max, ALU.min, ["RST", "pk"], ["R"], 256)
         r = T.R[:, 15::16]
         for i, (at, sh, mk) in enumerate(((1, 11, 2), (32, 17, 3), (33, 13, 15))):
@@ -469,24 +534,17 @@ def rank_program(g, core, T, topo):
         q1("pr", "np", -1.0, ALU.mult, 256.0, ALU.add)
         tt(T.zf[:], T.zi[:], T.CW[:], ALU.add, ["zi", "CW"], ["zf"])
         scan(T.zs[:], T.zf[:, 0:32], T.zf[:, 32:64], 0.0, ALU.mult, ALU.add, ["zf"], ["zs"], 32)
-        ts(m("fi"), T.zs[:, 1::2], 15, ALU.bitwise_and, ["zs"], ["fi"])
-        q1("un", "np", 16.0, ALU.mult)
-        tt(T.C16[:, 16:32], m("un"), T.C16[:, 0:16], ALU.max, ["un", ("C16", 0, 16)], [("C16", 16, 32)])
-        tt(m("ko"), T.zi[:, 33::2], T.C16[:, 0:16], ALU.add, [("zi", 2, 3), ("C16", 0, 16)], ["ko"])
-        q2("fo", "fi", "C16", ALU.add, 16, 16)
-        qc("offK", "ko")
+        ts(m("fo"), T.zs[:, 1::2], 0xC0F, ALU.bitwise_and, ["zs"], ["fo"])
+        tt(m("ko"), T.zi[:, 33::2], T.C16[:], ALU.add, [("zi", 2, 3), "C16"], ["ko"])
+        q2("oP", "kl", "CB", ALU.add)
+        cp(m("offK", 32), m("ko", 32), ["ko", "oP"], ["offK", "offP"])
         for rl in range(4):
             r4 = ("offF", 4 * rl, 4 * rl + 4)
-            cp(m("offF", 4, 4 * rl), T.sf[:, WHERE["fo"][1] + rl:WHERE["fo"][1] + 16:4], ["fo"], [r4])
-            out, a = T.xs[:, rl::4], T.yg[:].indirect(m("offF", 4, 4 * rl))
-            if rl % 2:
-                cp(out, a, ["yg", r4], [("xs", rl, rl + 1)], gath(64))
-            else:
-                act(out, a, AF.Copy, ["yg", r4], [("xs", rl, rl + 1)], gath(64))
-        q2("oP", "kl", "CB", ALU.add, 32)
-        q2("fa", "fi", "pr", ALU.mult)
-        q2("oN", "oN", "fa", ALU.add)
-        qc("offP", "oP")
+            ts(m("offF", 4, 4 * rl), T.si[:, WHERE["fo"][1] + rl:WHERE["fo"][1] + 16:4], col(8), ALU.add, ["fo", rc(8)], [r4], 16.0 * rl, ALU.add)
+            gather(XQ[0][rl], T.xs[:, rl::4], T.yg[:].indirect(m("offF", 4, 4 * rl)), ["yg", r4], [("xs", rl, rl + 1)], 64)
+        q2("f1", "fo", "CQ", ALU.add)
+        q2("fa", "f1", "pr", ALU.mult)
+        q2("oN", "fa", "CB", ALU.add)
         qc("offN", "oN")
         ts(T.po[:], T[pw][:].indirect(m("offP")), 4095, ALU.bitwise_and, [pw, "offP"], ["po"], c=gath(256))
         if last:
@@ -494,14 +552,14 @@ def rank_program(g, core, T, topo):
             dma([(T.yp[:], T.pout[:], [], ["pout"])], 128)
         else:
             send(T.po[:], "po", T["PW%d" % (t + 1)][:, 0:256], ("PW%d" % (t + 1), 0, 256), prv, "p%d" % (t + 1))
-        act(T.a1[:], T.PS[:].indirect(m("offN")), AF.Copy, ["PS", "offN"], ["a1"], gath(256))
+        gather("s", T.a1[:], T.PS[:].indirect(m("offN")), ["PS", "offN"], ["a1"], 256)
         q1("nq", "nm", -2048.0, ALU.add, 1.0 / 16, ALU.mult)
         q2("t16", "nq", "np", ALU.add)
         qc("t32", "t16")
         step = (1, 4, 16)[t]
         at = [(4 * q, 16 * (q % 4) + q // 4, q)[t] for q in range(16)]
         mms([(T.pb[:, 0:4, at[q]:at[q] + 3 * step + 1:step], T.SELT[:, q, :], m("t16")) for q in range(16)], ("spread", t), ["SELT", "t16"], "pb")
-        q2("w1", "nm", "CP", ALU.add, 16, 16 * t)
+        q2("w1", "nm", "CP", ALU.add, 16 * t)
         q2("w1p", "w1", "pr", ALU.mult)
         for a, b in ((8, 16), (0, 8)):
             for i in range(a, b):
@@ -510,11 +568,11 @@ def rank_program(g, core, T, topo):
             tt(m("w2", 8, a), T.FE[:, 64 * a + 63:64 * b:64], m("w1p", 8, a), ALU.add, [("FE", a, b), "w1p"], [("w2", a, b)])
             tt(m("w3", 8, a), m("w2", 8, a), T.DM[:, a:b], ALU.max, [("w2", a, b), "DM"], [("w3", a, b)])
             ts(m("offX", 8, a), m("w3", 8, a), 1.0 / 256, ALU.mult, [("w3", a, b)], [("offX", a, b)])
-        act(T.yv[:], T.yg[:].indirect(m("offK")), AF.Copy, ["yg", "offK"], ["yv"], gath(256))
+        gather("s", T.yv[:], T.yg[:].indirect(m("offK")), ["yg", "offK"], ["yv"], 256)
         act(T.ak[:], T.d[:].indirect(m("offK")), AF.Abs, ["d", "offK"], ["ak"], gath(256))
-        act(T.pk[:, 0:256], T.yv[:], AF.Sign, ["yv"], ["pk"], 256, scale=-1.0, bias=127.5)
+        act(T.sy[:], T.yv[:], AF.Sign, ["yv"], ["sy"], 256, scale=-1.0, bias=127.5)
         ts(T.nr[:], T.ak[:], 32.5, ALU.is_lt, ["ak"], ["nr"], 128.0, ALU.mult, c=128)
-        tt(T.e2[:], T.nr[:], T.pk[:, 0:256], ALU.mult, ["nr", "pk"], ["e2"], 256)
+        tt(T.e2[:], T.nr[:], T.sy[:], ALU.mult, ["nr", "sy"], ["e2"], 256)
         for c in (3, 2, 1, 0):
             tt(T.X[:].indirect(m("offX", 4, 4 * c)), T.yv[:, 64 * c:64 * c + 64], T.e2[:, 64 * c:64 * c + 64], ALU.add,
                ["yv", "e2", ("offX", 4 * c, 4 * c + 4)], ["X"], -60 - 64 * SCATTER)
@@ -522,8 +580,10 @@ def rank_program(g, core, T, topo):
             dma([(T.yx[:], XW, [], [XT])], 1024)
         else:
             allowance(t)
-        q1("u8", "np", 1.0 / 2048, ALU.mult)
-        tt(T.RC[:, 15::16], m("u8"), T.CV[:], ALU.add, ["u8", "CV"], ["RC"])
+        q1("u8", "np", 7.25 / 256, ALU.mult)
+        ts(T.RC[:, 13::16], m("np"), -2.0 ** 18, ALU.mult, ["np", ("RC", 8, 10)], [("RC", 1, 2)], -1.0 / 8, ALU.add)
+        ts(T.RC[:, 14::16], m("np"), 2.0 ** 18 - 1.0 / 32, ALU.mult, ["np", ("RC", 8, 10)], [("RC", 2, 3)], -1.0 / 8, ALU.add)
+        tt(T.RC[:, 15::16], m("u8"), T.CV[:], ALU.add, ["u8", "CV", ("RC", 8, 10)], [("RC", 3, 4)])
         for h in range(2):
             for b in range(4 * h, 4 * h + 4):
                 second(t, b)

from concourse.mybir import AluOpType as ALU, ActivationFunctionType as AF

BIG = 2.0 ** 30
U = 2.0 ** 17
KW = 18 * 128
_B = "bfloat16"
_F = "float32"
_H = "float16"
_I = "int32"
_U = "uint16"
SCRATCH = {
    "X": ("sbuf", [128, 4160], _B),
    "yg": ("sbuf", [128, 4096], _B), "d": ("sbuf", [128, 4096], _B), "s": ("sbuf", [128, 4096], _B), "rl": ("sbuf", [128, 4096], _B),
    "df": ("sbuf", [128, 4096], _B), "ab": ("sbuf", [128, 256, 16], _B),
    "KS": ("sbuf", [128, 2 * KW], _F), "PS": ("sbuf", [128, 4352], _F),
    "kd": ("dram", [2, 8, 33, 128], _F),
    "kin": ("sbuf", [128, 256], _I), "kp": ("sbuf", [128, 256], _F), "ku": ("sbuf", [128, 256], _U), "a1": ("sbuf", [128, 256], _F),
    "pu": ("sbuf", [128, 256], _U), "Pf": ("sbuf", [128, 256], _F), "po": ("sbuf", [128, 256], _I), "pout": ("sbuf", [128, 256], _F),
    "Pm": ("sbuf", [128, 2, 4, 2, 16], _H), "PT": ("sbuf", [128, 2, 4, 2, 16], _H),
    "t1": ("sbuf", [128, 256], _I), "t2": ("sbuf", [128, 256], _I),
    "pid": ("sbuf", [128, 8], _I), "col": ("sbuf", [128, 24], _F), "rowi": ("sbuf", [128, 160], _F), "rowg": ("sbuf", [128, 128], _F),
    "r16": ("sbuf", [128, 16], _F), "OH": ("sbuf", [128, 16], _F),
    "SEL": ("sbuf", [128, 144], _B), "SELT": ("sbuf", [128, 16, 128], _B), "PERM": ("sbuf", [128, 2, 160], _H), "BLK": ("sbuf", [128, 128], _B),
    "ID": ("sbuf", [128, 128], _B), "IDN": ("sbuf", [128, 128], _B), "ID64": ("sbuf", [128, 128], _B), "IDH": ("sbuf", [128, 128], _B),
    "JR": ("sbuf", [128, 256], _B), "TWO": ("sbuf", [128, 128], _B),
    "RST": ("sbuf", [128, 256], _F), "RC": ("sbuf", [128, 256], _F), "RSD": ("sbuf", [128, 1024], _B),
    "C16": ("sbuf", [128, 16], _F), "CB": ("sbuf", [128, 16], _F), "CV": ("sbuf", [128, 16], _F), "DM": ("sbuf", [128, 16], _F),
    "CQ": ("sbuf", [128, 16], _F), "CW": ("sbuf", [128, 64], _F), "CP": ("sbuf", [128, 48], _F),
    "R": ("sbuf", [128, 256], _I), "sg": ("sbuf", [128, 256], _B), "us": ("sbuf", [128, 256], _H),
    "zi": ("sbuf", [128, 64], _I), "zf": ("sbuf", [128, 64], _F), "zs": ("sbuf", [128, 32], _I),
    "sf": ("sbuf", [128, 320], _F), "si": ("sbuf", [128, 128], _I), "sh": ("sbuf", [128, 48], _H), "su": ("sbuf", [128, 128], _U),
    "kc": ("sbuf", [128, 4], _F), "kj": ("sbuf", [128, 16], _F), "Ai": ("sbuf", [128, 4], _I), "thr": ("sbuf", [128, 4], _F),
    "xs": ("sbuf", [128, 256], _B), "ns": ("sbuf", [128, 256], _B), "fs": ("sbuf", [128, 256], _F),
    "NE": ("sbuf", [128, 1024], _B), "FE": ("sbuf", [128, 1024], _B),
    "ak": ("sbuf", [128, 256], _B), "yv": ("sbuf", [128, 256], _B), "sy": ("sbuf", [128, 256], _B),
    "nr": ("sbuf", [128, 256], _B), "e2": ("sbuf", [128, 256], _B),
    "pk": ("psum", [128, 512], _F), "ps": ("psum", [128, 512], _F), "pb": ("psum", [128, 8, 64], _F),
}
ROUNDS = 3
YQ = ("vsssssvs", "vsssssss", "vsssssss")
MODE = ("vvvvvvss", "vvvvvvss", "vvvvvvss")
SIZE = ("ccssccss", "ccssccss", "ccssccss")
SECOND = ("ttts", "ttts", "ttts")
XQ = ("ssss",)
BANKS = ("db0", "db1", "db2", "db3", "db4", "db0", "db1", "db2")
for _c in range(5):
    SCRATCH["db%d" % _c] = ("psum", [128, 64, 8], _F)
for _t in range(ROUNDS):
    SCRATCH["PW%d" % _t] = ("sbuf", [128, 512], _I)
    SCRATCH["kl%d" % _t] = ("sbuf", [128, 256], _U)
    SCRATCH["kf%d" % _t] = ("sbuf", [128, 256], _F)
PSUM = ("pk", "ps", "pb", "db0", "db1", "db2", "db3", "db4")
SEMAPHORES = (["qv", "qs", "qt", "qg"] + ["dm%d" % i for i in range(40)]
              + [a + b + str(t) for a in "rl" for b in ("p", "u0", "u1") for t in (1, 2)])
SMALL = {"sf": ("ko", "oP", "oN", "far", "np", "nq", "f1", "fa", "t32", "w1", "w1p", "w2", "w3", "u8"),
         "si": ("nm", "fo"),
         "sh": ("kl", "pr", "t16"),
         "su": ("offK", "offP", "offF", "offN", "offX", "offV")}
WHERE = {n: (b, 16 * i) for b in SMALL for i, n in enumerate(SMALL[b])}

CYCLE, TCYCLE, GATHER, SCATTER = 0.00085, 0.00043, 1.56, 3.5
PASSES = 100
SWAPS = 8000
CASES = ({"compute": 1.0, "index": 1.0, "tensor": 1.0, "remote": 1.0, "local": 1.0, "wake": 0.2, "all": 0.8},
         {"compute": 1.1, "index": 1.1, "tensor": 2.2, "remote": 1.1, "local": 1.2, "wake": 0.22, "all": 1.4},
         {"compute": 1.3, "index": 1.6, "tensor": 1.7, "remote": 1.4, "local": 1.5, "wake": 0.25, "all": 1.4})
ORDER = []


def issue_order(calls):
    n = len(calls)
    cases = []
    for case in CASES:
        busy = [c["busy"] * case[c["kind"]] for c in calls]
        late = [c["late"] * case[c["kind"]] for c in calls]
        fwd = [[] for _ in range(n)]
        bwd = [[] for _ in range(n)]
        for j, c in enumerate(calls):
            for i, how in c["pre"].items():
                gap = busy[i] + (0.0 if how == "order" else late[i] + case["wake"])
                fwd[i].append((j, gap))
                bwd[j].append((i, gap + busy[j] - busy[i]))
        cases.append((busy, late, fwd, bwd))
    queue = [c["q"] for c in calls]

    def play(order, case):
        busy, late, fwd, _b = case
        can = [0.0] * n
        by = [-1] * n
        held = [False] * n
        free = {}
        end, j1 = 0.0, 0
        for j in order:
            at = can[j]
            f = free.get(queue[j])
            if f and f[0] > at:
                at, by[j], held[j] = f[0], f[1], True
            free[queue[j]] = (at + busy[j], j)
            if at + busy[j] + late[j] > end:
                end, j1 = at + busy[j] + late[j], j
            for k, gap in fwd[j]:
                if at + gap > can[k]:
                    can[k], by[k] = at + gap, j
        path = []
        while j1 >= 0:
            if held[j1]:
                path.append((j1, by[j1]))
            j1 = by[j1]
        return end, path

    def score(order):
        return sum(play(order, c)[0] / case["all"] for c, case in zip(cases, CASES))

    def place(rank, busy, nxt, prev, can):
        left = [len(p) for p in prev]
        ready = [j for j in range(n) if left[j] == 0]
        taken = {}
        start = [0.0] * n
        while ready:
            j = min(ready, key=lambda j: rank[j])
            ready.remove(j)
            at = can[j]
            line = taken.setdefault(queue[j], [])
            i = len(line)
            while i and line[i - 1][1] > at:
                i -= 1
            while i < len(line) and line[i][0] < at + busy[j]:
                at = max(at, line[i][1])
                i += 1
            line.insert(i, (at, at + busy[j]))
            start[j] = at
            for k, gap in nxt[j]:
                can[k] = max(can[k], at + gap)
                left[k] -= 1
                if left[k] == 0:
                    ready.append(k)
        return start

    best = None
    rank = list(range(n))
    for turn in range(PASSES):
        busy, late, fwd, bwd = cases[turn // 2 % len(cases)]
        start = place(rank, busy, fwd, bwd, [0.0] * n)
        order = sorted(range(n), key=lambda j: (start[j], j))
        s = score(order)
        if best is None or s < best[0]:
            best = (s, order, start)
        if turn % 2:
            lo = max(best[2]) * (turn * 7717 % 997) / 997
            amp = (0.3, 0.8, 1.6)[turn // 2 % 7 % 3]
            rank = [x + (amp * ((j * 7919 + turn * 104729) ** 2 % 1009) / 1009 if lo < x < lo + 8 else 0) for j, x in enumerate(best[2])]
        else:
            back = place([-(start[j] + busy[j]) for j in range(n)], busy, bwd, fwd, list(late))
            rank = [-(back[j] + busy[j]) for j in range(n)]
    now, order = best[0], best[1]
    best = (now, order)
    pre = [set(c["pre"]) for c in calls]
    for turn in range(SWAPS):
        path = play(order, cases[turn % len(cases)])[1]
        pick = (turn * 7919 + 13) ** 2 % 1000003
        j, p = path[pick % len(path)]
        a, b, more = order.index(p), order.index(j), pick // 1000 % 3
        if pick // 100 % 2:
            while more and a > 0:
                a -= 1
                more -= queue[order[a]] == queue[j]
            move, want = {j}, set(pre[j])
            for x in reversed(order[a:b]):
                if x in want:
                    move.add(x)
                    want |= pre[x]
            ahead = move
        else:
            while more and b < n - 1:
                b += 1
                more -= queue[order[b]] == queue[j]
            move = {p}
            for x in order[a + 1:b + 1]:
                if pre[x] & move:
                    move.add(x)
            ahead = set(order[a:b + 1]) - move
        if p in ahead or j not in ahead:
            continue
        new = order[:a] + [x for x in order[a:b + 1] if x in ahead] + [x for x in order[a:b + 1] if x not in ahead] + order[b + 1:]
        s = score(new)
        if s <= now + 0.5 * (1 - turn / SWAPS) ** 2 * (pick % 97) / 97:
            now, order = s, new
            if s < best[0]:
                best = (s, new)
    return best[1]


def rank_program(g, core, T, topo):
    rank = T.rank_of(core)
    if rank is None:
        return
    n_ranks = len(T.cores)
    eng = {"v": g.vector, "s": g.scalar, "t": g.tensor, "g": g, "y": g.sync}
    calls = []
    log = {}
    banks = {}
    dmas = [0]
    opened = {}

    def m(name, n=16, at=0):
        b, i = WHERE[name]
        return T[b][:, i + at:i + at + n]

    def reg(r):
        if isinstance(r, tuple):
            if r[0] in WHERE:
                b, i = WHERE[r[0]]
                return (b, i + r[1], i + r[2])
            return r
        if r in WHERE:
            b, i = WHERE[r]
            return (b, i, i + 16)
        return (r, 0, 1 << 20)

    def call(q, emit, busy, reads, writes, late=0.0, group=None, after=(), told=("done", "done"), kind="compute"):
        j = len(calls)
        pre = {i: "order" for i in after}
        own = q in "vstg" and told[0] == "done"

        def follow(i, how):
            if how != "order" or i not in pre:
                pre[i] = how

        for is_w, regs in ((False, reads), (True, writes)):
            for name, lo, hi in [reg(r) for r in regs]:
                if name in PSUM:
                    b = banks.setdefault(name, [None, [], []])
                    if b[0] != (q, group):
                        b[0], b[1], b[2] = (q, group), [], b[1]
                    for i, _l, _h, _w in b[2]:
                        follow(i, "order" if calls[i]["q"] == q == "t" else "done")
                    for i, l, h, w in b[1]:
                        if q != "t" and i != j and l < hi and lo < h and (w or is_w):
                            follow(i, "done" if w else "order")
                    b[1].append((j, lo, hi, is_w))
                    continue
                old = log.setdefault(name, [])
                for l, h, i, w, how in old:
                    if i != j and l < hi and lo < h and (w or is_w):
                        follow(i, "order" if (not w and own and calls[i]["own"] and calls[i]["q"] == q) else how)
                if is_w:
                    old[:] = [e for e in old if e[2] == j or not (lo <= e[0] and e[1] <= hi)]
                old.append((lo, hi, j, is_w, told[is_w]))
        calls.append({"q": q, "emit": emit, "busy": busy, "late": late, "pre": pre, "group": group, "own": own, "kind": kind})
        return j

    def vector(fn, reads, writes, c, q="v"):
        return call(q, fn, max(64, abs(c)) * CYCLE, reads, writes, kind="index" if c < 0 else "compute")

    def dma(pairs, kb, after=()):
        sem = "dm%d" % dmas[0]
        dmas[0] += 1

        def emit():
            for out, in_, _w, _r in pairs:
                g.sync.dma_start(out, in_).then_inc(T.sem[sem], 16)
            return {sem: 16 * len(pairs)}

        return call("y", emit, 0.05 * len(pairs), [x for p in pairs for x in p[3]], [x for p in pairs for x in p[2]], 2.0 + kb / 400.0,
                    after=after, told=(sem, sem), kind="local")

    def tt(out, a, b, o, reads, writes, c=0):
        vector(lambda: g.vector.tensor_tensor(out, a, b, o), reads, writes, c)

    def ts(out, a, s1, o1, reads, writes, s2=None, o2=None, c=0):
        if o2 is None:
            vector(lambda: g.vector.tensor_scalar(out, a, s1, None, o1), reads, writes, c)
        else:
            vector(lambda: g.vector.tensor_scalar(out, a, s1, s2, o1, o2), reads, writes, c)

    def q1(out, a, s1, o1, s2=None, o2=None):
        ts(m(out), m(a), s1, o1, [a], [out], s2, o2)

    def q2(out, a, b, o, at=0):
        tt(m(out), m(a), m(b) if b in WHERE else T[b][:, at:at + 16], o, [a, b], [out])

    def cp(out, a, reads, writes, c=0):
        vector(lambda: g.vector.tensor_copy(out, a), reads, writes, c)

    def qc(out, a):
        cp(m(out), m(a), [a], [out])

    def fill(name, x, ap=None, w=None, c=0):
        vector(lambda: g.vector.memset(T[name][:] if ap is None else ap, x), [], [w or name], c)

    def act(out, a, f, reads, writes, c, **kw):
        vector(lambda: g.scalar.activation(out, a, f, **kw), reads, writes, c, "s")

    def mms(each, group, reads, bank, c=64, after=()):
        def emit(st, sp):
            for k, (out, l, r) in enumerate(each):
                g.tensor.matmul(out, l, r, st and k == 0, sp and k == len(each) - 1).then_inc(T.sem.qt, 1)
            return len(each)

        if group[0] == "key":
            after = list(after) + opened.setdefault(group, [])
        j = call("t", emit, len(each) * max(64, c) * TCYCLE, reads, [bank], group=(bank, group), after=after, kind="tensor")
        if group[0] == "key" and not opened[group]:
            opened[group].append(j)
        return j

    def mm(out, l, r, group, reads, bank, c=64):
        return mms([(out, l, r)], group, reads, bank, c)

    def scan(out, a, b, first, o1, o2, reads, writes, c):
        vector(lambda: g.vector.tensor_tensor_scan(out, a, b, first, o1, o2), reads, writes, c)

    def iota(name, pat, base, mult=0, ap=None, w=None, after=()):
        n = 1
        for _s, k in pat:
            n *= k
        call("g", lambda: g.iota(T[name][:] if ap is None else ap, pat, base, mult, allow_small_or_imprecise_dtypes=True),
             0.13 + 2 * n * CYCLE, [], [w or name], after=after)

    def gath(n):
        return -70 - GATHER * n

    def col(i):
        return T.col[:, i:i + 1]

    def rc(i):
        return ("col", i, i + 1)

    XT = ("X", 64, 4160)
    XW = T.X[:, 64:4160]
    lists = dma([(T.PW0[:, 0:256], T.ph[:], [("PW0", 0, 256)], []), (T.kin[:], T.ka[:], ["kin"], [])], 128)
    dma([(XW, T.x0[:], [XT], [])], 800, [lists])
    iota("pid", [[0, 1]], 0, 1, T.pid[:, 0:1])
    iota("rowi", [[1, 160]], 0)
    iota("rowg", [[1, 8], [0, 16]], 0)
    iota("r16", [[1, 16]], 0)
    iota("JR", [[0, 16], [8192, 16]], 4096)
    iota("C16", [[1024, 4], [16, 4]], 0)
    iota("CB", [[64, 4], [1, 4]], 0)
    iota("CV", [[0, 2], [64, 2], [1, 4]], 4096 + 23 * 128)
    iota("DM", [[0, 4], [4096, 4]], 0)
    iota("CQ", [[-1024, 4], [0, 4]], 1)
    iota("CW", [[0, 16], [-1, 2]], 0, 0, T.CW[:, 0:32], ("CW", 0, 1))
    iota("CW", [[0, 16]], 1, 0, T.CW[:, 32::2], ("CW", 1, 2))
    iota("CW", [[1024, 4], [0, 4]], 16, 0, T.CW[:, 33::2], ("CW", 2, 3))
    iota("zi", [[0, 64]], 0)
    for i in range(3):
        iota("CP", [[0, 4], [4 ** i, 4]], -63, 0, T.CP[:, 16 * i:16 * i + 16], ("CP", 16 * i, 16 * i + 16))
    iota("PS", [[0, 4352]], 0, after=[j for j, c in enumerate(calls) if c["q"] == "g"])
    fill("RSD", -2.0 ** 21, c=512)
    fill("RSD", BIG, T.RSD[:, 0::64])
    dma([(T.KS[0::16, KW * h:KW * h + 2048], T.PS[1::16, 0:2048], [("KS", 4 * h, 4 * h + 1)], [("PS", 0, 2048)]) for h in range(2)]
        + [(T.kd[h, :, 0, :], T.PS[1::16, 0:128], [("kd", 40 * h, 40 * h + 1)], [("PS", 0, 128)]) for h in range(2)], 128)
    pid = lambda i: T.pid[:, i:i + 1]
    for i, sh, mk in ((1, 0, 15), (2, 4, 7), (3, 0, 3), (4, 2, 3), (5, 4, 1)):
        ts(pid(i), pid(0), sh, ALU.arith_shift_right, [("pid", 0, 1)], [("pid", i, i + 1)], mk, ALU.bitwise_and)
    cp(T.col[:, 0:6], T.pid[:, 0:6], [("pid", 0, 6)], [("col", 0, 6)])
    for i, a, s1, s2 in ((6, 2, 16.0, 15.0), (8, 1, 64.0, 0.0), (9, 1, 4.0, 0.0), (11, 0, 1.0, 16.0),
                         (12, 5, -1.0, 1.0), (13, 5, 1.0, 0.0), (14, 3, 16.0, col(4)), (16, 1, 4.0, -4096.0), (17, 1, 256.0, 0.0)):
        ts(col(i), col(a), s1, ALU.mult, [("col", 0, 6)], [rc(i)], s2, ALU.add)
    ts(T.ID[:], T.rowi[:, 0:128], col(0), ALU.is_equal, ["rowi", rc(0)], ["ID"], c=128)
    fill("JR", -992.0 * U, T.JR[32:64, :], c=128)
    fill("TWO", 1.0 / 32)
    fill("thr", 48.0 * U)
    cp(T.kl0[:], T.kin[:], ["kin"], ["kl0"], 256)
    for name, w in (("ID64", U / 64), ("IDN", -1.0), ("IDH", U / 4)):
        act(T[name][:], T.ID[:], AF.Copy, ["ID"], [name], 128, scale=w)
    for h in range(2):
        ts(T.PERM[:, h, :], T.rowi[:], col(11), ALU.is_equal, ["rowi", rc(11), rc(12 + h)], [("PERM", h, h + 1)], col(12 + h), ALU.mult, c=160)
        for name, x in (("RST", -BIG), ("RC", -1.0 / 8)):
            act(T[name][:, 128 * h:128 * h + 128], T.rowg[:], AF.Identity, ["rowg"], [(name, 8 + h, 9 + h)], 128, scale=0.0, bias=x)
    fill("RST", BIG, T.RST[:, 0::16])
    fill("X", 0.0, T.X[:, 0:64], ("X", 0, 64))
    ts(T.BLK[:], T.rowg[:], col(2), ALU.is_equal, ["rowg", rc(2)], ["BLK"], c=128)
    ts(T.SEL[:], T.rowi[:, 0:144], col(6), ALU.is_equal, ["rowi", rc(6)], ["SEL"], U, ALU.mult, c=144)
    ts(T.OH[:], T.r16[:], col(1), ALU.is_equal, ["r16", rc(1)], ["OH"])
    for q in range(16):
        act(T.SELT[:, q, :], T.BLK[:], AF.Copy, ["BLK", "OH"], [("SELT", q, q + 1)], 128, scale=T.OH[:, q:q + 1])
    for name, c in (("C16", 8), ("CB", 9), ("DM", 17)):
        ts(T[name][:], T[name][:], col(c), ALU.add, [name, rc(c)], [name])
    ts(T.CV[:], T.CV[:], 1.0 / 1024, ALU.mult, ["CV"], ["CV"])
    for i, c in enumerate((9, 14, 1)):
        r = ("CP", 16 * i, 16 * i + 16)
        ts(T.CP[:, r[1]:r[2]], T.CP[:, r[1]:r[2]], col(c), ALU.add, [r, rc(c)], [r], -8192.0, ALU.mult)
    ts(T.CP[:], T.CP[:], 64.0, ALU.add, ["CP"], ["CP"])

    nxt = T.cores[(rank + 1) % n_ranks]
    prv = T.cores[(rank - 1) % n_ranks]

    def send(src, r, land, w, dst, tag):
        rid, pid_, _ = topo.addr(dst)
        es = topo.engines(core, dst)
        other = prv if dst == nxt else nxt

        def emit():
            g.remote_dma(land, src, T.sem["r" + tag], T.sem["l" + tag], pid_, rid, sum(1 << e for e in es))
            return {"l" + tag: len(es), "r" + tag: len(topo.engines(other, core))}

        call("g", emit, 0.5, [r], [w], 5.6 if tag == "p1" else 2.6, told=("l" + tag, "r" + tag), kind="remote")

    def phage_forms(t):
        pw = "PW%d" % t
        cp(T.pu[:], T[pw][:, 0:256], [(pw, 0, 256)], ["pu"], 256)
        cp(T.Pf[:], T[pw][:, 0:256], [(pw, 0, 256)], ["Pf"], 256)
        dma([(T.PS[0::16, 256:4352], T.Pf[:], ["PS"], ["Pf"])], 128)
        for rl in range(4):
            ts(T.Pm[:, :, rl], T.pu[:, rl::4], -2048.0, ALU.add, ["pu"], [("Pm", rl, rl + 1)])
        vector(lambda: g.vector.transpose(T.PT[:], T.Pm[:]), ["Pm"], ["PT"], 128)
        act(T.pb[:, 4:8], T.Pf[:], AF.Copy, ["Pf"], ["pb"], 256)

    def shifted(t, h):
        kf = "kf%d" % t
        a, b = 128 * h, 128 * h + 128
        o = 40 * h
        dma([(T.kd[h, :, 1:17, :], T[kf][:, a:b], [("kd", o + 1, o + 17)], [(kf, a, b)])]
            + [(T.kd[h, :, i, :], T[kf][15::16, a:b], [("kd", o + i, o + i + 1)], [(kf, a, b)]) for i in range(17, 32)], 128)
        w = [("KS", 4 * h + 2, 4 * h + 3)]
        dma([(T.KS[j::16, KW * h:KW * h + 2048], T.kd[h, :, j + 1:j + 17, :], w, [("kd", o, o + 33)]) for j in range(1, 16)]
            + [(T.KS[:, KW * h + 2048:KW * h + 2176], T.kd[h, :, 0:16, :], w, [("kd", o, o + 33)]),
               (T.KS[:, KW * h + 2176:KW * h + 2304], T[kf][:, a:b], w, [(kf, a, b)])], 1152)

    def gather(q, out, a, reads, writes, n):
        if q == "v":
            cp(out, a, reads, writes, gath(n))
        else:
            act(out, a, AF.Copy, reads, writes, gath(n))

    def lanes(bank, base, src, e, group):
        c = e // 2
        each = []
        for q in range(8 * (e % 2), 8 * (e % 2) + 8):
            a = 1024 * c + 64 * q
            rhs = T.ab[:, a // 16:a // 16 + 4, :] if src == "ab" else T[src][:, a:a + 64]
            each.append((T[bank][:, base + 64 * c:base + 64 * c + 64], T.SEL[:, 15 - q:143 - q], rhs))
        return mms(each, group, ["SEL", ("ab", 2 * c, 2 * c + 2) if src == "ab" else (src, e, e + 1)], bank)

    def first(t, e):
        kl, a, b, r = "kl%d" % t, 512 * e, 512 * e + 512, (e, e + 1)
        s = XW.indirect(T[kl][:, 32 * e:32 * e + 32])
        if MODE[t][e] == "v":
            tt(T.d[:, a:b], s, T.yg[:, a:b], ALU.subtract, [XT, (kl, 32 * e, 32 * e + 32), ("yg",) + r], [("d",) + r], gath(512))
        else:
            gather("s", T.s[:, a:b], s, [XT, (kl, 32 * e, 32 * e + 32)], [("s",) + r], 512)
            tt(T.d[:, a:b], T.s[:, a:b], T.yg[:, a:b], ALU.subtract, [("s",) + r, ("yg",) + r], [("d",) + r], 512)
        lanes("ps", 0, "d", e, ("side", t, e // 2))
        if SIZE[t][e] == "s":
            act(T.rl[:, a:b], T.d[:, a:b], AF.Abs, [("d",) + r], [("rl",) + r], 512)
        else:
            ts(T.rl[:, a:b], T.d[:, a:b], 0.0, ALU.max, [("d",) + r], [("rl",) + r], 2.0, ALU.mult, c=256)
        return lanes("pk", 0, "rl", e, ("key", t))

    def names(t, c, sums):
        h = c % 2
        mms([(T.pk[:, 64 * c:64 * c + 64], T.PERM[:, h, 16 * (1 + h - g2):16 * (9 + h - g2)], T.PT[:, c // 2, :, g2, :]) for g2 in range(2)],
            ("key", t), ["PERM", "PT"], "pk", after=sums)

    def killed_names(t, h):
        pw, kf = "PW%d" % t, "kf%d" % t
        a, b = 128 * h, 128 * h + 128
        p, r = T.pb[:, 4 + 2 * h:6 + 2 * h], ("pb", 256 + a, 256 + b)
        tt(T.t1[:, a:b], T[kf][:, a:b], p, ALU.mult, [(kf, a, b), r], [("t1", a, b)], 128)
        ts(T.t2[:, a:b], T.t1[:, a:b], 5, ALU.arith_shift_right, [("t1", a, b)], [("t2", a, b)], c=128)
        tt(T[pw][:, 256 + a:256 + b], T.t2[:, a:b], p, ALU.add, [("t2", a, b), r], [(pw, 256 + a, 256 + b)], 128)

    def second(t, b):
        c, hj, db = b // 2, b % 2, BANKS[b]
        a, r = 1024 * c + 8 * hj, (2 * c, 2 * c + 2)
        out = T.ab[:, 64 * c:64 * c + 64, 8 * hj:8 * hj + 8]
        if SECOND[t][c] == "s":
            if hj == 0:
                for j in range(16):
                    tt(T.df[:, a + j:a + 1024:16], T.s[:, a + j:a + 1024:16], T.xs[:, 64 * c:64 * c + 64], ALU.subtract,
                       [("s",) + r, "xs"], [("df", 16 * c + j, 16 * c + j + 1)])
                act(T.ab[:, 64 * c:64 * c + 64, :], T.df[:, a:a + 1024], AF.Abs, [("df", 16 * c, 16 * c + 16)], [("ab",) + r], 1024)
            return
        for src in ("s",) if MODE[t][2 * c] == "s" else ("d", "yg"):
            mms([(T[db][:, :, jj], T.ID[:], T[src][:, a + jj:1024 * c + 1024:16]) for jj in range(8)], ("second", t, b), ["ID", (src,) + r], db)
        mms([(T[db][:, :, jj], T.IDN[:], T.xs[:, 64 * c:64 * c + 64]) for jj in range(8)], ("second", t, b), ["IDN", "xs"], db)
        act(out, T[db][:], AF.Abs, [db], [("ab", b, b + 1)], 512)

    def tail(t, h):
        a, b, i, j = 128 * h, 128 * h + 128, 8 * h, 8 * h + 8
        bank = ("pk", "ps")[h]
        for e in range(4 * h, 4 * h + 4):
            lanes(bank, 256 - 128 * h, "ab", e, ("near", t))
        act(T.ns[:, a:b], T[bank][:, 256:384], AF.Sign, [bank], [("ns", a, b)], 128, bias=-959.5 * U)
        scan(T.fs[:, a:b], T.ns[:, a:b], T.RC[:, a:b], BIG, ALU.min, ALU.add, ["RC", ("ns", a, b)], [("fs", a, b)], 128)
        ts(m("offV", 8, i), T.fs[:, a + 15:b:16], 1024.0, ALU.mult, [("fs", a, b), rc(16)], [("offV", i, j)], col(16), ALU.add)
        tt(T.kp[:, a:b], T.KS[:, KW * h:KW * h + KW].indirect(m("offV", 8, i)), T.a1[:, a:b], ALU.add,
           [("KS", 4 * h, 4 * h + 4), ("offV", i, j), "a1"], [("kp", a, b)], gath(128))
        if t == ROUNDS - 1:
            dma([(T.yk[:, a:b], T.kp[:, a:b], [], [("kp", a, b)])], 64)
        else:
            kl = "kl%d" % (t + 1)
            cp(T.ku[:, a:b], T.kp[:, a:b], [("kp", a, b)], [("ku", a, b)], 128)
            send(T.ku[:, a:b], ("ku", a, b), T[kl][:, a:b], (kl, a, b), nxt, "u%d%d" % (h, t + 1))

    def allowance(t):
        mm(T.pb[:, 4, 0:16], T.BLK[:], m("kl"), ("kills", t), ["BLK", "kl"], "pb")
        act(T.kj[:], T.pb[:, 4, 0:16], AF.Copy, ["pb"], ["kj", ("kc", t, t + 1)], 90, accum_out=T.kc[:, t:t + 1])
        ts(T.Ai[:, 0:1], T.kc[:, t:t + 1], T.kc[:, 0:1] if t else 0.0, ALU.add, ["kc"], [("Ai", 0, 1)], 1.0 / 256, ALU.mult)
        ts(T.Ai[:, 1:2], T.Ai[:, 0:1], 15, ALU.bitwise_and, [("Ai", 0, 1)], [("Ai", 1, 2)])
        ts(T.thr[:, 0:1], T.Ai[:, 1:2], 4.0 * U, ALU.mult, [("Ai", 1, 2)], ["thr"], 48.0 * U, ALU.add)

    for t in range(ROUNDS):
        last = t == ROUNDS - 1
        pw = "PW%d" % t
        phage_forms(t)
        mm(T.pk[:, 0:256], T.TWO[0:64, :], T.JR[0:64, :], ("key", t), ["TWO", "JR"], "pk", 256)
        for h in range(2):
            a, b, kl, kf = 128 * h, 128 * h + 128, "kl%d" % t, "kf%d" % t
            cp(T[kf][:, a:b], T[kl][:, a:b], [(kl, a, b)], [(kf, a, b)], 128)
            for e in range(4 * h, 4 * h + 4):
                gather(YQ[t][e], T.yg[:, 512 * e:512 * e + 512], XW.indirect(T.pu[:, 32 * e:32 * e + 32]), [XT, "pu"], [("yg", e, e + 1)], 512)
            for c in (2 * h, 2 * h + 1):
                a, b = 64 * c, 64 * c + 64
                sums = [first(t, 2 * c), first(t, 2 * c + 1)]
                if SIZE[t][2 * c] == "c":
                    ts(T.us[:, a:b], T.ps[:, a:b], -4.0 / U, ALU.mult, [("ps", a, b)], [("us", a, b)])
                    sums.append(mm(T.pk[:, a:b], T.IDH[:], T.us[:, a:b], ("key", t), ["IDH", ("us", a, b)], "pk"))
                act(T.sg[:, a:b], T.ps[:, a:b], AF.Sign, [("ps", a, b)], [("sg", a, b)], 64, bias=-0.5 * U)
                mm(T.pk[:, a:b], T.ID64[:], T.sg[:, a:b], ("key", t), ["ID64", ("sg", a, b)], "pk")
                names(t, c, sums)
            shifted(t, h)
            killed_names(t, h)
        scan(T.R[:], T.RST[:], T.pk[:, 0:256], 0.0, ALU.max, ALU.min, ["RST", "pk"], ["R"], 256)
        r = T.R[:, 15::16]
        for i, (at, sh, mk) in enumerate(((1, 11, 2), (32, 17, 3), (33, 13, 15))):
            ts(T.zi[:, at:at + 31:2], r, sh, ALU.arith_shift_right, ["R"], [("zi", i, i + 1)], mk, ALU.bitwise_and)
        ts(m("nm"), r, 4095, ALU.bitwise_and, ["R"], ["nm"])
        ts(m("kl"), r, -112.0 * U, ALU.is_lt, ["R"], ["kl"], 256.0, ALU.mult)
        ts(m("far"), r, T.thr[:, 0:1], ALU.is_ge, ["R", "thr"], ["far"], 256.0, ALU.mult)
        q2("np", "far", "kl", ALU.add)
        q1("pr", "np", -1.0, ALU.mult, 256.0, ALU.add)
        tt(T.zf[:], T.zi[:], T.CW[:], ALU.add, ["zi", "CW"], ["zf"])
        scan(T.zs[:], T.zf[:, 0:32], T.zf[:, 32:64], 0.0, ALU.mult, ALU.add, ["zf"], ["zs"], 32)
        ts(m("fo"), T.zs[:, 1::2], 0xC0F, ALU.bitwise_and, ["zs"], ["fo"])
        tt(m("ko"), T.zi[:, 33::2], T.C16[:], ALU.add, [("zi", 2, 3), "C16"], ["ko"])
        q2("oP", "kl", "CB", ALU.add)
        cp(m("offK", 32), m("ko", 32), ["ko", "oP"], ["offK", "offP"])
        for rl in range(4):
            r4 = ("offF", 4 * rl, 4 * rl + 4)
            ts(m("offF", 4, 4 * rl), T.si[:, WHERE["fo"][1] + rl:WHERE["fo"][1] + 16:4], col(8), ALU.add, ["fo", rc(8)], [r4], 16.0 * rl, ALU.add)
            gather(XQ[0][rl], T.xs[:, rl::4], T.yg[:].indirect(m("offF", 4, 4 * rl)), ["yg", r4], [("xs", rl, rl + 1)], 64)
        q2("f1", "fo", "CQ", ALU.add)
        q2("fa", "f1", "pr", ALU.mult)
        q2("oN", "fa", "CB", ALU.add)
        qc("offN", "oN")
        ts(T.po[:], T[pw][:].indirect(m("offP")), 4095, ALU.bitwise_and, [pw, "offP"], ["po"], c=gath(256))
        if last:
            cp(T.pout[:], T.po[:], ["po"], ["pout"], 256)
            dma([(T.yp[:], T.pout[:], [], ["pout"])], 128)
        else:
            send(T.po[:], "po", T["PW%d" % (t + 1)][:, 0:256], ("PW%d" % (t + 1), 0, 256), prv, "p%d" % (t + 1))
        gather("s", T.a1[:], T.PS[:].indirect(m("offN")), ["PS", "offN"], ["a1"], 256)
        q1("nq", "nm", -2048.0, ALU.add, 1.0 / 16, ALU.mult)
        q2("t16", "nq", "np", ALU.add)
        qc("t32", "t16")
        step = (1, 4, 16)[t]
        at = [(4 * q, 16 * (q % 4) + q // 4, q)[t] for q in range(16)]
        mms([(T.pb[:, 0:4, at[q]:at[q] + 3 * step + 1:step], T.SELT[:, q, :], m("t16")) for q in range(16)], ("spread", t), ["SELT", "t16"], "pb")
        q2("w1", "nm", "CP", ALU.add, 16 * t)
        q2("w1p", "w1", "pr", ALU.mult)
        for a, b in ((8, 16), (0, 8)):
            for i in range(a, b):
                ts(T.NE[:, 64 * i:64 * i + 64], T.pb[:, i // 4, :], m("t32", 1, i), ALU.not_equal, ["pb", "t32"], [("NE", i, i + 1)], 2.0 ** 28, ALU.mult)
            scan(T.FE[:, 64 * a:64 * b], T.RSD[:, 64 * a:64 * b], T.NE[:, 64 * a:64 * b], 0.0, ALU.add, ALU.min, ["RSD", ("NE", a, b)], [("FE", a, b)], 256)
            tt(m("w2", 8, a), T.FE[:, 64 * a + 63:64 * b:64], m("w1p", 8, a), ALU.add, [("FE", a, b), "w1p"], [("w2", a, b)])
            tt(m("w3", 8, a), m("w2", 8, a), T.DM[:, a:b], ALU.max, [("w2", a, b), "DM"], [("w3", a, b)])
            ts(m("offX", 8, a), m("w3", 8, a), 1.0 / 256, ALU.mult, [("w3", a, b)], [("offX", a, b)])
        gather("s", T.yv[:], T.yg[:].indirect(m("offK")), ["yg", "offK"], ["yv"], 256)
        act(T.ak[:], T.d[:].indirect(m("offK")), AF.Abs, ["d", "offK"], ["ak"], gath(256))
        act(T.sy[:], T.yv[:], AF.Sign, ["yv"], ["sy"], 256, scale=-1.0, bias=127.5)
        ts(T.nr[:], T.ak[:], 32.5, ALU.is_lt, ["ak"], ["nr"], 128.0, ALU.mult, c=128)
        tt(T.e2[:], T.nr[:], T.sy[:], ALU.mult, ["nr", "sy"], ["e2"], 256)
        for c in (3, 2, 1, 0):
            tt(T.X[:].indirect(m("offX", 4, 4 * c)), T.yv[:, 64 * c:64 * c + 64], T.e2[:, 64 * c:64 * c + 64], ALU.add,
               ["yv", "e2", ("offX", 4 * c, 4 * c + 4)], ["X"], -60 - 64 * SCATTER)
        if last:
            dma([(T.yx[:], XW, [], [XT])], 1024)
        else:
            allowance(t)
        q1("u8", "np", 7.25 / 256, ALU.mult)
        ts(T.RC[:, 13::16], m("np"), -2.0 ** 18, ALU.mult, ["np", ("RC", 8, 10)], [("RC", 1, 2)], -1.0 / 8, ALU.add)
        ts(T.RC[:, 14::16], m("np"), 2.0 ** 18 - 1.0 / 32, ALU.mult, ["np", ("RC", 8, 10)], [("RC", 2, 3)], -1.0 / 8, ALU.add)
        tt(T.RC[:, 15::16], m("u8"), T.CV[:], ALU.add, ["u8", "CV", ("RC", 8, 10)], [("RC", 3, 4)])
        for h in range(2):
            for b in range(4 * h, 4 * h + 4):
                second(t, b)
            tail(t, h)

    if not ORDER:
        ORDER.extend(issue_order(calls))
    size = {}
    for c in calls:
        size[c["group"]] = size.get(c["group"], 0) + 1
    seen = {}
    told = {}
    total = {}
    waited = {}
    for j in ORDER:
        c = calls[j]
        q = c["q"]
        need = {}
        for i, how in c["pre"].items():
            if how != "order":
                sem = "q" + calls[i]["q"] if how == "done" else how
                need[sem] = max(need.get(sem, 0), told[i][sem])
        for sem in sorted(need):
            if waited.get((q, sem), 0) < need[sem]:
                waited[(q, sem)] = need[sem]
                eng[q].wait_ge(T.sem[sem], need[sem])
        if c["own"]:
            sem = "q" + q
            if q == "t":
                seen[c["group"]] = seen.get(c["group"], 0) + 1
                total[sem] = total.get(sem, 0) + c["emit"](seen[c["group"]] == 1, seen[c["group"]] == size[c["group"]])
            else:
                c["emit"]().then_inc(T.sem[sem], 1)
                total[sem] = total.get(sem, 0) + 1
            told[j] = {sem: total[sem]}
        else:
            told[j] = c["emit"]()
            total.update(told[j])
    for sem in sorted(total):
        if waited.get(("g", sem), 0) < total[sem]:
            g.wait_ge(T.sem[sem], total[sem])
